import numpy as np, ml_dtypes
CORES = [8,136,40,168]
N = 4
BF = ml_dtypes.bfloat16
def gentries(a):
    return np.ascontiguousarray(a.reshape(8, 16, -1).transpose(0, 2, 1)).reshape(8, -1)
def gtable(e):
    e = np.asarray(e); return np.ascontiguousarray(e.reshape(8, -1, 16).transpose(0, 2, 1)).reshape(128, -1).astype(np.int32)
W, CELLS, K, RO, TH1, TH2 = 2048, 512, 256, 3, 256, 600
def world(rng, fam, uneven):
    X = np.zeros((N, 8, W, 16), np.int64)
    for g in range(8):
        P = int(fam[g]); pr = rng.integers(0, 256, (P, 16))
        if uneven: pr = np.floor(rng.random((P, 16)) * np.exp2(8 * rng.random((P, 1)))).astype(np.int64)
        w = rng.integers(0, P, (N, W)); s = rng.choice(np.array([2, 8, 24]), (N, W, 1))
        X[:, g] = np.clip(pr[w] + rng.integers(-24, 25, (N, W, 16)) * s // 24, 0, 255)
    return X
def parts(rng, fam, uneven=False):
    return (world(rng, fam, uneven), rng.integers(0, W, (N, 8, CELLS, 16)), rng.integers(0, CELLS, (N, 8, K)), rng.integers(0, 256, (N, 8, K, 16)),
            rng.integers(0, 256, (N, 8, 16, 16)), rng.integers(0, 256, (N, 8, 16)))
def half(a):
    return np.ascontiguousarray(a).astype(np.float32).astype(BF)
def pack(X, ce, v, z, kp, wv):
    return {"px": half(X.transpose(0, 1, 3, 2).reshape(N, 128, W)), "ce": np.ascontiguousarray(ce.transpose(0, 1, 3, 2).reshape(N, 128, CELLS)).astype(np.int32),
            "v0": np.stack([gtable(a) for a in v]), "z0": half(z.transpose(0, 1, 3, 2).reshape(N, 128, K)), "kap": half(kp.reshape(N, 128, 16)), "wu": half(wv.reshape(N, 128, 1))}
def cut(a):
    return a // 16 + (np.arange(16) < a % 16)
def setup_inputs(rng):
    return pack(*parts(rng, rng.choice(np.array([8, 10, 12, 16]), 8)))
def setup_inputs_spread(rng):
    X, ce, v, z, kp, wv = parts(rng, rng.permutation(np.array([2, 4, 8, 12, 16, 32, 64, 128])), True)
    e = rng.choice(np.array([1.0, 2.0, 6.0]), (N, 8, CELLS, 1)); ce = np.floor(W * rng.random(ce.shape) ** e).astype(np.int64)
    v = np.floor(CELLS * rng.random(v.shape) ** 3).astype(np.int64)
    z = np.floor(rng.random(z.shape) * np.exp2(8 * rng.random((N, 8, K, 1)))).astype(np.int64)
    kp = np.floor(256 * rng.random(kp.shape) ** rng.choice(np.array([0.5, 1.0, 4.0]), (N, 8, 1, 16))).astype(np.int64)
    wv = np.floor(256 * rng.random(wv.shape) ** 2).astype(np.int64)
    return pack(X, ce, v, z, kp, wv)
def setup_inputs_ends(rng):
    def mix(n):
        return np.where(rng.random((N, 8, n, 1)) < 0.5, 255 * rng.integers(0, 2, (N, 8, n, 16)), 255 * rng.integers(0, 2, (N, 8, n, 1)))
    i = np.arange(16); R = 255 * (i < 9)
    X = mix(W); X[:, :, W - 1] = 255; X[:, :, 0] = 0; X[:, 3, 0] = 255
    X[:, 7, W - 1] = R; X[:, 7, 0] = 255 * (i < 4); X[:, 7, W - 2] = 255
    kind = rng.integers(0, 6, (N, 8, CELLS, 1)); slot = rng.integers(0, 16, (N, 8, CELLS, 1)); coin = rng.integers(0, 2, (N, 8, CELLS, 16))
    on = np.where(kind == 0, 0, np.where(kind == 1, i == slot, np.where(kind == 2, (i == 0) | (i == 15), np.where(kind == 3, 1, coin))))
    ce = (W - 1) * on.astype(np.int64)
    ce = np.where((kind == 5) & (rng.random(ce.shape) < 0.5), rng.integers(0, W, ce.shape), ce)
    ce[:, 7, CELLS - 1] = 0; ce[:, 7, CELLS - 1, 15] = W - 1; ce[:, 7, 0] = 0; ce[:, 7, 0, 14:] = W - 2
    v = np.where(rng.random((N, 8, K)) < 0.8, (CELLS - 1) * rng.integers(0, 2, (N, 8, K)), rng.integers(0, CELLS, (N, 8, K)))
    v[:, :, 0] = 0; v[:, :, K - 1] = CELLS - 1; v[:, 7, K - 2] = 0
    z = mix(K); z[:, 6] = np.where(rng.random((N, K, 1)) < 0.8, 255, z[:, 6]); z[:, 7, K - 2:] = 255; z[:, :, K - 1] = 255
    kp = np.where(rng.random((N, 8, 16, 16)) < 0.15, rng.integers(0, 256, (N, 8, 16, 16)), 255 * rng.integers(0, 2, (N, 8, 16, 16)))
    wv = np.where(rng.random((N, 8, 16)) < 0.15, rng.integers(0, 256, (N, 8, 16)), 255 * rng.integers(0, 2, (N, 8, 16)))
    kp[:, 6] = 255; wv[:, 6] = 255
    last = np.where(i == 0, 255, np.where(i == 1, 2, 0))
    wv[:, 7] = np.where(i < 9, last, wv[:, 7]); kp[:, 7, :, 15] = np.where(i < 9, last, kp[:, 7, :, 15])
    ce[:, 4, CELLS - 1] = 0; ce[:, 4, 0] = i + 1
    X[:, 4, 1] = 255 * (i < 2); X[:, 4, 2:17] = 255 * (i >= 2)
    ce[:, 5, CELLS - 1] = (W - 1) * (i == 0); ce[:, 5, 0] = (W - 1) * (i == 0); wv[:, 5] = last
    kp[:, 5] = 255 * (kp[:, 5] > 127); X[:, 5, (65025 * np.arange(17)) & (W - 1)] = 0
    ce[:, 2, CELLS - 1] = np.where(i < 15, 1 + i % 10, W - 1); ce[:, 2, CELLS - 256] = 0; wv[:, 2] = last
    X[:, 2, 1:11] = 255; X[:, 2, 1:11, 0] = 254 - np.arange(10)
    return pack(X, ce, v, z, kp, wv)
def setup_inputs_corners(rng):
    X, ce, v, z, kp, wv = parts(rng, np.full(8, 12)); T = 64
    X = np.where(rng.random(X.shape) < 0.5, rng.integers(100, 128, X.shape), rng.integers(0, 21, X.shape))
    for g in range(8):
        ba = rng.integers(128, 224, (T, 16))
        for r in range(N):
            pl = (ba @ kp[r, g]) & (W - 1); cl = (ba @ wv[r, g]) & (CELLS - 1)
            own = rng.permutation(np.setdiff1d(np.arange(W), pl))[:5 * T].reshape(5, T)
            X[r, g, own[0]] = ba
            for i in range(1, 4): X[r, g, own[i]] = ba - cut(TH1 - 2 + i)
            st = rng.permutation(np.setdiff1d(np.arange(CELLS), cl))[:T]; ce[r, g, st, rng.integers(0, 16, T)] = own[0]
            for t in range(T):
                qs = rng.permutation(16); am = int(rng.choice(np.array([0, TH2 - 1, TH2, TH2 + 1])))
                X[r, g, pl[t, qs[1]]] = ba[t] - cut(am + int(rng.integers(0, 2))); X[r, g, pl[t, qs[0]]] = ba[t] - cut(am)
                n = int(rng.choice(np.array([0, 1, 1, 2, 2, 3, 15, 16])))
                ce[r, g, cl[t]] = rng.permutation(np.concatenate([own[rng.integers(0, 2, n), t], own[rng.integers(2, 5, 16 - n), t]]))
            tl = rng.permutation(np.arange(K) % T); v[r, g] = st[tl]; z[r, g] = ba[tl]
    return pack(X, ce, v, z, kp, wv)
def setup_inputs_crowd(rng):
    fam = np.full(8, 10); fam[4] = 1
    X, ce, v, z, kp, wv = parts(rng, fam); X[:, 5] = rng.integers(0, 256, (N, W, 16))
    for g in (0, 1, 4, 5):
        v[:, g] = v[:, g, :1].copy(); z[:, g] = z[:, g, :1].copy()
    for g in (1, 5):
        for r in range(N):
            o = int(rng.choice(np.array([0, K - 1, int(rng.integers(0, K))])))
            v[r, g, o] = (v[r, g, o] + 1 + int(rng.integers(0, CELLS - 1))) % CELLS; z[r, g, o] = rng.integers(0, 256, 16)
    wv[:, 2] = 0; kp[:, 2] = 0; kp[:, 6] = 0; v[:, 3] = v[:, 3, :1].copy()
    return pack(X, ce, v, z, kp, wv)
def setup_inputs_ties(rng):
    X, ce, v, z, kp, wv = parts(rng, np.full(8, 12)); val = np.array([0, 64, 128, 255])
    for g in range(8):
        a = rng.choice(val, (12, 16)); b = rng.choice(val, (6, 8))
        pool = np.concatenate([a, a[:, ::-1], np.concatenate([b, b[:, ::-1]], axis=1)])
        X[:, g] = pool[rng.integers(0, 30, (N, W))]
    h = rng.choice(val, (N, 8, K, 8)); z = np.concatenate([h, h[..., ::-1]], axis=3)
    return pack(X, ce, v, z, kp, wv)
def check_inputs(d):
    bad = []
    for k, hi in (("px", 255), ("ce", W - 1), ("v0", CELLS - 1), ("z0", 255), ("kap", 255), ("wu", 255)):
        a = np.asarray(d[k]).astype(np.float64)
        if not (np.min(a) >= 0 and np.max(a) <= hi): bad.append("range of " + k)
        elif not np.all(a == np.floor(a)): bad.append("whole numbers in " + k)
    return bad
def ints(a):
    return a.astype(np.float32).astype(np.int64)
def first(key):
    w = np.zeros(key.shape, bool)
    for g in range(8): w[g, np.unique(key[g], return_index=True)[1]] = True
    return w
def one(a, k):
    return np.take_along_axis(a, k.reshape(8, K, *([1] * (a.ndim - 2))), 2)[:, :, 0]
def reference(px, ce, v0, z0, kap, wu):
    X = ints(px).reshape(N, 8, 16, W).transpose(0, 1, 3, 2).copy()
    C = ce.astype(np.int64).reshape(N, 8, 16, CELLS).transpose(0, 1, 3, 2).copy()
    kp = ints(kap).reshape(N, 8, 16, 16); wv = ints(wu).reshape(N, 8, 16)
    v = [gentries(a).astype(np.int64) for a in v0]; z = [a for a in ints(z0).reshape(N, 8, 16, K).transpose(0, 1, 3, 2)]
    al = [np.zeros((8, K), np.int64) for p in range(N)]
    g2 = np.arange(8)[:, None]; g3 = g2[:, :, None]; lane = np.arange(K)[None, :] + np.zeros((8, 1), np.int64)
    for t in range(RO):
        hx = []; hn = []
        for p in range(N):
            L = C[p][g2, v[p]]; x = X[p][g3, L]
            k = np.argmax(np.add.reduce(np.minimum(x, z[p][:, :, None, :]), axis=3), axis=2)
            hx.append(one(x, k)); hn.append(one(L, k))
        nv = []; nz = []; na = []; F = []; nm = []; live = []
        for p in range(N):
            o = (p - 1) % N; x = hx[o]; zz = z[o]; a = al[o]
            b = np.add.reduce(wv[p][:, None, :] * x, axis=2) & (CELLS - 1)
            M = C[p][g2, b]; y = X[p][g3, M]
            d = np.add.reduce(np.abs(y - x[:, :, None, :]), axis=3); j = np.argmin(d, axis=2)
            ex = np.add.reduce((d < TH1).astype(np.int64), axis=2) >= 2 + (a & 1)
            s = np.add.reduce(np.minimum(y, x[:, :, None, :]), axis=3); np.put_along_axis(s, j[:, :, None], -1, 2); m = np.argmax(s, axis=2)
            yj = one(y, j); Mj = one(M, j)
            F.append(np.maximum(x, one(y, m))); nm.append(one(M, m)); live.append(~ex)
            win = first(np.where(ex, Mj, W + b)); new = (yj + x) >> 1
            g, l = np.nonzero(win & ex); X[p][g, Mj[g, l]] = new[g, l]
            g, l = np.nonzero(win & ~ex); C[p][g, b[g, l], j[g, l]] = hn[o][g, l]
            nz.append(np.where(ex[:, :, None], np.abs(zz - yj), zz)); na.append(a + ex); nv.append(b)
        for p in range(N):
            o = (p - 1) % N; f = F[o]; on = live[o]
            c = (f @ kp[p]) & (W - 1); w = X[p][g3, c]
            d = np.add.reduce(np.abs(w - f[:, :, None, :]), axis=3); q = np.argmin(d, axis=2)
            rec = one(d, q) < TH2; cq = one(c, q); wq = one(w, q); cc = cq & (CELLS - 1)
            win = first(np.where(on, np.where(rec, cq, W + cc), -1 - lane)) & on; new = (wq + f) >> 1
            g, l = np.nonzero(win & rec); X[p][g, cq[g, l]] = new[g, l]
            g, l = np.nonzero(win & ~rec); C[p][g, cc[g, l], q[g, l]] = nm[o][g, l]
            nz[o] = np.where(on[:, :, None], (nz[o] + wq) >> 1, nz[o])
        v = nv; z = nz; al = na
    return {"yx": X.transpose(0, 1, 3, 2).reshape(N, 128, W).astype(np.float32).astype(BF), "yc": C.transpose(0, 1, 3, 2).reshape(N, 128, CELLS).astype(np.float32),
            "yz": np.stack(z).transpose(0, 1, 3, 2).reshape(N, 128, K).astype(np.float32).astype(BF), "yv": np.stack([gtable(a) for a in v]).astype(np.float32), "ya": np.stack(al).astype(np.float32)}

@@ -1,0 +1,597 @@
+import numpy as np
+from concourse.mybir import AluOpType, ActivationFunctionType
+
+RO = 3
+BIG = float(1 << 21)
+MAGIC = 12582912.0
+BLK = 64
+NSH = (BLK - 1 + 14) // 15
+NC = BLK // 16
+TABW = 2560 + BLK
+YH = 2064
+LOADC = True
+ENDC = True
+SCANI = True
+HS = (1, 0)
+XBF = False
+G1 = (("v", 0, 32), ("s", 32, 64), ("v", 64, 80), ("s", 80, 128), ("s", 128, 192), ("s", 192, 256))
+G2 = (("v", 0, 64), ("s", 64, 128), ("v", 128, 144), ("v", 144, 160), ("s", 160, 192), ("s", 192, 256))
+GATHER = {1: G2, 2: G2, 3: G2} if XBF else {1: G1, 2: G1, 3: G1}
+M1 = ((0, 128), (128, 256)) if XBF else ((0, 64), (64, 128), (128, 192), (192, 256))
+MINS = {1: M1, 2: M1, 3: M1}
+EST = {"cy": 0.83, "gam": 1.5, "sca": 3.8, "pe": 0.5, "same": 60.0, "other": 100.0, "rem": 2200.0, "rbw": 40.0, "dma": 2000.0, "xbf": 0.5}
+
+S_, P_ = "sbuf", "psum"
+F32, BF, I32, U16 = "float32", "bfloat16", "int32", "uint16"
+SCRATCH = {
+    "tab": (S_, [128, TABW], F32), "pxs": (S_, [128, 2048], BF), "ces": (S_, [128, 512], I32),
+    "v0s": (S_, [128, 16], I32), "kaps": (S_, [128, 16], BF), "wus": (S_, [128, 8], BF),
+    "Y": (S_, [128, 2 * YH], BF), "M": (S_, [128, 4096], BF),
+    "offn": (S_, [128, 256], U16), "nf": (S_, [128, 768], F32), "nf2": (S_, [128, 256], F32),
+    "ci": (S_, [128, 256], I32), "cj": (S_, [128, 256], I32), "ck": (S_, [128, 256], I32),
+    "bu": (S_, [128, 16], U16), "bi": (S_, [128, 16], I32), "bj": (S_, [128, 16], I32), "bs": (S_, [128, 256], I32 if SCANI else F32),
+    "bt": (S_, [128, 16], I32), "btj": (S_, [128, 16], I32), "vf": (S_, [128, 16], F32),
+    "so": (S_, [128, 512], I32 if SCANI else F32), "sc": (S_, [128, 256], F32), "ind": (S_, [128, 256], BF), "ko": (S_, [128, 256], F32),
+    "ki": (S_, [128, 32], I32), "jj": (S_, [128, 16], I32), "mj": (S_, [128, 16], I32), "mi": (S_, [128, 16], I32),
+    "mm": (S_, [128, 16], I32), "cq": (S_, [128, 16], I32), "tA": (S_, [128, 16], F32), "thr": (S_, [128, 32], F32),
+    "dn": (S_, [128, 16], F32), "qd": (S_, [128, 16], F32), "wf": (S_, [128, 16], F32),
+    "noh": (S_, [128, 256], BF), "ex": (S_, [128, 256], BF), "go": (S_, [128, 16], U16), "gs": (S_, [128, 16], U16),
+    "nm": (S_, [128, 256], F32), "vt": (S_, [128, 160], F32),
+    "tf": (S_, [128, 256], F32), "tb": (S_, [128, 512], BF), "tn": (S_, [128, 256], F32),
+    "s1": (S_, [128, 256], F32), "s2": (S_, [128, 256], F32), "E": (S_, [128, 256 * NSH], BF),
+    "ku": (S_, [128, 16], U16), "wo": (S_, [128, 16], U16),
+    "xe": (S_, [128, 256], BF), "r2": (S_, [128, 256], F32), "bc": (S_, [128, 256], BF), "tt": (S_, [128, 512], F32),
+    "val": (S_, [128, 256], I32), "ey": (S_, [128, 256], BF), "z1": (S_, [128, 256], BF), "lz": (S_, [128, 256], BF),
+    "zm": (S_, [128, 256], F32), "at": (S_, [128, 128], F32),
+    "sx": (S_, [128, 256 * RO], BF), "lx": (S_, [128, 256 * RO], BF),
+    "sz": (S_, [128, 256 * (RO + 1)], BF), "lzz": (S_, [128, 256 * RO], BF),
+    "sna": (S_, [128, 32 * (RO + 1)], F32), "lna": (S_, [128, 32 * RO], F32),
+    "sf": (S_, [128, 256 * RO], BF), "lf": (S_, [128, 256 * RO], BF),
+    "sme": (S_, [128, 32 * RO], F32), "lme": (S_, [128, 32 * RO], F32),
+    "sw": (S_, [128, 256 * RO], BF), "lw": (S_, [128, 256 * RO], BF),
+    "pi": (S_, [128, 8], I32), "pj": (S_, [128, 8], I32), "col": (S_, [128, 32], F32),
+    "k16": (S_, [128, 128], F32), "ug": (S_, [128, 128], F32), "cexp": (S_, [128, 8], U16),
+    "wm": (S_, [128, 144], F32), "cown": (S_, [128, 128], F32), "cmin": (S_, [128, 128], F32), "c01": (S_, [128, 128], F32),
+    "rows": (S_, [128, 784], BF), "one": (S_, [128, 128], BF), "quart": (S_, [128, 128], BF), "dum": (S_, [128, 8], F32),
+    "bo": (S_, [128, 128], F32), "idf": (S_, [128, 128], F32), "idm2": (S_, [128, 128], F32),
+    "idb": (S_, [128, 640], BF), "bf8": (S_, [128, 8], F32), "bb": (S_, [128, 96], BF),
+    "bx": (S_, [128, 512], BF), "bo4": (S_, [128, 128], BF), "bwu": (S_, [128, 128], BF), "bw8": (S_, [128, 8], BF),
+    "bkap": (S_, [128, 128], BF), "selk": (S_, [128, 256], F32), "selb": (S_, [128, 384], BF),
+    "SA": (P_, [128, 512], F32), "SB": (P_, [128, 512], F32), "xt": (S_, [128, 256], BF),
+    "XA": (P_, [128, 1024], BF) if XBF else (P_, [128, 512], F32), "XB": (P_, [128, 1024], BF) if XBF else (P_, [128, 512], F32),
+    "R1": (P_, [128, 512], F32), "R2": (P_, [128, 512], F32), "R3": (P_, [128, 512], F32), "R4": (P_, [128, 512], F32),
+}
+MSG = ["xa", "xb", "z", "na", "fa", "fb", "ma", "mb", "wa", "wb"]
+NDMA = 16
+SEMAPHORES = (["qv", "qs", "qp", "qg", "sent"] + ["d%d" % i for i in range(NDMA)]
+              + ["%s%d" % (m, t) for m in MSG for t in range(RO)])
+A = AluOpType
+AF = ActivationFunctionType
+QS = ["v", "s", "p", "g", "y"]
+MOVES = ("load", "store", "send", "land")
+
+
+def r(name, a, b, step=1, p=128):
+    return (name, a, b, step, p)
+
+
+def ind(win, off):
+    return ("*", win, off)
+
+
+def plan():
+    ops = []
+
+    def acc(x):
+        if x is None or isinstance(x, (int, float)):
+            return []
+        return [x[1], x[2]] if x[0] == "*" else [x]
+
+    def add(q, kind, o, ins, args):
+        rd, wr = ([o[2]], [o[1]]) if o[0] == "*" else ([], [o])
+        for x in ins:
+            rd = rd + acc(x)
+        ops.append([q, kind, args, rd, wr])
+
+    def cp(o, i): add("v", "cp", o, [i], (o, i))
+    def tt(o, a, b, op): add("v", "tt", o, [a, b], (o, a, b, op))
+    def ts(o, a, s1, op0, s2=None, op1=None): add("v", "ts", o, [a, s1, s2], (o, a, s1, s2, op0, op1))
+    def scan(o, d0, d1, init, op0, op1): add("v", "scan", o, [d0, d1], (o, d0, d1, init, op0, op1))
+    def mset(o, c): add("v", "mset", o, [], (o, c))
+    def act(o, i, f, bias=0.0, scale=1.0): add("s", "act", o, [i], (o, i, f, bias, scale))
+    def mm(o, l, rh, st, sp): add("p", "mm", o, [l, rh], (o, l, rh, st, sp))
+    def iota(o, pat, base, cm): add("g", "iota", o, [], (o, pat, base, cm))
+    def load(q, o, src): ops.append([q, "load", (o, src), [], [o]])
+    def store(q, dst, i): ops.append([q, "store", (dst, i), [i], []])
+
+    def send(name, step, dst, src):
+        ops.append(["g", "send", (name, step, dst, src), [src], []])
+        ops.append([None, "land", (name, step, dst), [], [dst]])
+
+    def hf(name, h, base=0): return r(name, base + 128 * h, base + 128 * h + 128)
+    def sm(name, h, base=0): return r(name, base + 8 * h, base + 8 * h + 8)
+    def ends(name, h, base=0): return r(name, base + 128 * h + 15, base + 128 * h + 128, 16)
+    def c(i): return r("col", i, i + 1)
+    SC = ["SA", "SB"]; XP = ["XA", "XB"]
+    IDB, IDN, ID4, IDH, IDNH = [r("idb", 128 * i, 128 * i + 128) for i in range(5)]
+    IDF = r("idf", 0, 128); K16 = r("k16", 0, 128); UG = r("ug", 0, 128); WM = r("wm", 0, 128); BO = r("bo", 0, 128)
+    WC, GC, P7, P3, W16P, BIGC = c(0), c(1), c(2), c(3), c(4), c(5)
+    COWN = r("cown", 0, 128); CMIN = r("cmin", 0, 128); CEXP = r("cexp", 0, 8)
+    def selb(i): return r("selb", 128 * i, 128 * i + 128, 1, 40)
+    def row(a, b): return r("rows", a, b, 1, 1)
+    ONE = r("one", 0, 128, 1, 1); QUART = r("quart", 0, 128, 1, 1)
+    PLAS = r("tab", 0, 2048); CELL = r("tab", 2048, 2560); TAB = r("tab", 0, TABW)
+    def YW(h): return r("Y", YH * h, YH * h + YH)
+    def ycol(l): return YH * (l // 128) + 16 + 16 * (l % 128)
+
+    load("y", r("v0s", 0, 16), ("v0", None)); load("s", r("ces", 0, 512), ("ce", None))
+    load("y", r("pxs", 0, 1024), ("px", (0, 1024))); load("s", r("pxs", 1024, 2048), ("px", (1024, 2048)))
+    load("y", r("sz", 0, 256), ("z0", None))
+    load("y", r("wus", 0, 1), ("wu", None)); load("y", r("kaps", 0, 16), ("kap", None))
+    iota(r("pi", 0, 1), [[0, 1]], 0, 1)
+    iota(K16, [[0, 8], [1, 16]], 0, 0)
+    iota(UG, [[1, 8], [0, 16]], 0, 0)
+    iota(row(128, 256), [[0, 8], [1, 16]], -16, 0)
+    iota(row(768, 776), [[256, 8]], 0, 0)
+    send("z0", 1, r("lzz", 0, 256), r("sz", 0, 256))
+    if LOADC:
+        for j in range(4): act(r("tab", 512 * j, 512 * j + 512), r("pxs", 512 * j, 512 * j + 512), AF.Copy)
+    else:
+        load("g", PLAS, ("px", None))
+    iota(row(0, 128), [[0, 8], [4096, 16]], 0, 0)
+    iota(row(256, 384), [[0, 8], [512, 16]], 0, 0)
+    iota(row(384, 512), [[0, 8], [2048, 16]], 0, 0)
+    mset(r("rows", 512, 640), -2040.0 * 8192); mset(r("rows", 640, 768), -300.0 * 32768)
+    mset(r("one", 0, 128), 1.0); mset(r("Y", 0, 16), 0.0); mset(r("Y", YH, YH + 16), 0.0); mset(r("sna", 16, 32), 0.0)
+    ts(r("pj", 0, 1), r("pi", 0, 1), 15, A.bitwise_and); ts(r("pj", 1, 2), r("pi", 0, 1), 4, A.logical_shift_right)
+    ts(r("pj", 2, 3), r("pi", 0, 1), 7, A.bitwise_and); ts(r("pj", 3, 4), r("pi", 0, 1), 3, A.logical_shift_right)
+    cp(r("col", 0, 4), r("pj", 0, 4))
+    ts(W16P, WC, 16.0, A.mult, 16.0, A.add)
+    ts(BO, UG, GC, A.is_equal)
+    ts(WM, K16, WC, A.is_equal)
+    tt(IDB, BO, WM, A.mult)
+    ts(r("bf8", 0, 8), r("k16", 0, 8), GC, A.is_equal)
+    ts(r("bb", 0, 8), r("bf8", 0, 8), -16.0, A.mult)
+    cp(r("bb", 8, 16), r("bf8", 0, 8))
+    cp(r("bu", 0, 16), r("v0s", 0, 16))
+    cp(CEXP, r("k16", 0, 8))
+    ts(CMIN, K16, 0.0, A.is_equal, float(1 << 30), A.mult)
+    cp(CELL, r("ces", 0, 512))
+    cp(c(6), r("wus", 0, 1))
+    ts(r("bwu", 0, 128), BO, c(6), A.mult)
+    ts(r("bw8", 0, 8), r("bf8", 0, 8), c(6), A.mult)
+    cp(r("wm", 128, 144), r("wm", 0, 16))
+    ts(r("s1", 0, 128), r("wm", 15, 143), BIG, A.mult)
+    ts(r("s2", 0, 128), WM, -2 * BIG, A.mult)
+    tt(COWN, r("s1", 0, 128), r("s2", 0, 128), A.add)
+    ts(r("c01", 0, 128), K16, 0.0, A.not_equal)
+    act(IDF, IDB, AF.Copy)
+    mset(r("bb", 24, 32), 0.0); mset(r("bx", 128, 256), 0.0)
+    ts(r("bb", 16, 24), r("bf8", 0, 8), 65536.0, A.mult)
+    ts(r("bb", 32, 40), r("bf8", 0, 8), -131072.0, A.mult); cp(r("bb", 40, 48), r("bb", 0, 8))
+    act(r("bx", 0, 128), BO, AF.Identity, 0.0, 65536.0)
+    ts(BIGC, WC, 15.0, A.not_equal, BIG, A.mult)
+    ts(c(7), WC, 2560.0, A.add); tt(c(8), c(7), BIGC, A.add)
+    for j in range(8 // NC):
+        ts(r("dum", NC * j, NC * j + NC), r("k16", 0, NC), 16.0, A.mult, c(8), A.add)
+    ts(c(16), P3, 1.0, A.is_equal)
+    ts(c(17), P3, 1.0, A.is_equal, 2047.0, A.mult); ts(c(18), P3, 3.0, A.is_equal, 4095.0, A.mult)
+    ts(c(24), P3, 4.0, A.not_equal); ts(c(25), P3, 4.0, A.is_equal, BIG, A.mult)
+    tt(c(19), c(17), c(18), A.add); tt(c(20), c(19), c(24), A.add); tt(c(26), c(20), c(25), A.add)
+    ts(r("selk", 0, 128), UG, P7, A.is_equal, c(20), A.mult)
+    ts(r("selk", 128, 256), UG, P7, A.is_equal, c(26), A.mult)
+    for i, w in enumerate((-256.0, 4096.0, 0.5)):
+        ts(c(21 + i), c(16), w, A.mult)
+        ts(r("selb", 128 * i, 128 * i + 128), UG, P7, A.is_equal, c(21 + i), A.mult)
+    for ap, w in ((IDN, -1.0), (ID4, -4096.0), (IDH, 0.5), (IDNH, -0.5), (r("idm2", 0, 128), -2.0)):
+        act(ap, IDB, AF.Identity, 0.0, w)
+    act(r("bo4", 0, 128), BO, AF.Identity, 0.0, 4096.0)
+    mset(r("quart", 0, 128), -0.25); mset(r("tab", 2560, TABW), 0.0)
+    for j in range(4):
+        mset(r("vt", 40 * j + 32, 40 * j + 40), 1.0)
+        if j < 2: mset(r("vt", 40 * j + 24, 40 * j + 32), 0.0)
+    for i, w in enumerate((8192.0, 32768.0, -16384.0, -65536.0)):
+        ts(r("bb", 48 + 8 * i, 56 + 8 * i), r("bf8", 0, 8), w, A.mult)
+    act(r("bx", 256, 384), BO, AF.Identity, 0.0, 8192.0); act(r("bx", 384, 512), BO, AF.Identity, 0.0, 32768.0)
+    for g8 in range(8):
+        tt(r("bkap", 16 * g8, 16 * g8 + 16), r("kaps", 0, 16), r("bo", 16 * g8, 16 * g8 + 16), A.mult)
+
+    def to_psum(h, x):
+        if XBF:
+            add("p", "tr", r(XP[h], 128, 256), [x, IDB], (r(XP[h], 128, 256), x, IDB))
+            act(hf("xt", h), r(XP[h], 128, 256), AF.Copy)
+            add("p", "tr", r(XP[h], 0, 128), [hf("xt", h), IDB], (r(XP[h], 0, 128), hf("xt", h), IDB))
+        else:
+            mm(r(XP[h], 0, 128), IDB, x, True, True)
+
+    for h in range(2):
+        to_psum(h, hf("sz", h))
+
+    def scores(step, h, win, x):
+        nf = hf("nf", h, 256 * (step - 1))
+        if step == 1:
+            mm(r(SC[h], 0, 128), ONE, row(128, 256), True, False)
+        else:
+            o = 256 * (step - 2)
+            mm(r(SC[h], 0, 256), ONE, row(o, o + 256), True, False)
+            if step == 3: mm(r(SC[h], 0, 256), ONE, row(512, 768), False, False)
+            mm(r(SC[h], 0, 256), x, r("bx", o, o + 256), False, False)
+        for q, a, b in GATHER[step]:
+            a, b = a ^ (128 * HS[0]), (a ^ (128 * HS[0])) + b - a
+            if a // 128 == h:
+                o = r("Y", ycol(a), ycol(a) + 16 * (b - a)); i = ind(win, r("offn", a, b))
+                if q == "v": cp(o, i)
+                else: act(o, i, AF.Copy)
+        if step > 1:
+            for k in range(16):
+                mm(r(SC[h], k, 256, 16), r("Y", YH * h + 16 + k, YH * h + YH, 16), r("bb", 16, 32) if step == 2 else r("bb", 48, 64), False, False)
+        for a, b in MINS[step]:
+            if a // 128 == h:
+                for k in range(16):
+                    tt(r("M", 256 * k + a, 256 * k + b), r("Y", ycol(a) + k, ycol(a) + 16 * (b - a), 16), r(XP[h], a - 128 * h, b - 128 * h), A.min)
+        for k in range(16):
+            lm = hf("M", h, 256 * k)
+            if step == 1: mm(r(SC[h], k, 128, 16), lm, r("bb", 0, 8), False, k == 15)
+            else: mm(r(SC[h], k, 256, 16), lm, r("bb", 32, 48) if step == 2 else r("bb", 64, 80), False, False)
+        if step == 2:
+            mm(r(SC[h], 0, 128), nf, IDF, False, True)
+        if step == 3:
+            mm(r(SC[h], 0, 128), hf("nf2", h), IDF, False, False)
+            mm(r(SC[h], 128, 256), nf, IDF, False, True)
+
+    def whole(name, h, base, tmp):
+        if SCANI: return ends(name, h, base)
+        cp(tmp, ends(name, h, base))
+        return tmp
+
+    def names(step, h, win=CELL):
+        cp(hf("offn", h), ind(win, sm("bu", h)))
+        act(hf("nf", h, 256 * (step - 1)), ind(CELL, sm("bu", h)), AF.Copy)
+
+    def to_list(src, h, slots):
+        tt(hf("ex", h), ind(sm(src, h), CEXP), WM, A.mult)
+        mm(sm("R1", h), ONE, row(768, 776), True, False)
+        mm(sm("R1", h), hf("ex", h), r("bb", 8, 16), False, True)
+        if slots: mm(sm("R1", h, 16), hf("ex", h), r("bb", 8, 16), True, True)
+        ts(sm("go", h), sm("R1", h), W16P, A.add)
+        if slots: cp(sm("gs", h), sm("R1", h, 16))
+
+    def pick_name(step, h, dst):
+        tt(hf("nm", h), ind(r("wm", 0, 16), sm("gs", h)), hf("nf", h, 256 * (step - 1)), A.mult)
+        mm(sm("R1", h, 32), hf("nm", h), r("bf8", 0, 8), True, True)
+        act(dst, sm("R1", h, 32), AF.Copy)
+
+    def name_rows(h, src):
+        mm(r("R2", 128, 256, 1, 8), src, IDF, True, True)
+        act(r("tn", 128 * h, 128 * h + 128, 1, 8), r("R2", 128, 256, 1, 8), AF.Copy)
+
+    def write_prep(step, h, x):
+        j = 2 * (step - 2) + h
+        mm(r("R2", 0, 128, 1, 40), r("vt", 40 * j, 40 * j + 40), IDF, True, True)
+        TF = r("tf", 128 * h, 128 * h + 128, 1, 40); TB = r("tb", 128 * j, 128 * j + 128, 1, 40)
+        act(TF, r("R2", 0, 128, 1, 40), AF.Copy)
+        act(TB, r("R2", 0, 128, 1, 40), AF.Copy)
+        KR = r("R1", 256, 384) if XBF else r(XP[h], 0, 128); P = r(SC[h], 0, 128)
+        mm(KR, r("selk", 0, 128, 1, 40), TF, True, True)
+        mm(r("R3", 0, 128), r("selk", 128, 256, 1, 40), TF, True, True)
+        mm(P, r("selk", 0, 128, 1, 40), TF, True, False)
+        scan(hf("s1", h), COWN, KR, -1.0, A.add, A.max)
+        for i in range(NSH):
+            s = 15 * i; e = 256 * i + 128 * h
+            tt(r("E", e + s, e + 128), r("s1", 128 * h, 128 * h + 128 - s), r("R3", s, 128), A.is_equal)
+            mm(r(SC[h], s, 128), r("bo4", 0, 128), r("E", e + s, e + 128), False, i == NSH - 1)
+        o = r("R4", 0, 128)
+        mm(o, hf("noh", h), IDB, True, False); mm(o, selb(2), TB, False, True)
+        o = r("R4", 128, 256)
+        mm(o, IDB, x, True, False); mm(o, selb(0), TB, False, True)
+        o = r("R4", 256, 384)
+        mm(o, r("selk", 0, 128, 1, 8), r("tn", 128 * h, 128 * h + 128, 1, 8), True, False)
+        mm(o, hf("noh", h), ID4, False, False); mm(o, selb(1), TB, False, True)
+        act(hf("xe", h), r("R4", 128, 256), AF.Relu)
+        act(hf("r2", h), r("R4", 256, 384), AF.Relu, -4096.0)
+        act(hf("bc", h), r("R4", 0, 128), AF.Abs, -0.5)
+        o = r("R4", 384, 512)
+        mm(o, ONE, QUART, True, False); mm(o, IDH, hf("xe", h), False, False); mm(o, IDF, hf("r2", h), False, True)
+        T_ = hf("tt", h, 256 * (step - 2))
+        ts(sm("ku", h), ends("s1", h), BIGC, A.subtract, 2560.0, A.min)
+        tt(T_, ind(TAB, sm("ku", h)), hf("bc", h), A.mult)
+        tt(hf("val", h), T_, o, A.add)
+        scan(hf("s2", h), COWN, P, 0.0, A.add, A.max)
+        tt(sm("wf", h), ends("s2", h), r("dum", 0, 8), A.min)
+        ts(sm("wo", h), sm("wf", h), BIGC, A.subtract)
+
+    def scatter():
+        for b in range(256 // BLK - 1, -1, -1):
+            cp(ind(TAB, r("wo", NC * b, NC * b + NC)), r("val", BLK * b, BLK * b + BLK))
+
+    for t in range(RO):
+        o = 256 * t
+        for h in HS: names(1, h, r("ces", 0, 512) if t == 0 else CELL)
+        for h in HS:
+            scores(1, h, r("pxs", 0, 2048) if t == 0 else PLAS, None)
+            scan(hf("so", h), CMIN, r(SC[h], 0, 128), 0.0, A.add, A.min)
+            ts(sm("jj", h), whole("so", h, 0, sm("ki", h)), 15, A.bitwise_and)
+            to_list("jj", h, True)
+            act(hf("sx", h, o), ind(YW(h), sm("go", h)), AF.Copy)
+            send("x%s%d" % ("ab"[h], t), 1, hf("lx", h, o), hf("sx", h, o))
+            pick_name(1, h, sm("sna", h, 32 * t))
+        send("na%d" % t, 1, r("lna", 32 * t, 32 * t + 32), r("sna", 32 * t, 32 * t + 32))
+        for h in HS:
+            x = hf("lx", h, o); bank = r(("R2", "R3")[h], 256, 384)
+            mm(bank, r("bwu", 0, 128), x, True, True)
+            to_psum(h, x)
+            scan(hf("bs", h), COWN, bank, 0.0, A.add, A.max)
+            ts(sm("bj", h), whole("bs", h, 0, sm("bi", h)), 511, A.bitwise_and)
+            cp(sm("bu", h), sm("bj", h))
+            names(2, h)
+        ts(r("thr", 16, 32), r("lna", 32 * t + 16, 32 * t + 32), 1.0, A.is_equal, 2.0, A.mult)
+        act(r("thr", 0, 16), r("thr", 16, 32), AF.Identity, -12.0)
+        for h in HS:
+            x = hf("lx", h, o); v = 40 * h
+            mm(sm("R1", h, 48), x, r("bw8", 0, 8), True, True)
+            cp(sm("bt", h), sm("R1", h, 48)); ts(sm("btj", h), sm("bt", h), 511, A.bitwise_and)
+            name_rows(h, sm("lna", h, 32 * t))
+            scores(2, h, PLAS, x)
+            scan(hf("so", h), CMIN, r(SC[h], 0, 128), 0.0, A.add, A.min)
+            act(hf("ind", h), r(SC[h], 0, 128), AF.Sign, 255.985, -1.0 / 65536)
+            ki = whole("so", h, 0, sm("ki", h))
+            ts(sm("jj", h), ki, 12, A.arith_shift_right, 15, A.bitwise_and)
+            ts(sm("mj", h), ki, 2047, A.bitwise_and)
+            tt(hf("noh", h), ind(sm("jj", h), CEXP), K16, A.not_equal)
+            scan(hf("sc", h), r("c01", 0, 128), hf("ind", h), 0.0, A.mult, A.add)
+            tt(r("vt", v + 8, v + 16), ends("sc", h), sm("thr", h), A.is_lt)
+            tt(sm("tA", h), sm("btj", h), sm("mj", h), A.subtract)
+            cp(r("vt", v + 16, v + 24), sm("mj", h))
+            tt(r("vt", v, v + 8), sm("tA", h), r("vt", v + 8, v + 16), A.mult)
+            tt(hf("ko", h), hf("noh", h), r(SC[h], 128, 256), A.mult)
+            scan(hf("so", h, 256), CMIN, hf("ko", h), 0.0, A.add, A.min)
+            ts(sm("mm", h), whole("so", h, 256, sm("mi", h)), 15, A.bitwise_and)
+            to_list("mm", h, True)
+            tt(hf("sf", h, o), ind(YW(h), sm("go", h)), x, A.max)
+            send("f%s%d" % ("ab"[h], t), 1, hf("lf", h, o), hf("sf", h, o))
+            m = 32 * t + 16 * h; e = r("sme", m + 8, m + 16)
+            act(e, r("vt", v + 8, v + 16), AF.Identity, 1.0, -1.0)
+            pick_name(2, h, r("sme", m, m + 8))
+            send("m%s%d" % ("ab"[h], t), 1, r("lme", m, m + 16), r("sme", m, m + 16))
+            tt(sm("sna", h, 32 * t + 48), sm("lna", h, 32 * t + 16), e, A.add)
+            write_prep(2, h, x)
+        scatter()
+        if t == RO - 1:
+            cp(r("vf", 0, 16), r("bj", 0, 16)); store("y", ("yv", None), r("vf", 0, 16))
+            mm(r("R1", 128, 256, 1, 16), r("sna", 32 * RO + 16, 32 * RO + 32), IDF, True, True)
+            act(r("at", 0, 128, 1, 16), r("R1", 128, 256, 1, 16), AF.Copy)
+            for h in range(2): store("y", ("ya", h), r("at", 0, 128))
+        for h in HS:
+            f = hf("lf", h, o); bank = r(("R2", "R3")[h], 256, 384)
+            mm(bank, r("bkap", 0, 128), f, True, True)
+            to_psum(h, f)
+            cp(hf("ci", h), bank)
+            ts(hf("cj", h), hf("ci", h), 2047, A.bitwise_and)
+            cp(hf("offn", h), hf("cj", h))
+            cp(hf("nf", h, 512), hf("cj", h))
+            ts(hf("ck", h), hf("ci", h), 511, A.bitwise_and)
+            cp(hf("nf2", h), hf("ck", h))
+        for h in HS:
+            TB = r("tb", 128 * h, 128 * h + 128, 1, 40); z = hf("lzz", h, o)
+            mm(r("R4", 0, 128), r("idm2", 0, 128), hf("tt", h), True, False); mm(r("R4", 0, 128), selb(1), TB, False, True)
+            mm(r("R4", 128, 256), IDN, z, True, False); mm(r("R4", 128, 256), selb(0), TB, False, True)
+            act(hf("ey", h), r("R4", 0, 128), AF.Relu, 0.0, -1.0)
+            act(hf("lz", h), r("R4", 128, 256), AF.Relu, -256.0, -1.0)
+            mm(r("R4", 256, 384), IDB, z, True, False); mm(r("R4", 256, 384), IDN, hf("ey", h), False, True)
+            act(hf("z1", h), r("R4", 256, 384), AF.Abs)
+        for h in HS:
+            f = hf("lf", h, o); v = 80 + 40 * h; m = 32 * t + 16 * h
+            name_rows(h, r("lme", m, m + 8))
+            act(r("vt", v + 24, v + 32), r("lme", m + 8, m + 16), AF.Copy)
+            act(sm("dn", h), r("lme", m + 8, m + 16), AF.Identity, 0.0, -8192.0)
+            scores(3, h, PLAS, f)
+            for q in range(2):
+                scan(hf("so", h, 256 * q), CMIN, r(SC[h], 128 * q, 128 * q + 128), 0.0, A.add, A.min)
+            ki = whole("so", h, 0, sm("ki", h))
+            ts(r("vt", v + 8, v + 16), ends("so", h), float((600 - 2040) * 8192), A.is_ge)
+            ts(sm("jj", h), ki, 9, A.arith_shift_right, 15, A.bitwise_and)
+            ts(sm("mj", h), ki, 511, A.bitwise_and)
+            ts(sm("cq", h), whole("so", h, 256, sm("ki", h, 16)), 2047, A.bitwise_and)
+            tt(sm("tA", h), sm("mj", h), sm("cq", h), A.subtract)
+            cp(r("vt", v + 16, v + 24), sm("cq", h))
+            tt(r("vt", v, v + 8), sm("tA", h), r("vt", v + 8, v + 16), A.mult)
+            tt(sm("qd", h), sm("jj", h), sm("dn", h), A.add)
+            to_list("qd", h, False)
+            act(hf("sw", h, o), ind(YW(h), sm("go", h)), AF.Copy)
+            send("w%s%d" % ("ab"[h], t), -1, hf("lw", h, o), hf("sw", h, o))
+            tt(hf("noh", h), ind(sm("jj", h), CEXP), K16, A.not_equal)
+            write_prep(3, h, f)
+        scatter()
+        ZN = r("sz", o + 256, o + 512)
+        for h in HS:
+            p = r("R2", 384, 512)
+            mm(p, ONE, QUART, True, False); mm(p, IDB, hf("z1", h), False, False)
+            mm(p, IDNH, hf("lz", h), False, False); mm(p, IDH, hf("lw", h, o), False, True)
+            act(hf("zm", h), p, AF.Identity, MAGIC)
+            act(hf("sz", h, o + 256), hf("zm", h), AF.Identity, -MAGIC)
+            if t < RO - 1: to_psum(h, hf("sz", h, o + 256))
+        if t < RO - 1:
+            send("z%d" % (t + 1), 1, r("lzz", o + 256, o + 512), ZN)
+        else:
+            store("y", ("yc", None), CELL); store("s", ("yz", None), ZN)
+            if ENDC:
+                cp(r("pxs", 0, 1024), r("tab", 0, 1024)); store("y", ("yx", (0, 1024)), r("pxs", 0, 1024))
+                act(r("pxs", 1024, 2048), r("tab", 1024, 2048), AF.Copy); store("s", ("yx", (1024, 2048)), r("pxs", 1024, 2048))
+            else:
+                store("g", ("yx", None), PLAS)
+    return ops
+
+
+def needs(ops):
+    seen = {n: [] for n in SCRATCH}
+    run = {n: [None, [], []] for n, s in SCRATCH.items() if s[0] == P_}
+    deps = []; after = []
+    for i, (q, kind, args, rd, wr) in enumerate(ops):
+        d = set(); f = set()
+        for (n, a, b, st, p) in rd:
+            d.update(j for (j, a2, b2, w) in seen[n] if w and a2 < b and a < b2)
+        for (n, a, b, st, p) in wr:
+            d.update(j for (j, a2, b2, w) in seen[n] if a2 < b and a < b2)
+        for n in set(x[0] for x in rd + wr):
+            if n in run:
+                if run[n][0] != q: run[n] = [q, [], run[n][1]]
+                d.update(run[n][2])
+                if q == "p" and run[n][1]: f.add(run[n][1][-1])
+                run[n][1].append(i)
+        if q == "p":
+            f.update(j for j in d if ops[j][0] == "p"); d = set(j for j in d if ops[j][0] != "p")
+        for (n, a, b, st, p) in wr:
+            if st == 1 and p == 128 and args[0][0] != "*": seen[n] = [x for x in seen[n] if not (a <= x[1] and x[2] <= b)]
+            seen[n].append((i, a, b, True))
+        for (n, a, b, st, p) in rd:
+            seen[n].append((i, a, b, False))
+        d.discard(i)
+        deps.append(d); after.append(f)
+    return deps, after
+
+
+def cost(o):
+    q, kind, a, rd, wr = o
+    E = EST
+    def n(x): return 16 * n(x[2]) if x[0] == "*" else len(range(x[1], x[2], x[3]))
+    def two(x): return SCRATCH[x[0]][2] in (BF, U16)
+    if kind == "land": return 0.0, E["rem"] + n(a[2]) * 128 * (2 if two(a[2]) else 4) / E["rbw"]
+    if kind == "send": return 300.0, 0.0
+    if kind in ("load", "store"):
+        x = a[0] if kind == "load" else a[1]
+        return (1000.0 if q == "g" else 100.0), E["dma"] + n(x) * 128 * (2 if two(x) or a[0][0] == "yx" else 4) / 200.0
+    if kind == "iota": return 130 + 2 * E["cy"] * n(a[0]), 0.0
+    if kind == "tt" and a[1][0] != "*" and a[2][0] in ("XA", "XB") and XBF: return max(64, n(a[0]) * E["xbf"]) * E["cy"], 0.0
+    if kind in ("mm", "tr"): return max(min(64, n(a[1])), n(a[2])) * E["pe"] * (1 if two(a[1]) else 4), 60.0
+    if a[0][0] == "*": return 50 + n(a[0]) * E["sca"] * E["cy"], 0.0
+    if kind != "mset" and a[1][0] == "*": return (50 if q == "v" else 65) + n(a[0]) * E["gam"] * E["cy"], 0.0
+    m = 1.0
+    if kind == "tt" and SCRATCH[a[1][0]][0] == SCRATCH[a[2][0]][0]: m = 2.0
+    if kind in ("cp", "ts") and two(a[0]) and two(a[1]): m = 0.5
+    return max(64, n(a[0]) * m) * E["cy"], 0.0
+
+
+def arrange(ops):
+    deps, after = needs(ops)
+    N = len(ops); cs = [cost(o) for o in ops]
+    pre = [dict() for o in ops]
+    for i, o in enumerate(ops):
+        for j in after[i]: pre[i][j] = cs[j][0]
+        for j in deps[i]: pre[i][j] = cs[j][0] + cs[j][1] + (EST["same"] if ops[j][0] == o[0] else EST["other"])
+        if o[1] == "land": pre[i][i - 1] = cs[i - 1][0]
+    left = [cs[i][0] + cs[i][1] for i in range(N)]
+    nxt = [[] for o in ops]
+    for i in range(N - 1, -1, -1):
+        for j, w in pre[i].items():
+            left[j] = max(left[j], w + left[i]); nxt[j].append(i)
+    todo = [len(p) for p in pre]; ready = [0.0] * N
+    pool = {q: [] for q in QS + [None]}; free = {q: 0.0 for q in pool}
+    for i in range(N):
+        if not todo[i]: pool[ops[i][0]].append(i)
+    out = []
+    while len(out) < N:
+        t, q = min((max(free[q], min(ready[i] for i in p)), k) for k, (q, p) in enumerate(pool.items()) if p)
+        q = list(pool)[q]
+        i = max((i for i in pool[q] if ready[i] <= t + 1.0), key=lambda i: left[i])
+        soon = [j for j in pool[q] if t < ready[j] < t + 0.6 * cs[i][0] and left[j] > left[i] + cs[i][0]]
+        if soon and q is not None:
+            i = min(soon, key=lambda j: ready[j]); t = ready[i]
+        pool[q].remove(i); out.append(i)
+        if q is not None: free[q] = t + cs[i][0]
+        for j in nxt[i]:
+            ready[j] = max(ready[j], t + pre[j][i]); todo[j] -= 1
+            if not todo[j]: pool[ops[j][0]].append(j)
+    pos = {i: k for k, i in enumerate(out)}
+    return [ops[i] for i in out], [sorted((pos[j] for j in deps[i]), reverse=True) for i in out]
+
+
+def waits_of(ops, deps):
+    known = {q: {} for q in QS}
+    clock = [None] * len(ops); waits = [[] for o in ops]
+    def chan(j): return ("d", j) if ops[j][1] in MOVES else ("c", ops[j][0])
+    for i, o in enumerate(ops):
+        if o[0] is None:
+            clock[i] = {chan(i): i}
+            continue
+        kn = known[o[0]]
+        for j in deps[i]:
+            if kn.get(chan(j), -1) < j:
+                waits[i].append(j)
+                for c2, v in clock[j].items():
+                    if kn.get(c2, -1) < v: kn[c2] = v
+        clock[i] = dict(kn); clock[i][chan(i)] = i
+    return waits
+
+
+PROGRAM = []
+
+
+def rank_program(g, core, T, topo):
+    rank = T.rank_of(core)
+    if rank is None:
+        return
+    n = len(T.cores)
+    if not PROGRAM:
+        ops, deps = arrange(plan())
+        PROGRAM.extend([ops, waits_of(ops, deps)])
+    ops, waits = PROGRAM
+    Q = {"v": g.vector, "s": g.scalar, "p": g.tensor, "g": g, "y": g.sync}
+    need = set(j for w in waits for j in w)
+    sig = {}; cnt = {q: 0 for q in QS}; nd = 0
+    for i, o in enumerate(ops):
+        if o[1] in ("load", "store"):
+            sig[i] = ("d%d" % nd, 16); nd += 1
+        elif o[1] == "land":
+            sig[i] = (o[2][0], len(topo.engines(T.cores[(rank - o[2][1]) % n], core)))
+        elif o[1] != "send" and i in need:
+            cnt[o[0]] += 1; sig[i] = ("q" + o[0], cnt[o[0]])
+
+    def ap(x):
+        if x is None or isinstance(x, (int, float)):
+            return x
+        if x[0] == "*":
+            return ap(x[1]).indirect(ap(x[2]))
+        return T[x[0]][0:x[4], x[1]:x[2]:x[3]] if x[3] != 1 else T[x[0]][0:x[4], x[1]:x[2]]
+
+    sent = 0; stores = []
+    for i, (q, kind, a, rd, wr) in enumerate(ops):
+        if kind == "land":
+            continue
+        e = Q[q]
+        for j in waits[i]:
+            e.wait_ge(T.sem[sig[j][0]], sig[j][1])
+        if kind == "send":
+            dst = T.cores[(rank + a[1]) % n]
+            rid, pid = topo.addr(dst, core)
+            g.remote_dma(ap(a[2]), ap(a[3]), T.sem[a[0]], T.sem.sent, pid, rid, topo.mask(core, dst))
+            sent += len(topo.engines(core, dst))
+            continue
+        if kind == "load":
+            src = T[a[1][0]]
+            ins = e.dma_start(ap(a[0]), src[:, :] if a[1][1] is None else src[:, a[1][1][0]:a[1][1][1]])
+        elif kind == "store":
+            dst = T[a[0][0]]; h = a[0][1]
+            if h is None: ins = e.dma_start(dst[:, :], ap(a[1]))
+            elif a[0][0] == "yx": ins = e.dma_start(dst[:, h[0]:h[1]], ap(a[1]))
+            else: ins = e.dma_start(dst[:, 128 * h:128 * h + 128], T[a[1][0]][8 * h:8 * h + 8, 0:128])
+            stores.append(i)
+        elif kind == "cp": ins = e.tensor_copy(ap(a[0]), ap(a[1]))
+        elif kind == "tt": ins = e.tensor_tensor(ap(a[0]), ap(a[1]), ap(a[2]), a[3])
+        elif kind == "ts":
+            if a[5] is None: ins = e.tensor_scalar(ap(a[0]), ap(a[1]), ap(a[2]), None, a[4])
+            else: ins = e.tensor_scalar(ap(a[0]), ap(a[1]), ap(a[2]), ap(a[3]), a[4], a[5])
+        elif kind == "scan": ins = e.tensor_tensor_scan(ap(a[0]), ap(a[1]), ap(a[2]), a[3], a[4], a[5])
+        elif kind == "mset": ins = e.memset(ap(a[0]), a[1])
+        elif kind == "act":
+            if a[2] == AF.Copy: ins = e.activation(ap(a[0]), ap(a[1]), a[2])
+            else: ins = e.activation(ap(a[0]), ap(a[1]), a[2], bias=a[3], scale=a[4])
+        elif kind == "mm": ins = e.matmul(ap(a[0]), ap(a[1]), ap(a[2]), a[3], a[4])
+        elif kind == "tr": ins = e.transpose(ap(a[0]), ap(a[1]), ap(a[2]))
+        elif kind == "iota":
+            if SCRATCH[a[0][0]][2] == I32: ins = e.iota(ap(a[0]), a[1], a[2], a[3])
+            else: ins = e.iota(ap(a[0]), a[1], a[2], a[3], allow_small_or_imprecise_dtypes=True)
+        if i in sig:
+            ins.then_inc(T.sem[sig[i][0]], 16 if kind in ("load", "store") else 1)
+    for i in stores:
+        Q[ops[i][0]].wait_ge(T.sem[sig[i][0]], 16)
+    g.wait_ge(T.sem.sent, sent)

@@ -5,74 +5,77 @@ RO = 3
 BIG = float(1 << 21)
 MAGIC = 12582912.0
 BLK = 64
-NSH = (BLK - 1 + 14) // 15
+NSH = BLK // 16
 NC = BLK // 16
 TABW = 2560 + BLK
 YH = 2064
-LOADC = True
-ENDC = True
-SCANI = True
-HS = (1, 0)
-XBF = False
-G1 = (("v", 0, 32), ("s", 32, 64), ("v", 64, 80), ("s", 80, 128), ("s", 128, 192), ("s", 192, 256))
-G2 = (("v", 0, 64), ("s", 64, 128), ("v", 128, 144), ("v", 144, 160), ("s", 160, 192), ("s", 192, 256))
-GATHER = {1: G2, 2: G2, 3: G2} if XBF else {1: G1, 2: G1, 3: G1}
-M1 = ((0, 128), (128, 256)) if XBF else ((0, 64), (64, 128), (128, 192), (192, 256))
+GA = (("v", 0, 16), ("s", 16, 64), ("s", 64, 96), ("s", 96, 128))
+GATHER = {1: GA, 2: GA, 3: GA}
+M1 = ((0, 64), (64, 128))
 MINS = {1: M1, 2: M1, 3: M1}
-EST = {"cy": 0.83, "gam": 1.5, "sca": 3.8, "pe": 0.5, "same": 60.0, "other": 100.0, "rem": 2200.0, "rbw": 40.0, "dma": 2000.0, "xbf": 0.5}
+BIAS = 1500.0
+PASSES = 100
+SPLIT = False
+SEED = 1
+NOISE = 500.0
+OFFS = False
+WAW = False
+INFO = []
+EST = {"cy": 0.83, "gam": 1.5, "sca": 3.8, "pe": 0.5, "same": 60.0, "other": 100.0, "rem": 2200.0, "rbw": 40.0, "dma": 2000.0}
 
 S_, P_ = "sbuf", "psum"
 F32, BF, I32, U16 = "float32", "bfloat16", "int32", "uint16"
+H = "float16"
+VT = 56
 SCRATCH = {
-    "tab": (S_, [128, TABW], F32), "pxs": (S_, [128, 2048], BF), "ces": (S_, [128, 512], I32),
-    "v0s": (S_, [128, 16], I32), "kaps": (S_, [128, 16], BF), "wus": (S_, [128, 8], BF),
+    "tab0": (S_, [128, TABW], F32), "tab1": (S_, [128, TABW], F32), "pxs": (S_, [128, 4096], BF), "ces": (S_, [128, 1024], I32),
+    "v0s": (S_, [128, 16], I32), "wk": (S_, [128, 24], BF),
     "Y": (S_, [128, 2 * YH], BF), "M": (S_, [128, 4096], BF),
-    "offn": (S_, [128, 256], U16), "nf": (S_, [128, 768], F32), "nf2": (S_, [128, 256], F32),
-    "ci": (S_, [128, 256], I32), "cj": (S_, [128, 256], I32), "ck": (S_, [128, 256], I32),
-    "bu": (S_, [128, 16], U16), "bi": (S_, [128, 16], I32), "bj": (S_, [128, 16], I32), "bs": (S_, [128, 256], I32 if SCANI else F32),
-    "bt": (S_, [128, 16], I32), "btj": (S_, [128, 16], I32), "vf": (S_, [128, 16], F32),
-    "so": (S_, [128, 512], I32 if SCANI else F32), "sc": (S_, [128, 256], F32), "ind": (S_, [128, 256], BF), "ko": (S_, [128, 256], F32),
-    "ki": (S_, [128, 32], I32), "jj": (S_, [128, 16], I32), "mj": (S_, [128, 16], I32), "mi": (S_, [128, 16], I32),
-    "mm": (S_, [128, 16], I32), "cq": (S_, [128, 16], I32), "tA": (S_, [128, 16], F32), "thr": (S_, [128, 32], F32),
-    "dn": (S_, [128, 16], F32), "qd": (S_, [128, 16], F32), "wf": (S_, [128, 16], F32),
+    "offn": (S_, [128, 256], U16), "nf": (S_, [128, 768], H),
+    "ci": (S_, [128, 256], I32), "cj": (S_, [128, 256], I32),
+    "bu": (S_, [128, 16], U16), "bj": (S_, [128, 16], I32), "bs": (S_, [128, 256], I32),
+    "bt": (S_, [128, 16], I32), "kk": (S_, [128, 32], I32), "vf": (S_, [128, 16], F32),
+    "so": (S_, [128, 512], I32), "sc": (S_, [128, 256], F32), "ind": (S_, [128, 256], BF), "ko": (S_, [128, 256], F32),
+    "jj": (S_, [128, 16], I32), "mm": (S_, [128, 16], I32), "thr": (S_, [128, 32], F32),
+    "dn": (S_, [128, 16], F32), "qd": (S_, [128, 16], F32), "wf": (S_, [128, 16], H),
     "noh": (S_, [128, 256], BF), "ex": (S_, [128, 256], BF), "go": (S_, [128, 16], U16), "gs": (S_, [128, 16], U16),
-    "nm": (S_, [128, 256], F32), "vt": (S_, [128, 160], F32),
-    "tf": (S_, [128, 256], F32), "tb": (S_, [128, 512], BF), "tn": (S_, [128, 256], F32),
-    "s1": (S_, [128, 256], F32), "s2": (S_, [128, 256], F32), "E": (S_, [128, 256 * NSH], BF),
-    "ku": (S_, [128, 16], U16), "wo": (S_, [128, 16], U16),
-    "xe": (S_, [128, 256], BF), "r2": (S_, [128, 256], F32), "bc": (S_, [128, 256], BF), "tt": (S_, [128, 512], F32),
-    "val": (S_, [128, 256], I32), "ey": (S_, [128, 256], BF), "z1": (S_, [128, 256], BF), "lz": (S_, [128, 256], BF),
-    "zm": (S_, [128, 256], F32), "at": (S_, [128, 128], F32),
+    "nm": (S_, [128, 256], H), "vt": (S_, [128, 4 * RO * VT], H),
+    "tf": (S_, [128, 512], H),
+    "s1": (S_, [128, 256], F32), "s2": (S_, [128, 512], F32), "E": (S_, [128, 256 * NSH], BF),
+    "ku": (S_, [128, 16], U16), "wo": (S_, [128, 32], U16),
+    "xe": (S_, [128, 256], BF), "r2": (S_, [128, 256], H), "bc": (S_, [128, 256], BF), "tt": (S_, [128, 512], H),
+    "val": (S_, [128, 512], F32), "ey": (S_, [128, 256], BF), "z1": (S_, [128, 256], BF), "lz": (S_, [128, 256], BF),
+    "zm": (S_, [128, 256], F32), "at": (S_, [128, 256], F32),
     "sx": (S_, [128, 256 * RO], BF), "lx": (S_, [128, 256 * RO], BF),
     "sz": (S_, [128, 256 * (RO + 1)], BF), "lzz": (S_, [128, 256 * RO], BF),
-    "sna": (S_, [128, 32 * (RO + 1)], F32), "lna": (S_, [128, 32 * RO], F32),
+    "sna": (S_, [128, 32 * (RO + 1)], H),
     "sf": (S_, [128, 256 * RO], BF), "lf": (S_, [128, 256 * RO], BF),
-    "sme": (S_, [128, 32 * RO], F32), "lme": (S_, [128, 32 * RO], F32),
     "sw": (S_, [128, 256 * RO], BF), "lw": (S_, [128, 256 * RO], BF),
     "pi": (S_, [128, 8], I32), "pj": (S_, [128, 8], I32), "col": (S_, [128, 32], F32),
-    "k16": (S_, [128, 128], F32), "ug": (S_, [128, 128], F32), "cexp": (S_, [128, 8], U16),
-    "wm": (S_, [128, 144], F32), "cown": (S_, [128, 128], F32), "cmin": (S_, [128, 128], F32), "c01": (S_, [128, 128], F32),
-    "rows": (S_, [128, 784], BF), "one": (S_, [128, 128], BF), "quart": (S_, [128, 128], BF), "dum": (S_, [128, 8], F32),
-    "bo": (S_, [128, 128], F32), "idf": (S_, [128, 128], F32), "idm2": (S_, [128, 128], F32),
-    "idb": (S_, [128, 640], BF), "bf8": (S_, [128, 8], F32), "bb": (S_, [128, 96], BF),
-    "bx": (S_, [128, 512], BF), "bo4": (S_, [128, 128], BF), "bwu": (S_, [128, 128], BF), "bw8": (S_, [128, 8], BF),
-    "bkap": (S_, [128, 128], BF), "selk": (S_, [128, 256], F32), "selb": (S_, [128, 384], BF),
-    "SA": (P_, [128, 512], F32), "SB": (P_, [128, 512], F32), "xt": (S_, [128, 256], BF),
-    "XA": (P_, [128, 1024], BF) if XBF else (P_, [128, 512], F32), "XB": (P_, [128, 1024], BF) if XBF else (P_, [128, 512], F32),
-    "R1": (P_, [128, 512], F32), "R2": (P_, [128, 512], F32), "R3": (P_, [128, 512], F32), "R4": (P_, [128, 512], F32),
+    "k16": (S_, [128, 128], F32), "ug": (S_, [128, 128], F32), "u4": (S_, [128, 128], F32), "cexp": (S_, [128, 8], U16),
+    "wm": (S_, [128, 128], F32), "cown": (S_, [128, 256], F32), "cmin": (S_, [128, 256], F32), "c01": (S_, [128, 128], F32),
+    "rows": (S_, [128, 1296], BF), "nhi": (S_, [128, 256], BF), "one": (S_, [128, 128], BF), "dum": (S_, [128, 16], F32), "nob": (S_, [128, 256], BF),
+    "bo": (S_, [128, 128], F32), "idf": (S_, [128, 128], H), "idm2": (S_, [128, 128], H), "bh8": (S_, [128, 8], H),
+    "idb": (S_, [128, 768], BF), "bf8": (S_, [128, 8], F32), "bb": (S_, [128, 96], BF),
+    "bx": (S_, [128, 384], BF), "bo4": (S_, [128, 256], BF), "bwu": (S_, [128, 256], BF), "bw8": (S_, [128, 16], BF),
+    "bkap": (S_, [128, 256], BF), "kps": (S_, [128, 48], F32), "selk": (S_, [128, 512], H), "selb": (S_, [128, 384], H),
+    "sef": (S_, [128, 256], H), "seh": (S_, [128, 256], BF), "w4": (S_, [128, 256], F32),
 }
-MSG = ["xa", "xb", "z", "na", "fa", "fb", "ma", "mb", "wa", "wb"]
-NDMA = 16
+for _h in range(2):
+    for _n in ("X", "SC", "RA", "RB"):
+        SCRATCH["%s%d" % (_n, _h)] = (P_, [128, 512], F32)
+MSG = ["x", "z", "n", "f", "m", "w"]
+NDMA = 48
 SEMAPHORES = (["qv", "qs", "qp", "qg", "sent"] + ["d%d" % i for i in range(NDMA)]
-              + ["%s%d" % (m, t) for m in MSG for t in range(RO)])
+              + ["%s%d%d" % (m, h, t) for m in MSG for h in range(2) for t in range(RO)])
 A = AluOpType
 AF = ActivationFunctionType
 QS = ["v", "s", "p", "g", "y"]
 MOVES = ("load", "store", "send", "land")
 
 
-def r(name, a, b, step=1, p=128):
-    return (name, a, b, step, p)
+def r(name, a, b, step=1, p=128, p0=0):
+    return (name, a, b, step, p, p0)
 
 
 def ind(win, off):
@@ -81,6 +84,7 @@ def ind(win, off):
 
 def plan():
     ops = []
+    cur = [None]
 
     def acc(x):
         if x is None or isinstance(x, (int, float)):
@@ -91,7 +95,7 @@ def plan():
         rd, wr = ([o[2]], [o[1]]) if o[0] == "*" else ([], [o])
         for x in ins:
             rd = rd + acc(x)
-        ops.append([q, kind, args, rd, wr])
+        ops.append([q, kind, args, rd, wr, cur[0]])
 
     def cp(o, i): add("v", "cp", o, [i], (o, i))
     def tt(o, a, b, op): add("v", "tt", o, [a, b], (o, a, b, op))
@@ -99,326 +103,327 @@ def plan():
     def scan(o, d0, d1, init, op0, op1): add("v", "scan", o, [d0, d1], (o, d0, d1, init, op0, op1))
     def mset(o, c): add("v", "mset", o, [], (o, c))
     def act(o, i, f, bias=0.0, scale=1.0): add("s", "act", o, [i], (o, i, f, bias, scale))
-    def mm(o, l, rh, st, sp): add("p", "mm", o, [l, rh], (o, l, rh, st, sp))
+    def mm(o, l, rh, st, sp):
+        if SPLIT and l[0] in ("Y", "M"):
+            m = l[1] + 64 * l[3]
+            l0 = r(l[0], l[1], m, l[3]); l1 = r(l[0], m, l[2], l[3])
+            o0 = o[:4] + (64, 0); o1 = o[:4] + (128, 64)
+            add("p", "mm", o0, [l0, rh], (o0, l0, rh, st, sp)); add("p", "mm", o1, [l1, rh], (o1, l1, rh, st, sp))
+        else:
+            add("p", "mm", o, [l, rh], (o, l, rh, st, sp))
     def iota(o, pat, base, cm): add("g", "iota", o, [], (o, pat, base, cm))
-    def load(q, o, src): ops.append([q, "load", (o, src), [], [o]])
-    def store(q, dst, i): ops.append([q, "store", (dst, i), [i], []])
+    def load(q, o, src): ops.append([q, "load", (o, src), [], [o], cur[0]])
+    def store(q, dst, i): ops.append([q, "store", (dst, i), [i], [], cur[0]])
 
     def send(name, step, dst, src):
-        ops.append(["g", "send", (name, step, dst, src), [src], []])
-        ops.append([None, "land", (name, step, dst), [], [dst]])
+        ops.append(["g", "send", (name, step, dst, src), [src], [], cur[0]])
+        ops.append([None, "land", (name, step, dst), [], [dst], cur[0]])
 
     def hf(name, h, base=0): return r(name, base + 128 * h, base + 128 * h + 128)
     def sm(name, h, base=0): return r(name, base + 8 * h, base + 8 * h + 8)
     def ends(name, h, base=0): return r(name, base + 128 * h + 15, base + 128 * h + 128, 16)
     def c(i): return r("col", i, i + 1)
-    SC = ["SA", "SB"]; XP = ["XA", "XB"]
-    IDB, IDN, ID4, IDH, IDNH = [r("idb", 128 * i, 128 * i + 128) for i in range(5)]
-    IDF = r("idf", 0, 128); K16 = r("k16", 0, 128); UG = r("ug", 0, 128); WM = r("wm", 0, 128); BO = r("bo", 0, 128)
-    WC, GC, P7, P3, W16P, BIGC = c(0), c(1), c(2), c(3), c(4), c(5)
-    COWN = r("cown", 0, 128); CMIN = r("cmin", 0, 128); CEXP = r("cexp", 0, 8)
-    def selb(i): return r("selb", 128 * i, 128 * i + 128, 1, 40)
+    def ps(name, h, a, b, step=1, p=128): return r("%s%d" % (name, h), a, b, step, p)
+    IDB, IDN, ID4, IDH, IDNH, IDG = [r("idb", 128 * i, 128 * i + 128) for i in range(6)]
+    IDF = r("idf", 0, 128); K16 = r("k16", 0, 128); UG = r("ug", 0, 128); U4 = r("u4", 0, 128); WM = r("wm", 0, 128); BO = r("bo", 0, 128)
+    WC, GC, P7, P3, W16P, G3, R6 = c(0), c(1), c(2), c(3), c(8), c(4), c(5)
+    COWN = r("cown", 0, 128); CMIN = r("cmin", 0, 128); CMAX = r("cmin", 128, 256); CEXP = r("cexp", 0, 8); NOB = r("nob", 0, 128)
+    def selb(i): return r("selb", 128 * i, 128 * i + 128, 1, 8)
     def row(a, b): return r("rows", a, b, 1, 1)
-    ONE = r("one", 0, 128, 1, 1); QUART = r("quart", 0, 128, 1, 1)
-    PLAS = r("tab", 0, 2048); CELL = r("tab", 2048, 2560); TAB = r("tab", 0, TABW)
+    ONE = r("one", 0, 128, 1, 1); QUART = row(384, 640)
+    def PLAS(h): return r("tab%d" % h, 0, 2048)
+    def CELL(h): return r("tab%d" % h, 2048, 2560)
+    def TAB(h): return r("tab%d" % h, 0, TABW)
     def YW(h): return r("Y", YH * h, YH * h + YH)
-    def ycol(l): return YH * (l // 128) + 16 + 16 * (l % 128)
+    def vt(t, step, h, a, b): o = VT * (4 * t + 2 * (step - 2) + h); return r("vt", o + a, o + b)
 
-    load("y", r("v0s", 0, 16), ("v0", None)); load("s", r("ces", 0, 512), ("ce", None))
-    load("y", r("pxs", 0, 1024), ("px", (0, 1024))); load("s", r("pxs", 1024, 2048), ("px", (1024, 2048)))
-    load("y", r("sz", 0, 256), ("z0", None))
-    load("y", r("wus", 0, 1), ("wu", None)); load("y", r("kaps", 0, 16), ("kap", None))
+    for h in range(2):
+        cur[0] = h
+        for q in range(2):
+            def part(name, a, b): return r(name, a, b, 1, 64 * q + 64, 64 * q)
+            load("y", part("v0s", 8 * h, 8 * h + 8), ("v0", 64 * h, 64 * h + 64, 8 * q, 8 * q + 8))
+            load("y", part("ces", 512 * h, 512 * h + 512), ("ce", 64 * h, 64 * h + 64, 0, 512))
+            load("s" if h == 0 else "y", part("pxs", 2048 * h, 2048 * h + 2048), ("px", 64 * h, 64 * h + 64, 0, 2048))
+            load("y", part("sz", 128 * h, 128 * h + 128), ("z0", 64 * h, 64 * h + 64, 128 * q, 128 * q + 128))
+    cur[0] = None
+    load("y", r("wk", 16, 17), ("wu", 0, 128, 0, 1)); load("y", r("wk", 0, 16), ("kap", 0, 128, 0, 16))
     iota(r("pi", 0, 1), [[0, 1]], 0, 1)
     iota(K16, [[0, 8], [1, 16]], 0, 0)
     iota(UG, [[1, 8], [0, 16]], 0, 0)
     iota(row(128, 256), [[0, 8], [1, 16]], -16, 0)
     iota(row(768, 776), [[256, 8]], 0, 0)
-    send("z0", 1, r("lzz", 0, 256), r("sz", 0, 256))
-    if LOADC:
-        for j in range(4): act(r("tab", 512 * j, 512 * j + 512), r("pxs", 512 * j, 512 * j + 512), AF.Copy)
-    else:
-        load("g", PLAS, ("px", None))
+    for h in range(2):
+        cur[0] = h
+        send("z%d0" % h, 1, hf("lzz", h), hf("sz", h))
+        for j in range(4): act(r("tab%d" % h, 512 * j, 512 * j + 512), r("pxs", 2048 * h + 512 * j, 2048 * h + 512 * j + 512), AF.Copy)
+        cp(sm("bu", h), sm("v0s", h))
+        cp(CELL(h), r("ces", 512 * h, 512 * h + 512))
+        mset(r("tab%d" % h, 2560, TABW), 0.0)
+    cur[0] = None
     iota(row(0, 128), [[0, 8], [4096, 16]], 0, 0)
-    iota(row(256, 384), [[0, 8], [512, 16]], 0, 0)
-    iota(row(384, 512), [[0, 8], [2048, 16]], 0, 0)
-    mset(r("rows", 512, 640), -2040.0 * 8192); mset(r("rows", 640, 768), -300.0 * 32768)
-    mset(r("one", 0, 128), 1.0); mset(r("Y", 0, 16), 0.0); mset(r("Y", YH, YH + 16), 0.0); mset(r("sna", 16, 32), 0.0)
+    iota(U4, [[0, 2], [1, 4], [0, 16]], 0, 0)
+    mset(r("one", 0, 128), 1.0); mset(r("Y", 0, 16), 0.0); mset(r("Y", YH, YH + 16), 0.0)
+    ts(r("sna", 0, 32), r("k16", 0, 32), 0.0, A.mult); mset(r("rows", 384, 640), -0.25); mset(r("rows", 256, 384), -1024.0)
     ts(r("pj", 0, 1), r("pi", 0, 1), 15, A.bitwise_and); ts(r("pj", 1, 2), r("pi", 0, 1), 4, A.logical_shift_right)
     ts(r("pj", 2, 3), r("pi", 0, 1), 7, A.bitwise_and); ts(r("pj", 3, 4), r("pi", 0, 1), 3, A.logical_shift_right)
-    cp(r("col", 0, 4), r("pj", 0, 4))
+    ts(r("pj", 4, 5), r("pi", 0, 1), 4, A.logical_shift_right, 3, A.bitwise_and)
+    ts(r("pj", 5, 6), r("pi", 0, 1), 6, A.logical_shift_right)
+    cp(r("col", 0, 6), r("pj", 0, 6))
     ts(W16P, WC, 16.0, A.mult, 16.0, A.add)
     ts(BO, UG, GC, A.is_equal)
     ts(WM, K16, WC, A.is_equal)
     tt(IDB, BO, WM, A.mult)
     ts(r("bf8", 0, 8), r("k16", 0, 8), GC, A.is_equal)
     ts(r("bb", 0, 8), r("bf8", 0, 8), -16.0, A.mult)
-    cp(r("bb", 8, 16), r("bf8", 0, 8))
-    cp(r("bu", 0, 16), r("v0s", 0, 16))
+    cp(r("bb", 8, 16), r("bf8", 0, 8)); cp(r("bh8", 0, 8), r("bf8", 0, 8))
     cp(CEXP, r("k16", 0, 8))
     ts(CMIN, K16, 0.0, A.is_equal, float(1 << 30), A.mult)
-    cp(CELL, r("ces", 0, 512))
-    cp(c(6), r("wus", 0, 1))
-    ts(r("bwu", 0, 128), BO, c(6), A.mult)
-    ts(r("bw8", 0, 8), r("bf8", 0, 8), c(6), A.mult)
-    cp(r("wm", 128, 144), r("wm", 0, 16))
-    ts(r("s1", 0, 128), r("wm", 15, 143), BIG, A.mult)
-    ts(r("s2", 0, 128), WM, -2 * BIG, A.mult)
-    tt(COWN, r("s1", 0, 128), r("s2", 0, 128), A.add)
+    act(COWN, WM, AF.Identity, 0.0, -2 * BIG)
+    act(NOB, WM, AF.Identity, -BIG, BIG)
+    act(r("bo4", 0, 128), BO, AF.Identity, 0.0, 4096.0)
     ts(r("c01", 0, 128), K16, 0.0, A.not_equal)
     act(IDF, IDB, AF.Copy)
-    mset(r("bb", 24, 32), 0.0); mset(r("bx", 128, 256), 0.0)
     ts(r("bb", 16, 24), r("bf8", 0, 8), 65536.0, A.mult)
-    ts(r("bb", 32, 40), r("bf8", 0, 8), -131072.0, A.mult); cp(r("bb", 40, 48), r("bb", 0, 8))
-    act(r("bx", 0, 128), BO, AF.Identity, 0.0, 65536.0)
-    ts(BIGC, WC, 15.0, A.not_equal, BIG, A.mult)
-    ts(c(7), WC, 2560.0, A.add); tt(c(8), c(7), BIGC, A.add)
-    for j in range(8 // NC):
-        ts(r("dum", NC * j, NC * j + NC), r("k16", 0, NC), 16.0, A.mult, c(8), A.add)
-    ts(c(16), P3, 1.0, A.is_equal)
-    ts(c(17), P3, 1.0, A.is_equal, 2047.0, A.mult); ts(c(18), P3, 3.0, A.is_equal, 4095.0, A.mult)
-    ts(c(24), P3, 4.0, A.not_equal); ts(c(25), P3, 4.0, A.is_equal, BIG, A.mult)
-    tt(c(19), c(17), c(18), A.add); tt(c(20), c(19), c(24), A.add); tt(c(26), c(20), c(25), A.add)
-    ts(r("selk", 0, 128), UG, P7, A.is_equal, c(20), A.mult)
-    ts(r("selk", 128, 256), UG, P7, A.is_equal, c(26), A.mult)
-    for i, w in enumerate((-256.0, 4096.0, 0.5)):
-        ts(c(21 + i), c(16), w, A.mult)
-        ts(r("selb", 128 * i, 128 * i + 128), UG, P7, A.is_equal, c(21 + i), A.mult)
-    for ap, w in ((IDN, -1.0), (ID4, -4096.0), (IDH, 0.5), (IDNH, -0.5), (r("idm2", 0, 128), -2.0)):
-        act(ap, IDB, AF.Identity, 0.0, w)
-    act(r("bo4", 0, 128), BO, AF.Identity, 0.0, 4096.0)
-    mset(r("quart", 0, 128), -0.25); mset(r("tab", 2560, TABW), 0.0)
-    for j in range(4):
-        mset(r("vt", 40 * j + 32, 40 * j + 40), 1.0)
-        if j < 2: mset(r("vt", 40 * j + 24, 40 * j + 32), 0.0)
+    ts(r("bb", 32, 40), r("bf8", 0, 8), -131072.0, A.mult)
     for i, w in enumerate((8192.0, 32768.0, -16384.0, -65536.0)):
-        ts(r("bb", 48 + 8 * i, 56 + 8 * i), r("bf8", 0, 8), w, A.mult)
-    act(r("bx", 256, 384), BO, AF.Identity, 0.0, 8192.0); act(r("bx", 384, 512), BO, AF.Identity, 0.0, 32768.0)
-    for g8 in range(8):
-        tt(r("bkap", 16 * g8, 16 * g8 + 16), r("kaps", 0, 16), r("bo", 16 * g8, 16 * g8 + 16), A.mult)
+        act(r("bb", 48 + 8 * i, 56 + 8 * i), r("bf8", 0, 8), AF.Identity, 0.0, w)
+    for i, w in enumerate((65536.0, 8192.0, 32768.0)):
+        act(hf("bx", i), BO, AF.Identity, 0.0, w)
+    iota(row(784, 912), [[0, 8], [512, 16]], 0, 0); iota(row(912, 1040), [[0, 8], [2048, 16]], 0, 0)
+    mset(r("rows", 1040, 1168), -2032.0 * 8192); mset(r("rows", 1168, 1296), -300.0 * 32768)
+    for q in range(2):
+        ts(c(9 + q), R6, float(q), A.is_equal)
+        ts(hf("w4", q), U4, G3, A.is_equal, c(9 + q), A.mult)
+        tt(hf("sef", q), hf("w4", q), WM, A.mult)
+        act(hf("seh", q), hf("sef", q), AF.Identity, 0.0, 0.5)
+    for h in range(2):
+        cur[0] = h
+        mm(ps("RB", h, 0, 17), hf("seh", h), r("wk", 0, 17), True, True)
+        act(r("kps", 24 * h, 24 * h + 17), ps("RB", h, 0, 17), AF.Identity, 0.0, 2.0)
+        wu = r("kps", 24 * h + 16, 24 * h + 17)
+        ts(hf("bwu", h), BO, wu, A.mult)
+        ts(sm("bw8", h), r("bf8", 0, 8), wu, A.mult)
+        for g8 in range(8):
+            add("s", "act", r("bkap", 128 * h + 16 * g8, 128 * h + 16 * g8 + 16), [r("kps", 24 * h, 24 * h + 16), r("bf8", g8, g8 + 1)],
+                (r("bkap", 128 * h + 16 * g8, 128 * h + 16 * g8 + 16), r("kps", 24 * h, 24 * h + 16), AF.Identity, 0.0, r("bf8", g8, g8 + 1)))
+    cur[0] = None
+    ts(c(11), WC, 2560.0 - 1024.0, A.add)
+    for j in range(8 // NC):
+        ts(r("dum", NC * j, NC * j + NC), r("k16", 0, NC), 16.0, A.mult, c(11), A.add)
+    ts(c(16), P3, 0.0, A.is_equal); ts(c(17), P3, 3.0, A.is_equal)
+    ts(c(18), P3, 0.0, A.is_equal, 2047.0, A.mult); ts(c(19), P3, 4.0, A.is_equal, 4095.0, A.mult)
+    tt(c(20), c(18), c(19), A.add); tt(c(24), c(20), c(17), A.subtract); ts(c(25), c(24), 1.0, A.add)
+    ts(r("selk", 0, 128), UG, P7, A.is_equal, c(25), A.mult)
+    ts(c(21), c(16), 4096.0, A.mult, c(17), A.add)
+    ts(r("selk", 128, 256), UG, P7, A.is_equal, c(21), A.mult)
+    for i, w in enumerate((-256.0, 4096.0, 0.5)):
+        ts(r("selb", 128 * i, 128 * i + 128), UG, P7, A.is_equal, w, A.mult)
+    for ap, w in ((IDN, -1.0), (ID4, -4096.0), (IDH, 0.5), (IDNH, -0.5), (IDG, -BIG), (r("idm2", 0, 128), -2.0)):
+        act(ap, IDB, AF.Identity, 0.0, w)
 
     def to_psum(h, x):
-        if XBF:
-            add("p", "tr", r(XP[h], 128, 256), [x, IDB], (r(XP[h], 128, 256), x, IDB))
-            act(hf("xt", h), r(XP[h], 128, 256), AF.Copy)
-            add("p", "tr", r(XP[h], 0, 128), [hf("xt", h), IDB], (r(XP[h], 0, 128), hf("xt", h), IDB))
-        else:
-            mm(r(XP[h], 0, 128), IDB, x, True, True)
-
-    for h in range(2):
-        to_psum(h, hf("sz", h))
+        mm(ps("X", h, 0, 128), IDB, x, True, True)
 
     def scores(step, h, win, x):
-        nf = hf("nf", h, 256 * (step - 1))
-        if step == 1:
-            mm(r(SC[h], 0, 128), ONE, row(128, 256), True, False)
+        nf = hf("nf", h, 256 * (step - 1)); y0 = YH * h + 16
+        if step == 2:
+            mm(ps("SC", h, 0, 128), ONE, row(0, 128), True, False)
+            mm(ps("SC", h, 0, 128), x, r("bx", 0, 128), False, False)
+            mm(ps("RB", h, 128, 256), ONE, row(128, 256), True, False)
+        elif step == 1:
+            mm(ps("SC", h, 0, 128), ONE, row(128, 256), True, False)
         else:
-            o = 256 * (step - 2)
-            mm(r(SC[h], 0, 256), ONE, row(o, o + 256), True, False)
-            if step == 3: mm(r(SC[h], 0, 256), ONE, row(512, 768), False, False)
-            mm(r(SC[h], 0, 256), x, r("bx", o, o + 256), False, False)
+            mm(ps("SC", h, 0, 256), ONE, row(784, 1040), True, False); mm(ps("SC", h, 0, 256), ONE, row(1040, 1296), False, False)
+            mm(ps("SC", h, 0, 256), x, r("bx", 128, 384), False, False)
+            mm(ps("SC", h, 0, 128), hf("nhi", h), IDN, False, False)
+        w = 256 if step == 3 else 128
         for q, a, b in GATHER[step]:
-            a, b = a ^ (128 * HS[0]), (a ^ (128 * HS[0])) + b - a
-            if a // 128 == h:
-                o = r("Y", ycol(a), ycol(a) + 16 * (b - a)); i = ind(win, r("offn", a, b))
-                if q == "v": cp(o, i)
-                else: act(o, i, AF.Copy)
+            o = r("Y", y0 + 16 * a, y0 + 16 * b); i = ind(win, r("offn", 128 * h + a, 128 * h + b))
+            if q == "v": cp(o, i)
+            else: act(o, i, AF.Copy)
         if step > 1:
             for k in range(16):
-                mm(r(SC[h], k, 256, 16), r("Y", YH * h + 16 + k, YH * h + YH, 16), r("bb", 16, 32) if step == 2 else r("bb", 48, 64), False, False)
+                mm(ps("SC", h, k, w, 16), r("Y", y0 + k, y0 + 2048, 16), r("bb", 16, 24) if step == 2 else r("bb", 48, 64), False, False)
         for a, b in MINS[step]:
-            if a // 128 == h:
-                for k in range(16):
-                    tt(r("M", 256 * k + a, 256 * k + b), r("Y", ycol(a) + k, ycol(a) + 16 * (b - a), 16), r(XP[h], a - 128 * h, b - 128 * h), A.min)
+            for k in range(16):
+                m0 = 2048 * h + 128 * k
+                tt(r("M", m0 + a, m0 + b), r("Y", y0 + 16 * a + k, y0 + 16 * b, 16), ps("X", h, a, b), A.min)
         for k in range(16):
-            lm = hf("M", h, 256 * k)
-            if step == 1: mm(r(SC[h], k, 128, 16), lm, r("bb", 0, 8), False, k == 15)
-            else: mm(r(SC[h], k, 256, 16), lm, r("bb", 32, 48) if step == 2 else r("bb", 64, 80), False, False)
-        if step == 2:
-            mm(r(SC[h], 0, 128), nf, IDF, False, True)
+            mm(ps("SC", h, k, w, 16), r("M", 2048 * h + 128 * k, 2048 * h + 128 * k + 128),
+               (r("bb", 0, 8), r("bb", 32, 40), r("bb", 64, 80))[step - 1], False, k == 15 and step == 1)
         if step == 3:
-            mm(r(SC[h], 0, 128), hf("nf2", h), IDF, False, False)
-            mm(r(SC[h], 128, 256), nf, IDF, False, True)
+            mm(ps("SC", h, 0, 128), nf, IDF, False, False); mm(ps("SC", h, 128, 256), nf, IDF, False, True)
+        if step == 2:
+            mm(ps("SC", h, 0, 128), nf, IDF, False, True)
+            for k in range(16):
+                mm(ps("RB", h, 128 + k, 256, 16), r("M", 2048 * h + 128 * k, 2048 * h + 128 * k + 128), r("bb", 0, 8), False, False)
 
-    def whole(name, h, base, tmp):
-        if SCANI: return ends(name, h, base)
-        cp(tmp, ends(name, h, base))
-        return tmp
-
-    def names(step, h, win=CELL):
-        cp(hf("offn", h), ind(win, sm("bu", h)))
-        act(hf("nf", h, 256 * (step - 1)), ind(CELL, sm("bu", h)), AF.Copy)
+    def names(step, h, win):
+        act(hf("nf", h, 256 * (step - 1)), ind(win, sm("bu", h)), AF.Copy)
+        cp(hf("offn", h), hf("nf", h, 256 * (step - 1)) if OFFS else ind(win, sm("bu", h)))
 
     def to_list(src, h, slots):
         tt(hf("ex", h), ind(sm(src, h), CEXP), WM, A.mult)
-        mm(sm("R1", h), ONE, row(768, 776), True, False)
-        mm(sm("R1", h), hf("ex", h), r("bb", 8, 16), False, True)
-        if slots: mm(sm("R1", h, 16), hf("ex", h), r("bb", 8, 16), True, True)
-        ts(sm("go", h), sm("R1", h), W16P, A.add)
-        if slots: cp(sm("gs", h), sm("R1", h, 16))
+        mm(ps("RB", h, 0, 8), ONE, row(768, 776), True, False)
+        mm(ps("RB", h, 0, 8), hf("ex", h), r("bb", 8, 16), False, True)
+        if slots: mm(ps("RB", h, 8, 16), hf("ex", h), r("bb", 8, 16), True, True)
+        ts(sm("go", h), ps("RB", h, 0, 8), W16P, A.add)
+        if slots: cp(sm("gs", h), ps("RB", h, 8, 16))
 
     def pick_name(step, h, dst):
         tt(hf("nm", h), ind(r("wm", 0, 16), sm("gs", h)), hf("nf", h, 256 * (step - 1)), A.mult)
-        mm(sm("R1", h, 32), hf("nm", h), r("bf8", 0, 8), True, True)
-        act(dst, sm("R1", h, 32), AF.Copy)
+        mm(ps("RB", h, 16, 24), hf("nm", h), r("bh8", 0, 8), True, True)
+        act(dst, ps("RB", h, 16, 24), AF.Copy)
 
-    def name_rows(h, src):
-        mm(r("R2", 128, 256, 1, 8), src, IDF, True, True)
-        act(r("tn", 128 * h, 128 * h + 128, 1, 8), r("R2", 128, 256, 1, 8), AF.Copy)
-
-    def write_prep(step, h, x):
-        j = 2 * (step - 2) + h
-        mm(r("R2", 0, 128, 1, 40), r("vt", 40 * j, 40 * j + 40), IDF, True, True)
-        TF = r("tf", 128 * h, 128 * h + 128, 1, 40); TB = r("tb", 128 * j, 128 * j + 128, 1, 40)
-        act(TF, r("R2", 0, 128, 1, 40), AF.Copy)
-        act(TB, r("R2", 0, 128, 1, 40), AF.Copy)
-        KR = r("R1", 256, 384) if XBF else r(XP[h], 0, 128); P = r(SC[h], 0, 128)
-        mm(KR, r("selk", 0, 128, 1, 40), TF, True, True)
-        mm(r("R3", 0, 128), r("selk", 128, 256, 1, 40), TF, True, True)
-        mm(P, r("selk", 0, 128, 1, 40), TF, True, False)
-        scan(hf("s1", h), COWN, KR, -1.0, A.add, A.max)
-        for i in range(NSH):
-            s = 15 * i; e = 256 * i + 128 * h
-            tt(r("E", e + s, e + 128), r("s1", 128 * h, 128 * h + 128 - s), r("R3", s, 128), A.is_equal)
-            mm(r(SC[h], s, 128), r("bo4", 0, 128), r("E", e + s, e + 128), False, i == NSH - 1)
-        o = r("R4", 0, 128)
+    def write(t, step, h, x, between=None):
+        K = 32 if step == 2 else 40; j = 2 * (step - 2) + h
+        mm(ps("RA", h, 0, 128, 1, K), vt(t, step, h, 16, 16 + K), IDF, True, True)
+        TF = r("tf", 128 * j, 128 * j + 128, 1, K); TB = r("tf", 128 * j, 128 * j + 128, 1, 8)
+        act(TF, ps("RA", h, 0, 128, 1, K), AF.Copy)
+        def sel(i): return r("selk", 128 * i, 128 * i + 128, 1, K)
+        KM = ps("X", h, 0, 128)
+        mm(KM, IDB, NOB, True, False); mm(KM, sel(0), TF, False, True)
+        mm(ps("RA", h, 128, 256), sel(0), TF, True, True)
+        scan(hf("s1", h), COWN, KM, -1.0, A.add, A.max)
+        o = ps("RB", h, 128, 256)
         mm(o, hf("noh", h), IDB, True, False); mm(o, selb(2), TB, False, True)
-        o = r("R4", 128, 256)
+        o = ps("RB", h, 256, 384)
         mm(o, IDB, x, True, False); mm(o, selb(0), TB, False, True)
-        o = r("R4", 256, 384)
-        mm(o, r("selk", 0, 128, 1, 8), r("tn", 128 * h, 128 * h + 128, 1, 8), True, False)
-        mm(o, hf("noh", h), ID4, False, False); mm(o, selb(1), TB, False, True)
-        act(hf("xe", h), r("R4", 128, 256), AF.Relu)
-        act(hf("r2", h), r("R4", 256, 384), AF.Relu, -4096.0)
-        act(hf("bc", h), r("R4", 0, 128), AF.Abs, -0.5)
-        o = r("R4", 384, 512)
-        mm(o, ONE, QUART, True, False); mm(o, IDH, hf("xe", h), False, False); mm(o, IDF, hf("r2", h), False, True)
+        o = ps("RB", h, 384, 512)
+        mm(o, hf("noh", h), ID4, True, False); mm(o, sel(1), TF, False, True)
+        act(hf("bc", h), ps("RB", h, 128, 256), AF.Abs, -0.5)
+        act(hf("xe", h), ps("RB", h, 256, 384), AF.Relu)
+        act(hf("r2", h), ps("RB", h, 384, 512), AF.Relu, -4096.0)
+        if between: between()
+        mm(ps("SC", h, 256, 384), IDB, NOB, True, False); mm(ps("SC", h, 256, 384), ONE, row(256, 384), False, False)
+        mm(ps("SC", h, 256, 384), sel(0), TF, False, False)
         T_ = hf("tt", h, 256 * (step - 2))
-        ts(sm("ku", h), ends("s1", h), BIGC, A.subtract, 2560.0, A.min)
-        tt(T_, ind(TAB, sm("ku", h)), hf("bc", h), A.mult)
-        tt(hf("val", h), T_, o, A.add)
-        scan(hf("s2", h), COWN, P, 0.0, A.add, A.max)
+        ts(sm("ku", h), ends("s1", h), 2560.0, A.min)
+        tt(T_, ind(TAB(h), sm("ku", h)), hf("bc", h), A.mult)
+        for i in range(NSH):
+            s = 1 + 16 * i; e = 256 * i + 128 * h
+            tt(r("E", e + s, e + 128), r("s1", 128 * h, 128 * h + 128 - s), ps("RA", h, 128 + s, 256), A.is_equal)
+            mm(ps("SC", h, 256 + s, 384), r("bo4", 0, 128), r("E", e + s, e + 128), False, i == NSH - 1)
+        mm(ps("X", h, 256, 512), ONE, QUART, True, False)
+        for q in range(2):
+            o = ps("X", h, 256 + 128 * q, 384 + 128 * q)
+            mm(o, hf("seh", q), hf("xe", h), False, False); mm(o, hf("sef", q), hf("r2", h), False, False)
+        for q in (1, 0): mm(ps("X", h, 256 + 128 * q, 384 + 128 * q), hf("sef", q), T_, False, q == 0)
+        for q in (1, 0): act(hf("val", q, 256 * h), ps("X", h, 256 + 128 * q, 384 + 128 * q), AF.Identity, MAGIC)
+        scan(hf("s2", h), COWN, ps("SC", h, 256, 384), -2048.0, A.add, A.max)
         tt(sm("wf", h), ends("s2", h), r("dum", 0, 8), A.min)
-        ts(sm("wo", h), sm("wf", h), BIGC, A.subtract)
-
-    def scatter():
+        for q in range(2): mm(ps("SC", h, 384 + 8 * q, 392 + 8 * q), hf("sef", q), sm("wf", h), True, True)
+        ts(r("wo", 16 * h, 16 * h + 16), ps("SC", h, 384, 400), 1024.0, A.add)
         for b in range(256 // BLK - 1, -1, -1):
-            cp(ind(TAB, r("wo", NC * b, NC * b + NC)), r("val", BLK * b, BLK * b + BLK))
+            ts(ind(TAB(h), r("wo", 16 * h + NC * b, 16 * h + NC * b + NC)), r("val", 256 * h + BLK * b, 256 * h + BLK * b + BLK),
+               1.0, A.mult, -MAGIC, A.add)
 
-    for t in range(RO):
-        o = 256 * t
-        for h in HS: names(1, h, r("ces", 0, 512) if t == 0 else CELL)
-        for h in HS:
-            scores(1, h, r("pxs", 0, 2048) if t == 0 else PLAS, None)
-            scan(hf("so", h), CMIN, r(SC[h], 0, 128), 0.0, A.add, A.min)
-            ts(sm("jj", h), whole("so", h, 0, sm("ki", h)), 15, A.bitwise_and)
+    def stream(h):
+        to_psum(h, hf("sz", h))
+        for t in range(RO):
+            o = 256 * t; na = 32 * t + 16 * h
+            names(1, h, r("ces", 512 * h, 512 * h + 512) if t == 0 else CELL(h))
+            scores(1, h, r("pxs", 2048 * h, 2048 * h + 2048) if t == 0 else PLAS(h), None)
+            scan(hf("so", h), CMIN, ps("SC", h, 0, 128), 0.0, A.add, A.min)
+            ts(sm("jj", h), ends("so", h), 15, A.bitwise_and)
             to_list("jj", h, True)
             act(hf("sx", h, o), ind(YW(h), sm("go", h)), AF.Copy)
-            send("x%s%d" % ("ab"[h], t), 1, hf("lx", h, o), hf("sx", h, o))
-            pick_name(1, h, sm("sna", h, 32 * t))
-        send("na%d" % t, 1, r("lna", 32 * t, 32 * t + 32), r("sna", 32 * t, 32 * t + 32))
-        for h in HS:
-            x = hf("lx", h, o); bank = r(("R2", "R3")[h], 256, 384)
-            mm(bank, r("bwu", 0, 128), x, True, True)
+            send("x%d%d" % (h, t), 1, hf("lx", h, o), hf("sx", h, o))
+            pick_name(1, h, r("sna", na, na + 8))
+            send("n%d%d" % (h, t), 1, vt(t, 2, h, 40, 56), r("sna", na, na + 16))
+            x = hf("lx", h, o); bank = ps("RA", h, 256, 384)
+            mm(bank, IDB, NOB, True, False); mm(bank, hf("bwu", h), x, False, True)
             to_psum(h, x)
             scan(hf("bs", h), COWN, bank, 0.0, A.add, A.max)
-            ts(sm("bj", h), whole("bs", h, 0, sm("bi", h)), 511, A.bitwise_and)
+            ts(sm("bj", h), ends("bs", h), 511, A.bitwise_and)
             cp(sm("bu", h), sm("bj", h))
-            names(2, h)
-        ts(r("thr", 16, 32), r("lna", 32 * t + 16, 32 * t + 32), 1.0, A.is_equal, 2.0, A.mult)
-        act(r("thr", 0, 16), r("thr", 16, 32), AF.Identity, -12.0)
-        for h in HS:
-            x = hf("lx", h, o); v = 40 * h
-            mm(sm("R1", h, 48), x, r("bw8", 0, 8), True, True)
-            cp(sm("bt", h), sm("R1", h, 48)); ts(sm("btj", h), sm("bt", h), 511, A.bitwise_and)
-            name_rows(h, sm("lna", h, 32 * t))
-            scores(2, h, PLAS, x)
-            scan(hf("so", h), CMIN, r(SC[h], 0, 128), 0.0, A.add, A.min)
-            act(hf("ind", h), r(SC[h], 0, 128), AF.Sign, 255.985, -1.0 / 65536)
-            ki = whole("so", h, 0, sm("ki", h))
-            ts(sm("jj", h), ki, 12, A.arith_shift_right, 15, A.bitwise_and)
-            ts(sm("mj", h), ki, 2047, A.bitwise_and)
+            names(2, h, CELL(h))
+            act(sm("thr", h, 16), vt(t, 2, h, 48, 56), AF.Abs, -2.0, 2.0)
+            act(sm("thr", h), sm("thr", h, 16), AF.Identity, -10.0, -1.0)
+            mm(ps("RB", h, 24, 32), x, sm("bw8", h), True, True)
+            cp(sm("bt", h), ps("RB", h, 24, 32)); ts(r("kk", 16 * h + 8, 16 * h + 16), sm("bt", h), 511, A.bitwise_and)
+            scores(2, h, PLAS(h), x)
+            scan(hf("so", h), CMIN, ps("SC", h, 0, 128), 0.0, A.add, A.min)
+            act(hf("ind", h), ps("SC", h, 0, 128), AF.Sign, 255.985, -1.0 / 65536)
+            ts(sm("jj", h), ends("so", h), 12, A.arith_shift_right, 15, A.bitwise_and)
             tt(hf("noh", h), ind(sm("jj", h), CEXP), K16, A.not_equal)
+            mm(ps("RB", h, 128, 256), IDG, hf("noh", h), False, True)
+            ts(r("kk", 16 * h, 16 * h + 8), ends("so", h), 2047, A.bitwise_and)
             scan(hf("sc", h), r("c01", 0, 128), hf("ind", h), 0.0, A.mult, A.add)
-            tt(r("vt", v + 8, v + 16), ends("sc", h), sm("thr", h), A.is_lt)
-            tt(sm("tA", h), sm("btj", h), sm("mj", h), A.subtract)
-            cp(r("vt", v + 16, v + 24), sm("mj", h))
-            tt(r("vt", v, v + 8), sm("tA", h), r("vt", v + 8, v + 16), A.mult)
-            tt(hf("ko", h), hf("noh", h), r(SC[h], 128, 256), A.mult)
-            scan(hf("so", h, 256), CMIN, hf("ko", h), 0.0, A.add, A.min)
-            ts(sm("mm", h), whole("so", h, 256, sm("mi", h)), 15, A.bitwise_and)
+            tt(vt(t, 2, h, 16, 24), ends("sc", h), sm("thr", h), A.is_lt)
+            e = vt(t, 2, h, 8, 16)
+            tt(e, ends("sc", h), sm("thr", h), A.is_ge)
+            tt(vt(t, 2, h, 24, 40), r("kk", 16 * h, 16 * h + 16), vt(t, 2, h, 8, 24), A.mult)
+            scan(hf("so", h, 256), CMIN, ps("RB", h, 128, 256), 0.0, A.add, A.min)
+            ts(sm("mm", h), ends("so", h, 256), 15, A.bitwise_and)
             to_list("mm", h, True)
             tt(hf("sf", h, o), ind(YW(h), sm("go", h)), x, A.max)
-            send("f%s%d" % ("ab"[h], t), 1, hf("lf", h, o), hf("sf", h, o))
-            m = 32 * t + 16 * h; e = r("sme", m + 8, m + 16)
-            act(e, r("vt", v + 8, v + 16), AF.Identity, 1.0, -1.0)
-            pick_name(2, h, r("sme", m, m + 8))
-            send("m%s%d" % ("ab"[h], t), 1, r("lme", m, m + 16), r("sme", m, m + 16))
-            tt(sm("sna", h, 32 * t + 48), sm("lna", h, 32 * t + 16), e, A.add)
-            write_prep(2, h, x)
-        scatter()
-        if t == RO - 1:
-            cp(r("vf", 0, 16), r("bj", 0, 16)); store("y", ("yv", None), r("vf", 0, 16))
-            mm(r("R1", 128, 256, 1, 16), r("sna", 32 * RO + 16, 32 * RO + 32), IDF, True, True)
-            act(r("at", 0, 128, 1, 16), r("R1", 128, 256, 1, 16), AF.Copy)
-            for h in range(2): store("y", ("ya", h), r("at", 0, 128))
-        for h in HS:
-            f = hf("lf", h, o); bank = r(("R2", "R3")[h], 256, 384)
-            mm(bank, r("bkap", 0, 128), f, True, True)
+            send("f%d%d" % (h, t), 1, hf("lf", h, o), hf("sf", h, o))
+            tt(r("sna", na + 40, na + 48), vt(t, 2, h, 48, 56), e, A.add)
+
+            def name_m():
+                pick_name(2, h, vt(t, 2, h, 0, 8))
+                send("m%d%d" % (h, t), 1, vt(t, 3, h, 40, 56), vt(t, 2, h, 0, 16))
+            write(t, 2, h, x, name_m)
+            if t == RO - 1:
+                cp(sm("vf", h), sm("bj", h))
+                mm(ps("RB", h, 0, 128, 1, 8), r("sna", na + 40, na + 48), IDF, True, True)
+                act(r("at", 128 * h, 128 * h + 128, 1, 8), ps("RB", h, 0, 128, 1, 8), AF.Copy)
+                for q in range(2):
+                    store("y", ("yv", 64 * h, 64 * h + 64, 8 * q, 8 * q + 8), r("vf", 8 * h, 8 * h + 8, 1, 64 * q + 64, 64 * q))
+                    store("y", ("ya", 4 * h, 4 * h + 4, 128 * q, 128 * q + 128), r("at", 128 * h, 128 * h + 128, 1, 4 * q + 4, 4 * q))
+            f = hf("lf", h, o); bank = ps("RA", h, 256, 384)
+            mm(bank, hf("bkap", h), f, True, True)
             to_psum(h, f)
             cp(hf("ci", h), bank)
             ts(hf("cj", h), hf("ci", h), 2047, A.bitwise_and)
             cp(hf("offn", h), hf("cj", h))
             cp(hf("nf", h, 512), hf("cj", h))
-            ts(hf("ck", h), hf("ci", h), 511, A.bitwise_and)
-            cp(hf("nf2", h), hf("ck", h))
-        for h in HS:
-            TB = r("tb", 128 * h, 128 * h + 128, 1, 40); z = hf("lzz", h, o)
-            mm(r("R4", 0, 128), r("idm2", 0, 128), hf("tt", h), True, False); mm(r("R4", 0, 128), selb(1), TB, False, True)
-            mm(r("R4", 128, 256), IDN, z, True, False); mm(r("R4", 128, 256), selb(0), TB, False, True)
-            act(hf("ey", h), r("R4", 0, 128), AF.Relu, 0.0, -1.0)
-            act(hf("lz", h), r("R4", 128, 256), AF.Relu, -256.0, -1.0)
-            mm(r("R4", 256, 384), IDB, z, True, False); mm(r("R4", 256, 384), IDN, hf("ey", h), False, True)
-            act(hf("z1", h), r("R4", 256, 384), AF.Abs)
-        for h in HS:
-            f = hf("lf", h, o); v = 80 + 40 * h; m = 32 * t + 16 * h
-            name_rows(h, r("lme", m, m + 8))
-            act(r("vt", v + 24, v + 32), r("lme", m + 8, m + 16), AF.Copy)
-            act(sm("dn", h), r("lme", m + 8, m + 16), AF.Identity, 0.0, -8192.0)
-            scores(3, h, PLAS, f)
-            for q in range(2):
-                scan(hf("so", h, 256 * q), CMIN, r(SC[h], 128 * q, 128 * q + 128), 0.0, A.add, A.min)
-            ki = whole("so", h, 0, sm("ki", h))
-            ts(r("vt", v + 8, v + 16), ends("so", h), float((600 - 2040) * 8192), A.is_ge)
-            ts(sm("jj", h), ki, 9, A.arith_shift_right, 15, A.bitwise_and)
-            ts(sm("mj", h), ki, 511, A.bitwise_and)
-            ts(sm("cq", h), whole("so", h, 256, sm("ki", h, 16)), 2047, A.bitwise_and)
-            tt(sm("tA", h), sm("mj", h), sm("cq", h), A.subtract)
-            cp(r("vt", v + 16, v + 24), sm("cq", h))
-            tt(r("vt", v, v + 8), sm("tA", h), r("vt", v + 8, v + 16), A.mult)
+            act(hf("nhi", h), hf("nf", h, 512), AF.Identity, 98304.0 - 255.5)
+            TB = r("tf", 128 * h, 128 * h + 128, 1, 8); z = hf("lzz", h, o)
+            mm(ps("RB", h, 0, 128), r("idm2", 0, 128), hf("tt", h), True, False); mm(ps("RB", h, 0, 128), selb(1), TB, False, True)
+            mm(ps("RB", h, 128, 256), IDN, z, True, False); mm(ps("RB", h, 128, 256), selb(0), TB, False, True)
+            act(hf("ey", h), ps("RB", h, 0, 128), AF.Relu, 0.0, -1.0)
+            act(hf("lz", h), ps("RB", h, 128, 256), AF.Relu, -256.0, -1.0)
+            mm(ps("RB", h, 256, 384), IDB, z, True, False); mm(ps("RB", h, 256, 384), IDN, hf("ey", h), False, True)
+            act(hf("z1", h), ps("RB", h, 256, 384), AF.Abs)
+            act(sm("dn", h), vt(t, 3, h, 48, 56), AF.Identity, 0.0, -8192.0)
+            scores(3, h, PLAS(h), f)
+            scan(hf("so", h), CMIN, ps("SC", h, 0, 128), 0.0, A.add, A.min)
+            scan(hf("so", h, 256), CMIN, ps("SC", h, 128, 256), 0.0, A.add, A.min)
+            ts(sm("jj", h), ends("so", h), 9, A.arith_shift_right, 15, A.bitwise_and)
             tt(sm("qd", h), sm("jj", h), sm("dn", h), A.add)
             to_list("qd", h, False)
             act(hf("sw", h, o), ind(YW(h), sm("go", h)), AF.Copy)
-            send("w%s%d" % ("ab"[h], t), -1, hf("lw", h, o), hf("sw", h, o))
+            send("w%d%d" % (h, t), -1, hf("lw", h, o), hf("sw", h, o))
             tt(hf("noh", h), ind(sm("jj", h), CEXP), K16, A.not_equal)
-            write_prep(3, h, f)
-        scatter()
-        ZN = r("sz", o + 256, o + 512)
-        for h in HS:
-            p = r("R2", 384, 512)
-            mm(p, ONE, QUART, True, False); mm(p, IDB, hf("z1", h), False, False)
+            ts(vt(t, 3, h, 16, 24), ends("so", h), float((600 - 2044) * 8192), A.is_ge)
+            ts(vt(t, 3, h, 8, 16), ends("so", h), float((600 - 2044) * 8192), A.is_lt)
+            ts(r("kk", 16 * h, 16 * h + 8), ends("so", h, 256), 2047, A.bitwise_and)
+            ts(r("kk", 16 * h + 8, 16 * h + 16), ends("so", h), 511, A.bitwise_and)
+            tt(vt(t, 3, h, 24, 40), r("kk", 16 * h, 16 * h + 16), vt(t, 3, h, 8, 24), A.mult)
+            write(t, 3, h, f)
+            p = ps("RB", h, 0, 128); ZN = hf("sz", h, o + 256)
+            mm(p, ONE, row(384, 512), True, False); mm(p, IDB, hf("z1", h), False, False)
             mm(p, IDNH, hf("lz", h), False, False); mm(p, IDH, hf("lw", h, o), False, True)
             act(hf("zm", h), p, AF.Identity, MAGIC)
-            act(hf("sz", h, o + 256), hf("zm", h), AF.Identity, -MAGIC)
-            if t < RO - 1: to_psum(h, hf("sz", h, o + 256))
-        if t < RO - 1:
-            send("z%d" % (t + 1), 1, r("lzz", o + 256, o + 512), ZN)
-        else:
-            store("y", ("yc", None), CELL); store("s", ("yz", None), ZN)
-            if ENDC:
-                cp(r("pxs", 0, 1024), r("tab", 0, 1024)); store("y", ("yx", (0, 1024)), r("pxs", 0, 1024))
-                act(r("pxs", 1024, 2048), r("tab", 1024, 2048), AF.Copy); store("s", ("yx", (1024, 2048)), r("pxs", 1024, 2048))
+            act(ZN, hf("zm", h), AF.Identity, -MAGIC)
+            if t < RO - 1:
+                to_psum(h, ZN)
+                send("z%d%d" % (h, t + 1), 1, hf("lzz", h, o + 256), ZN)
             else:
-                store("g", ("yx", None), PLAS)
+                tab = "tab%d" % h; o = 2048 * h
+                for q in range(2):
+                    store("y", ("yz", 64 * h, 64 * h + 64, 128 * q, 128 * q + 128), r("sz", 768 + 128 * h, 896 + 128 * h, 1, 64 * q + 64, 64 * q))
+                store("y", ("yc", 64 * h, 64 * h + 64, 0, 512), r(tab, 2048, 2560, 1, 64))
+                cp(r("pxs", o, o + 1024, 1, 64), r(tab, 0, 1024, 1, 64))
+                store("y", ("yx", 64 * h, 64 * h + 64, 0, 1024), r("pxs", o, o + 1024, 1, 64))
+                act(r("pxs", o + 1024, o + 2048, 1, 128, 64), r(tab, 1024, 2048, 1, 128, 64), AF.Copy)
+                store("s", ("yx", 64 * h, 64 * h + 64, 1024, 2048), r("pxs", o + 1024, o + 2048, 1, 128, 64))
+
+    for h in range(2):
+        cur[0] = h
+        stream(h)
     return ops
 
 
@@ -426,12 +431,16 @@ def needs(ops):
     seen = {n: [] for n in SCRATCH}
     run = {n: [None, [], []] for n, s in SCRATCH.items() if s[0] == P_}
     deps = []; after = []
-    for i, (q, kind, args, rd, wr) in enumerate(ops):
+    def meet(x, y): return x[1] < y[2] and y[1] < x[2] and x[5] < y[4] and y[5] < x[4]
+    for i, (q, kind, args, rd, wr, st) in enumerate(ops):
         d = set(); f = set()
-        for (n, a, b, st, p) in rd:
-            d.update(j for (j, a2, b2, w) in seen[n] if w and a2 < b and a < b2)
-        for (n, a, b, st, p) in wr:
-            d.update(j for (j, a2, b2, w) in seen[n] if a2 < b and a < b2)
+        for x in rd:
+            d.update(j for (j, y, w) in seen[x[0]] if w and meet(x, y))
+        for x in wr:
+            for (j, y, w) in seen[x[0]]:
+                if meet(x, y):
+                    if WAW and q in ("v", "s") and ops[j][0] == q and kind not in MOVES and ops[j][1] not in MOVES: f.add(j)
+                    else: d.add(j)
         for n in set(x[0] for x in rd + wr):
             if n in run:
                 if run[n][0] != q: run[n] = [q, [], run[n][1]]
@@ -440,29 +449,29 @@ def needs(ops):
                 run[n][1].append(i)
         if q == "p":
             f.update(j for j in d if ops[j][0] == "p"); d = set(j for j in d if ops[j][0] != "p")
-        for (n, a, b, st, p) in wr:
-            if st == 1 and p == 128 and args[0][0] != "*": seen[n] = [x for x in seen[n] if not (a <= x[1] and x[2] <= b)]
-            seen[n].append((i, a, b, True))
-        for (n, a, b, st, p) in rd:
-            seen[n].append((i, a, b, False))
+        for x in wr:
+            if x[3] == 1 and args[0][0] != "*":
+                seen[x[0]] = [s for s in seen[x[0]] if not (x[1] <= s[1][1] and s[1][2] <= x[2] and x[5] <= s[1][5] and s[1][4] <= x[4])]
+            seen[x[0]].append((i, x, True))
+        for x in rd:
+            seen[x[0]].append((i, x, False))
         d.discard(i)
         deps.append(d); after.append(f)
     return deps, after
 
 
 def cost(o):
-    q, kind, a, rd, wr = o
+    q, kind, a = o[:3]
     E = EST
     def n(x): return 16 * n(x[2]) if x[0] == "*" else len(range(x[1], x[2], x[3]))
-    def two(x): return SCRATCH[x[0]][2] in (BF, U16)
+    def two(x): return SCRATCH[x[0]][2] in (BF, U16, "float16")
     if kind == "land": return 0.0, E["rem"] + n(a[2]) * 128 * (2 if two(a[2]) else 4) / E["rbw"]
     if kind == "send": return 300.0, 0.0
     if kind in ("load", "store"):
         x = a[0] if kind == "load" else a[1]
-        return (1000.0 if q == "g" else 100.0), E["dma"] + n(x) * 128 * (2 if two(x) or a[0][0] == "yx" else 4) / 200.0
+        return (1000.0 if q == "g" else 100.0), E["dma"] + n(x) * (x[4] - x[5]) * (2 if two(x) else 4) / 100.0
     if kind == "iota": return 130 + 2 * E["cy"] * n(a[0]), 0.0
-    if kind == "tt" and a[1][0] != "*" and a[2][0] in ("XA", "XB") and XBF: return max(64, n(a[0]) * E["xbf"]) * E["cy"], 0.0
-    if kind in ("mm", "tr"): return max(min(64, n(a[1])), n(a[2])) * E["pe"] * (1 if two(a[1]) else 4), 60.0
+    if kind == "mm": return max(min(64, n(a[1])), n(a[2])) * E["pe"] * (1 if two(a[1]) else 4), 60.0
     if a[0][0] == "*": return 50 + n(a[0]) * E["sca"] * E["cy"], 0.0
     if kind != "mset" and a[1][0] == "*": return (50 if q == "v" else 65) + n(a[0]) * E["gam"] * E["cy"], 0.0
     m = 1.0
@@ -479,28 +488,49 @@ def arrange(ops):
         for j in after[i]: pre[i][j] = cs[j][0]
         for j in deps[i]: pre[i][j] = cs[j][0] + cs[j][1] + (EST["same"] if ops[j][0] == o[0] else EST["other"])
         if o[1] == "land": pre[i][i - 1] = cs[i - 1][0]
-    left = [cs[i][0] + cs[i][1] for i in range(N)]
-    nxt = [[] for o in ops]
-    for i in range(N - 1, -1, -1):
-        for j, w in pre[i].items():
-            left[j] = max(left[j], w + left[i]); nxt[j].append(i)
-    todo = [len(p) for p in pre]; ready = [0.0] * N
-    pool = {q: [] for q in QS + [None]}; free = {q: 0.0 for q in pool}
+    dur = [x[0] for x in cs]; tail = [x[1] for x in cs]; qs = [o[0] for o in ops]
+    back = [dict() for o in ops]
     for i in range(N):
-        if not todo[i]: pool[ops[i][0]].append(i)
-    out = []
-    while len(out) < N:
-        t, q = min((max(free[q], min(ready[i] for i in p)), k) for k, (q, p) in enumerate(pool.items()) if p)
-        q = list(pool)[q]
-        i = max((i for i in pool[q] if ready[i] <= t + 1.0), key=lambda i: left[i])
-        soon = [j for j in pool[q] if t < ready[j] < t + 0.6 * cs[i][0] and left[j] > left[i] + cs[i][0]]
-        if soon and q is not None:
-            i = min(soon, key=lambda j: ready[j]); t = ready[i]
-        pool[q].remove(i); out.append(i)
-        if q is not None: free[q] = t + cs[i][0]
-        for j in nxt[i]:
-            ready[j] = max(ready[j], t + pre[j][i]); todo[j] -= 1
-            if not todo[j]: pool[ops[j][0]].append(j)
+        for j, w in pre[i].items(): back[j][i] = w + dur[i] - dur[j]
+
+    def issue(links, nxt, first, prio, look):
+        todo = [len(p) for p in links]; ready = list(first); at = [0.0] * N
+        pool = {q: [] for q in QS + [None]}; free = {q: 0.0 for q in pool}
+        for i in range(N):
+            if not todo[i]: pool[qs[i]].append(i)
+        for done in range(N):
+            t = 1e18
+            for q2, p2 in pool.items():
+                if p2:
+                    t2 = max(free[q2], min([ready[i] for i in p2]))
+                    if t2 < t: t = t2; q = q2; p = p2
+            i = max([i for i in p if ready[i] <= t + 1.0], key=lambda i: prio[i])
+            if q is not None:
+                soon = [j for j in p if t < ready[j] < t + look * dur[i] and prio[j] > prio[i] + dur[i]]
+                if soon:
+                    i = min(soon, key=lambda j: ready[j]); t = ready[i]
+                free[q] = t + dur[i]
+            p.remove(i); at[i] = t
+            for j in nxt[i]:
+                ready[j] = max(ready[j], t + links[j][i]); todo[j] -= 1
+                if not todo[j]: pool[qs[j]].append(j)
+        return at
+
+    def end(s): return max(s[i] + dur[i] + tail[i] for i in range(N))
+    left = [dur[i] + tail[i] + (BIAS if ops[i][5] == 0 else 0.0) for i in range(N)]
+    for i in range(N - 1, -1, -1):
+        for j, w in pre[i].items(): left[j] = max(left[j], w + left[i])
+    s = issue(pre, back, [0.0] * N, left, 0.6)
+    best = cur = (end(s), s)
+    rng = np.random.default_rng(SEED)
+    for it in range(PASSES):
+        shake = rng.random(N // 25 + 1) * NOISE * rng.random()
+        u = issue(back, pre, tail, [cur[1][i] + dur[i] + float(shake[i // 25]) for i in range(N)], float(rng.random()))
+        s = issue(pre, back, [0.0] * N, [u[i] + dur[i] for i in range(N)], float(rng.random()))
+        if end(s) < cur[0] + 800.0: cur = (end(s), s)
+        if end(s) < best[0]: best = (end(s), s)
+    out = sorted(range(N), key=lambda i: (best[1][i], i))
+    INFO[:] = [best[0]]
     pos = {i: k for k, i in enumerate(out)}
     return [ops[i] for i in out], [sorted((pos[j] for j in deps[i]), reverse=True) for i in out]
 
@@ -551,10 +581,14 @@ def rank_program(g, core, T, topo):
             return x
         if x[0] == "*":
             return ap(x[1]).indirect(ap(x[2]))
-        return T[x[0]][0:x[4], x[1]:x[2]:x[3]] if x[3] != 1 else T[x[0]][0:x[4], x[1]:x[2]]
+        return T[x[0]][x[5]:x[4], x[1]:x[2]:x[3]] if x[3] != 1 else T[x[0]][x[5]:x[4], x[1]:x[2]]
+
+    def hbm(x):
+        t = T[x[0]]
+        return t[:, :] if [x[2] - x[1], x[4] - x[3]] == list(t.shape) else t[x[1]:x[2], x[3]:x[4]]
 
     sent = 0; stores = []
-    for i, (q, kind, a, rd, wr) in enumerate(ops):
+    for i, (q, kind, a, rd, wr, st) in enumerate(ops):
         if kind == "land":
             continue
         e = Q[q]
@@ -566,14 +600,9 @@ def rank_program(g, core, T, topo):
             g.remote_dma(ap(a[2]), ap(a[3]), T.sem[a[0]], T.sem.sent, pid, rid, topo.mask(core, dst))
             sent += len(topo.engines(core, dst))
             continue
-        if kind == "load":
-            src = T[a[1][0]]
-            ins = e.dma_start(ap(a[0]), src[:, :] if a[1][1] is None else src[:, a[1][1][0]:a[1][1][1]])
+        if kind == "load": ins = e.dma_start(ap(a[0]), hbm(a[1]))
         elif kind == "store":
-            dst = T[a[0][0]]; h = a[0][1]
-            if h is None: ins = e.dma_start(dst[:, :], ap(a[1]))
-            elif a[0][0] == "yx": ins = e.dma_start(dst[:, h[0]:h[1]], ap(a[1]))
-            else: ins = e.dma_start(dst[:, 128 * h:128 * h + 128], T[a[1][0]][8 * h:8 * h + 8, 0:128])
+            ins = e.dma_start(hbm(a[0]), ap(a[1]))
             stores.append(i)
         elif kind == "cp": ins = e.tensor_copy(ap(a[0]), ap(a[1]))
         elif kind == "tt": ins = e.tensor_tensor(ap(a[0]), ap(a[1]), ap(a[2]), a[3])
@@ -584,9 +613,8 @@ def rank_program(g, core, T, topo):
         elif kind == "mset": ins = e.memset(ap(a[0]), a[1])
         elif kind == "act":
             if a[2] == AF.Copy: ins = e.activation(ap(a[0]), ap(a[1]), a[2])
-            else: ins = e.activation(ap(a[0]), ap(a[1]), a[2], bias=a[3], scale=a[4])
+            else: ins = e.activation(ap(a[0]), ap(a[1]), a[2], bias=a[3], scale=ap(a[4]))
         elif kind == "mm": ins = e.matmul(ap(a[0]), ap(a[1]), ap(a[2]), a[3], a[4])
-        elif kind == "tr": ins = e.transpose(ap(a[0]), ap(a[1]), ap(a[2]))
         elif kind == "iota":
             if SCRATCH[a[0][0]][2] == I32: ins = e.iota(ap(a[0]), a[1], a[2], a[3])
             else: ins = e.iota(ap(a[0]), a[1], a[2], a[3], allow_small_or_imprecise_dtypes=True)

@@ -7,7 +7,12 @@ MAGIC = 12582912.0
 BLK = 64
 NSH = BLK // 16
 NC = BLK // 16
-TABW = 2560 + BLK
+TABW = 2560 + 256
+DIRECT = False
+NMS = False
+NFS = False
+NPS = False
+ENDV = 1024
 YH = 2064
 GA = (("v", 0, 16), ("s", 16, 64), ("s", 64, 96), ("s", 96, 128))
 GATHER = {1: GA, 2: GA, 3: GA}
@@ -21,7 +26,7 @@ NOISE = 500.0
 OFFS = False
 WAW = False
 INFO = []
-EST = {"cy": 0.83, "gam": 1.5, "sca": 3.8, "pe": 0.5, "same": 60.0, "other": 100.0, "rem": 2200.0, "rbw": 40.0, "dma": 2000.0}
+EST = {"cy": 0.83, "gam": 1.56, "sca": 3.8, "pe": 0.5, "same": 150.0, "other": 200.0, "rem": 2200.0, "rbw": 40.0, "dma": 2000.0}
 
 S_, P_ = "sbuf", "psum"
 F32, BF, I32, U16 = "float32", "bfloat16", "int32", "uint16"
@@ -41,7 +46,7 @@ SCRATCH = {
     "noh": (S_, [128, 256], BF), "ex": (S_, [128, 256], BF), "go": (S_, [128, 16], U16), "gs": (S_, [128, 16], U16),
     "nm": (S_, [128, 256], H), "vt": (S_, [128, 4 * RO * VT], H),
     "tf": (S_, [128, 512], H),
-    "s1": (S_, [128, 256], F32), "s2": (S_, [128, 512], F32), "E": (S_, [128, 256 * NSH], BF),
+    "s1": (S_, [128, 256], F32), "s2": (S_, [128, 512], F32), "E": (S_, [128, 256 * 8], BF),
     "ku": (S_, [128, 16], U16), "wo": (S_, [128, 32], U16),
     "xe": (S_, [128, 256], BF), "r2": (S_, [128, 256], H), "bc": (S_, [128, 256], BF), "tt": (S_, [128, 512], H),
     "val": (S_, [128, 512], F32), "ey": (S_, [128, 256], BF), "z1": (S_, [128, 256], BF), "lz": (S_, [128, 256], BF),
@@ -52,9 +57,9 @@ SCRATCH = {
     "sf": (S_, [128, 256 * RO], BF), "lf": (S_, [128, 256 * RO], BF),
     "sw": (S_, [128, 256 * RO], BF), "lw": (S_, [128, 256 * RO], BF),
     "pi": (S_, [128, 8], I32), "pj": (S_, [128, 8], I32), "col": (S_, [128, 32], F32),
-    "k16": (S_, [128, 128], F32), "ug": (S_, [128, 128], F32), "u4": (S_, [128, 128], F32), "cexp": (S_, [128, 8], U16),
+    "k16": (S_, [128, 128], F32), "ug": (S_, [128, 128], F32), "u4": (S_, [128, 128], F32), "cexp": (S_, [128, 8], U16), "cid": (S_, [128, 8], U16), "oh": (S_, [128, 256], BF),
     "wm": (S_, [128, 128], F32), "cown": (S_, [128, 256], F32), "cmin": (S_, [128, 256], F32), "c01": (S_, [128, 128], F32),
-    "rows": (S_, [128, 1296], BF), "nhi": (S_, [128, 256], BF), "one": (S_, [128, 128], BF), "dum": (S_, [128, 16], F32), "nob": (S_, [128, 256], BF),
+    "rows": (S_, [128, 1296], BF), "nhi": (S_, [128, 256], BF), "one": (S_, [128, 128], BF), "dum": (S_, [128, 256], F32), "s2h": (S_, [128, 256], H), "nob": (S_, [128, 256], BF),
     "bo": (S_, [128, 128], F32), "idf": (S_, [128, 128], H), "idm2": (S_, [128, 128], H), "bh8": (S_, [128, 8], H),
     "idb": (S_, [128, 768], BF), "bf8": (S_, [128, 8], F32), "bb": (S_, [128, 96], BF),
     "bx": (S_, [128, 384], BF), "bo4": (S_, [128, 256], BF), "bwu": (S_, [128, 256], BF), "bw8": (S_, [128, 16], BF),
@@ -177,10 +182,10 @@ def plan():
     ts(r("bb", 0, 8), r("bf8", 0, 8), -16.0, A.mult)
     cp(r("bb", 8, 16), r("bf8", 0, 8)); cp(r("bh8", 0, 8), r("bf8", 0, 8))
     cp(CEXP, r("k16", 0, 8))
+    if NFS: ts(r("cid", 0, 8), r("k16", 0, 8), 16.0, A.mult, WC, A.add)
     ts(CMIN, K16, 0.0, A.is_equal, float(1 << 30), A.mult)
     act(COWN, WM, AF.Identity, 0.0, -2 * BIG)
     act(NOB, WM, AF.Identity, -BIG, BIG)
-    act(r("bo4", 0, 128), BO, AF.Identity, 0.0, 4096.0)
     ts(r("c01", 0, 128), K16, 0.0, A.not_equal)
     act(IDF, IDB, AF.Copy)
     ts(r("bb", 16, 24), r("bf8", 0, 8), 65536.0, A.mult)
@@ -207,13 +212,29 @@ def plan():
             add("s", "act", r("bkap", 128 * h + 16 * g8, 128 * h + 16 * g8 + 16), [r("kps", 24 * h, 24 * h + 16), r("bf8", g8, g8 + 1)],
                 (r("bkap", 128 * h + 16 * g8, 128 * h + 16 * g8 + 16), r("kps", 24 * h, 24 * h + 16), AF.Identity, 0.0, r("bf8", g8, g8 + 1)))
     cur[0] = None
-    ts(c(11), WC, 2560.0 - 1024.0, A.add)
-    for j in range(8 // NC):
-        ts(r("dum", NC * j, NC * j + NC), r("k16", 0, NC), 16.0, A.mult, c(11), A.add)
+    if DIRECT:
+        iota(r("s2", 0, 256), [[1, 256]], 2560, 0)
+        for q in range(2): tt(hf("dum", q), hf("s2", q), WM, A.mult)
+    else:
+        iota(r("s2", 0, 128), [[1, 128]], 2560 + 1024, 0)
+        ts(c(11), R6, 128.0, A.mult)
+        ts(r("s2", 128, 256), r("s2", 0, 128), c(11), A.add)
+        tt(r("s2", 256, 384), r("s2", 128, 256), WM, A.mult)
+        act(hf("dum", 0), r("s2", 256, 384), AF.Identity, -2048.0)
     ts(c(16), P3, 0.0, A.is_equal); ts(c(17), P3, 3.0, A.is_equal)
     ts(c(18), P3, 0.0, A.is_equal, 2047.0, A.mult); ts(c(19), P3, 4.0, A.is_equal, 4095.0, A.mult)
     tt(c(20), c(18), c(19), A.add); tt(c(24), c(20), c(17), A.subtract); ts(c(25), c(24), 1.0, A.add)
     ts(r("selk", 0, 128), UG, P7, A.is_equal, c(25), A.mult)
+    if DIRECT:
+        ts(r("pj", 6, 7), r("pi", 0, 1), 2, A.logical_shift_right, 1, A.bitwise_and); ts(r("pj", 7, 8), r("pi", 0, 1), 3, A.bitwise_and)
+        cp(r("col", 6, 8), r("pj", 6, 8))
+        for q in range(2):
+            ts(c(26 + q), c(6), float(q), A.is_equal, c(25), A.mult)
+            ts(r("selk", 256 + 128 * q, 384 + 128 * q), U4, c(7), A.is_equal, c(26 + q), A.mult)
+            act(hf("bo4", q), hf("w4", q), AF.Identity, 0.0, 4096.0)
+        act(r("nob", 128, 256), WM, AF.Identity, -BIG, BIG)
+    else:
+        act(r("bo4", 0, 128), BO, AF.Identity, 0.0, 4096.0)
     ts(c(21), c(16), 4096.0, A.mult, c(17), A.add)
     ts(r("selk", 128, 256), UG, P7, A.is_equal, c(21), A.mult)
     for i, w in enumerate((-256.0, 4096.0, 0.5)):
@@ -271,7 +292,13 @@ def plan():
         if slots: cp(sm("gs", h), ps("RB", h, 8, 16))
 
     def pick_name(step, h, dst):
-        tt(hf("nm", h), ind(r("wm", 0, 16), sm("gs", h)), hf("nf", h, 256 * (step - 1)), A.mult)
+        if NMS:
+            act(hf("oh", h), ind(r("wm", 0, 16), sm("gs", h)), AF.Identity, 0.0, -1.0)
+            mm(ps("RB", h, 384, 512), ID4, hf("oh", h), True, False)
+            mm(ps("RB", h, 384, 512), IDF, hf("nf", h, 256 * (step - 1)), False, True)
+            act(hf("nm", h), ps("RB", h, 384, 512), AF.Relu, -4096.0)
+        else:
+            tt(hf("nm", h), ind(r("wm", 0, 16), sm("gs", h)), hf("nf", h, 256 * (step - 1)), A.mult)
         mm(ps("RB", h, 16, 24), hf("nm", h), r("bh8", 0, 8), True, True)
         act(dst, ps("RB", h, 16, 24), AF.Copy)
 
@@ -295,25 +322,36 @@ def plan():
         act(hf("xe", h), ps("RB", h, 256, 384), AF.Relu)
         act(hf("r2", h), ps("RB", h, 384, 512), AF.Relu, -4096.0)
         if between: between()
-        mm(ps("SC", h, 256, 384), IDB, NOB, True, False); mm(ps("SC", h, 256, 384), ONE, row(256, 384), False, False)
-        mm(ps("SC", h, 256, 384), sel(0), TF, False, False)
+        if DIRECT:
+            mm(ps("SC", h, 256, 512), IDN, r("nob", 0, 256), True, False)
+            for q in range(2): mm(ps("SC", h, 256 + 128 * q, 384 + 128 * q), sel(2 + q), TF, False, False)
+        else:
+            mm(ps("SC", h, 256, 384), IDN, NOB, True, False); mm(ps("SC", h, 256, 384), ONE, row(256, 384), False, False)
+            mm(ps("SC", h, 256, 384), sel(0), TF, False, False)
         T_ = hf("tt", h, 256 * (step - 2))
         ts(sm("ku", h), ends("s1", h), 2560.0, A.min)
         tt(T_, ind(TAB(h), sm("ku", h)), hf("bc", h), A.mult)
         for i in range(NSH):
             s = 1 + 16 * i; e = 256 * i + 128 * h
             tt(r("E", e + s, e + 128), r("s1", 128 * h, 128 * h + 128 - s), ps("RA", h, 128 + s, 256), A.is_equal)
-            mm(ps("SC", h, 256 + s, 384), r("bo4", 0, 128), r("E", e + s, e + 128), False, i == NSH - 1)
+            if DIRECT:
+                for q in range(2):
+                    mm(ps("SC", h, 256 + 128 * q + s, 384 + 128 * q), hf("bo4", q), r("E", e + s, e + 128), False, i == NSH - 1 and q == 1)
+            else:
+                mm(ps("SC", h, 256 + s, 384), r("bo4", 0, 128), r("E", e + s, e + 128), False, i == NSH - 1)
         mm(ps("X", h, 256, 512), ONE, QUART, True, False)
         for q in range(2):
             o = ps("X", h, 256 + 128 * q, 384 + 128 * q)
             mm(o, hf("seh", q), hf("xe", h), False, False); mm(o, hf("sef", q), hf("r2", h), False, False)
         for q in (1, 0): mm(ps("X", h, 256 + 128 * q, 384 + 128 * q), hf("sef", q), T_, False, q == 0)
         for q in (1, 0): act(hf("val", q, 256 * h), ps("X", h, 256 + 128 * q, 384 + 128 * q), AF.Identity, MAGIC)
-        scan(hf("s2", h), COWN, ps("SC", h, 256, 384), -2048.0, A.add, A.max)
-        tt(sm("wf", h), ends("s2", h), r("dum", 0, 8), A.min)
-        for q in range(2): mm(ps("SC", h, 384 + 8 * q, 392 + 8 * q), hf("sef", q), sm("wf", h), True, True)
-        ts(r("wo", 16 * h, 16 * h + 16), ps("SC", h, 384, 400), 1024.0, A.add)
+        if DIRECT:
+            scan(r("s2", 256 * h, 256 * h + 256), r("dum", 0, 256), ps("SC", h, 256, 512), 0.0, A.max, A.min)
+            cp(r("wo", 16 * h, 16 * h + 16), r("s2", 256 * h + 15, 256 * h + 256, 16))
+        else:
+            scan(hf("s2h", h), r("dum", 0, 128), ps("SC", h, 256, 384), -2048.0, A.max, A.min)
+            for q in range(2): mm(ps("SC", h, 384 + 8 * q, 392 + 8 * q), hf("sef", q), ends("s2h", h), True, True)
+            ts(r("wo", 16 * h, 16 * h + 16), ps("SC", h, 384, 400), 1024.0, A.add)
         for b in range(256 // BLK - 1, -1, -1):
             ts(ind(TAB(h), r("wo", 16 * h + NC * b, 16 * h + NC * b + NC)), r("val", 256 * h + BLK * b, 256 * h + BLK * b + BLK),
                1.0, A.mult, -MAGIC, A.add)
@@ -378,7 +416,8 @@ def plan():
             cp(hf("ci", h), bank)
             ts(hf("cj", h), hf("ci", h), 2047, A.bitwise_and)
             cp(hf("offn", h), hf("cj", h))
-            cp(hf("nf", h, 512), hf("cj", h))
+            if NFS: act(hf("nf", h, 512), ind(hf("cj", h), r("cid", 0, 8)), AF.Copy)
+            else: cp(hf("nf", h, 512), hf("cj", h))
             act(hf("nhi", h), hf("nf", h, 512), AF.Identity, 98304.0 - 255.5)
             TB = r("tf", 128 * h, 128 * h + 128, 1, 8); z = hf("lzz", h, o)
             mm(ps("RB", h, 0, 128), r("idm2", 0, 128), hf("tt", h), True, False); mm(ps("RB", h, 0, 128), selb(1), TB, False, True)
@@ -398,7 +437,8 @@ def plan():
             send("w%d%d" % (h, t), -1, hf("lw", h, o), hf("sw", h, o))
             tt(hf("noh", h), ind(sm("jj", h), CEXP), K16, A.not_equal)
             ts(vt(t, 3, h, 16, 24), ends("so", h), float((600 - 2044) * 8192), A.is_ge)
-            ts(vt(t, 3, h, 8, 16), ends("so", h), float((600 - 2044) * 8192), A.is_lt)
+            if NPS: act(vt(t, 3, h, 8, 16), vt(t, 3, h, 16, 24), AF.Identity, 1.0, -1.0)
+            else: ts(vt(t, 3, h, 8, 16), ends("so", h), float((600 - 2044) * 8192), A.is_lt)
             ts(r("kk", 16 * h, 16 * h + 8), ends("so", h, 256), 2047, A.bitwise_and)
             ts(r("kk", 16 * h + 8, 16 * h + 16), ends("so", h), 511, A.bitwise_and)
             tt(vt(t, 3, h, 24, 40), r("kk", 16 * h, 16 * h + 16), vt(t, 3, h, 8, 24), A.mult)
@@ -416,10 +456,12 @@ def plan():
                 for q in range(2):
                     store("y", ("yz", 64 * h, 64 * h + 64, 128 * q, 128 * q + 128), r("sz", 768 + 128 * h, 896 + 128 * h, 1, 64 * q + 64, 64 * q))
                 store("y", ("yc", 64 * h, 64 * h + 64, 0, 512), r(tab, 2048, 2560, 1, 64))
-                cp(r("pxs", o, o + 1024, 1, 64), r(tab, 0, 1024, 1, 64))
-                store("y", ("yx", 64 * h, 64 * h + 64, 0, 1024), r("pxs", o, o + 1024, 1, 64))
-                act(r("pxs", o + 1024, o + 2048, 1, 128, 64), r(tab, 1024, 2048, 1, 128, 64), AF.Copy)
-                store("s", ("yx", 64 * h, 64 * h + 64, 1024, 2048), r("pxs", o + 1024, o + 2048, 1, 128, 64))
+                n = ENDV
+                if n:
+                    cp(r("pxs", o, o + n, 1, 64), r(tab, 0, n, 1, 64))
+                    store("y", ("yx", 64 * h, 64 * h + 64, 0, n), r("pxs", o, o + n, 1, 64))
+                act(r("pxs", o + n, o + 2048, 1, 128, 64), r(tab, n, 2048, 1, 128, 64), AF.Copy)
+                store("s", ("yx", 64 * h, 64 * h + 64, n, 2048), r("pxs", o + n, o + 2048, 1, 128, 64))
 
     for h in range(2):
         cur[0] = h

@@ -3,6 +3,7 @@ from concourse.mybir import AluOpType, ActivationFunctionType
 
 RO = 3
 BIG = float(1 << 21)
+OWN = 16384.0
 MAGIC = 12582912.0
 BLK = 64
 NSH = BLK // 16
@@ -12,38 +13,52 @@ DIRECT = False
 NMS = False
 NFS = False
 NPS = False
-ENDV = 1024
+ENDS = [(("v", 512), ("s", 512), ("v", 512), ("s", 512))] * 2
+SPQ = "vsvv"
+HOLD = 0.0
+SPREAD = False
+CH = 64
+CN = 64
+PX2 = True
+CAST = (0,)
+SXV = False
+SWV = False
+ZV = False
 YH = 2064
 GA = (("v", 0, 16), ("s", 16, 64), ("s", 64, 96), ("s", 96, 128))
 GATHER = {1: GA, 2: GA, 3: GA}
 M1 = ((0, 64), (64, 128))
 MINS = {1: M1, 2: M1, 3: M1}
 BIAS = 1500.0
-PASSES = 100
+PASSES = 120
 SPLIT = False
-SEED = 1
+SEED = 3
 NOISE = 500.0
 OFFS = False
 WAW = False
 INFO = []
 EST = {"cy": 0.83, "gam": 1.56, "sca": 3.8, "pe": 0.5, "same": 150.0, "other": 200.0, "rem": 2200.0, "rbw": 40.0, "dma": 2000.0}
 
+CASES = ({"cy": 0.9, "pe": 0.55, "rem": 2000.0}, {}, {"cy": 1.05, "pe": 0.62, "rem": 1600.0}, {"gam": 1.9, "sca": 5.0, "rem": 2800.0},
+         {"gam": 1.2, "sca": 2.5, "same": 190.0, "other": 250.0})
+PLAN = 2
+
 S_, P_ = "sbuf", "psum"
 F32, BF, I32, U16 = "float32", "bfloat16", "int32", "uint16"
 H = "float16"
-VT = 56
+VT = 64
 SCRATCH = {
     "tab0": (S_, [128, TABW], F32), "tab1": (S_, [128, TABW], F32), "pxs": (S_, [128, 4096], BF), "ces": (S_, [128, 1024], I32),
-    "v0s": (S_, [128, 16], I32), "wk": (S_, [128, 24], BF),
+    "v0s": (S_, [128, 16], I32), "wk": (S_, [128, 32], BF),
     "Y": (S_, [128, 2 * YH], BF), "M": (S_, [128, 4096], BF),
     "offn": (S_, [128, 256], U16), "nf": (S_, [128, 768], H),
     "ci": (S_, [128, 256], I32), "cj": (S_, [128, 256], I32),
-    "bu": (S_, [128, 16], U16), "bj": (S_, [128, 16], I32), "bs": (S_, [128, 256], I32),
+    "bu": (S_, [128, 16 * (RO + 1)], U16), "bj": (S_, [128, 32], I32), "bs": (S_, [128, 256], I32),
     "bt": (S_, [128, 16], I32), "kk": (S_, [128, 32], I32), "vf": (S_, [128, 16], F32),
     "so": (S_, [128, 512], I32), "sc": (S_, [128, 256], F32), "ind": (S_, [128, 256], BF), "ko": (S_, [128, 256], F32),
-    "jj": (S_, [128, 16], I32), "mm": (S_, [128, 16], I32), "thr": (S_, [128, 32], F32),
-    "dn": (S_, [128, 16], F32), "qd": (S_, [128, 16], F32), "wf": (S_, [128, 16], H),
-    "noh": (S_, [128, 256], BF), "ex": (S_, [128, 256], BF), "go": (S_, [128, 16], U16), "gs": (S_, [128, 16], U16),
+    "jj": (S_, [128, 32], I32), "mm": (S_, [128, 32], I32), "thr": (S_, [128, 32], F32),
+    "dn": (S_, [128, 16], F32), "qd": (S_, [128, 32], F32), "wf": (S_, [128, 16], H),
+    "noh": (S_, [128, 288], BF), "ex": (S_, [128, 256], H), "go": (S_, [128, 16], U16), "gs": (S_, [128, 16], U16),
     "nm": (S_, [128, 256], H), "vt": (S_, [128, 4 * RO * VT], H),
     "tf": (S_, [128, 512], H),
     "s1": (S_, [128, 256], F32), "s2": (S_, [128, 512], F32), "E": (S_, [128, 256 * 8], BF),
@@ -53,15 +68,16 @@ SCRATCH = {
     "zm": (S_, [128, 256], F32), "at": (S_, [128, 256], F32),
     "sx": (S_, [128, 256 * RO], BF), "lx": (S_, [128, 256 * RO], BF),
     "sz": (S_, [128, 256 * (RO + 1)], BF), "lzz": (S_, [128, 256 * RO], BF),
-    "sna": (S_, [128, 32 * (RO + 1)], H),
+    "sna": (S_, [128, 48 * (RO + 1)], H),
     "sf": (S_, [128, 256 * RO], BF), "lf": (S_, [128, 256 * RO], BF),
     "sw": (S_, [128, 256 * RO], BF), "lw": (S_, [128, 256 * RO], BF),
-    "pi": (S_, [128, 8], I32), "pj": (S_, [128, 8], I32), "col": (S_, [128, 32], F32),
+    "pi": (S_, [128, 8], I32), "pj": (S_, [128, 8], I32), "col": (S_, [128, 40], F32), "cr": (S_, [128, 4], U16), "wp": (S_, [128, 48], H),
     "k16": (S_, [128, 128], F32), "ug": (S_, [128, 128], F32), "u4": (S_, [128, 128], F32), "cexp": (S_, [128, 8], U16), "cid": (S_, [128, 8], U16), "oh": (S_, [128, 256], BF),
     "wm": (S_, [128, 128], F32), "cown": (S_, [128, 256], F32), "cmin": (S_, [128, 256], F32), "c01": (S_, [128, 128], F32),
-    "rows": (S_, [128, 1296], BF), "nhi": (S_, [128, 256], BF), "one": (S_, [128, 128], BF), "dum": (S_, [128, 256], F32), "s2h": (S_, [128, 256], H), "nob": (S_, [128, 256], BF),
+    "rows": (S_, [128, 1936], BF), "cend": (S_, [128, 8], U16), "bws": (S_, [128, 32], BF), "bwn": (S_, [128, 32], BF), "id5": (S_, [128, 128], H),
+    "qf": (S_, [128, 256], H), "fr": (S_, [128, 256], H), "exb": (S_, [128, 256], H), "sb": (S_, [128, 16 * RO], U16), "nhi": (S_, [128, 256], BF), "one": (S_, [128, 128], BF), "dum": (S_, [128, 256], F32), "s2h": (S_, [128, 256], H), "nob": (S_, [128, 256], BF),
     "bo": (S_, [128, 128], F32), "idf": (S_, [128, 128], H), "idm2": (S_, [128, 128], H), "bh8": (S_, [128, 8], H),
-    "idb": (S_, [128, 768], BF), "bf8": (S_, [128, 8], F32), "bb": (S_, [128, 96], BF),
+    "idb": (S_, [128, 1024], BF), "bf8": (S_, [128, 8], F32), "bb": (S_, [128, 96], BF),
     "bx": (S_, [128, 384], BF), "bo4": (S_, [128, 256], BF), "bwu": (S_, [128, 256], BF), "bw8": (S_, [128, 16], BF),
     "bkap": (S_, [128, 256], BF), "kps": (S_, [128, 48], F32), "selk": (S_, [128, 512], H), "selb": (S_, [128, 384], H),
     "sef": (S_, [128, 256], H), "seh": (S_, [128, 256], BF), "w4": (S_, [128, 256], F32),
@@ -69,9 +85,9 @@ SCRATCH = {
 for _h in range(2):
     for _n in ("X", "SC", "RA", "RB"):
         SCRATCH["%s%d" % (_n, _h)] = (P_, [128, 512], F32)
-MSG = ["x", "z", "n", "f", "m", "w"]
+MSG = ["b", "x", "z", "n", "f", "m", "w"]
 NDMA = 48
-SEMAPHORES = (["qv", "qs", "qp", "qg", "sent"] + ["d%d" % i for i in range(NDMA)]
+SEMAPHORES = (["qv", "qs", "qp", "qg", "sent", "u"] + ["d%d" % i for i in range(NDMA)]
               + ["%s%d%d" % (m, h, t) for m in MSG for h in range(2) for t in range(RO)])
 A = AluOpType
 AF = ActivationFunctionType
@@ -107,7 +123,7 @@ def plan():
     def ts(o, a, s1, op0, s2=None, op1=None): add("v", "ts", o, [a, s1, s2], (o, a, s1, s2, op0, op1))
     def scan(o, d0, d1, init, op0, op1): add("v", "scan", o, [d0, d1], (o, d0, d1, init, op0, op1))
     def mset(o, c): add("v", "mset", o, [], (o, c))
-    def act(o, i, f, bias=0.0, scale=1.0): add("s", "act", o, [i], (o, i, f, bias, scale))
+    def act(o, i, f, bias=0.0, scale=1.0): add("s", "act", o, [i, bias, scale], (o, i, f, bias, scale))
     def mm(o, l, rh, st, sp):
         if SPLIT and l[0] in ("Y", "M"):
             m = l[1] + 64 * l[3]
@@ -126,10 +142,11 @@ def plan():
 
     def hf(name, h, base=0): return r(name, base + 128 * h, base + 128 * h + 128)
     def sm(name, h, base=0): return r(name, base + 8 * h, base + 8 * h + 8)
+    def s16(name, h): return r(name, 16 * h, 16 * h + 8)
     def ends(name, h, base=0): return r(name, base + 128 * h + 15, base + 128 * h + 128, 16)
     def c(i): return r("col", i, i + 1)
     def ps(name, h, a, b, step=1, p=128): return r("%s%d" % (name, h), a, b, step, p)
-    IDB, IDN, ID4, IDH, IDNH, IDG = [r("idb", 128 * i, 128 * i + 128) for i in range(6)]
+    IDB, IDN, ID4, IDH, IDNH, IDG = [hf("idb", i) for i in range(6)]
     IDF = r("idf", 0, 128); K16 = r("k16", 0, 128); UG = r("ug", 0, 128); U4 = r("u4", 0, 128); WM = r("wm", 0, 128); BO = r("bo", 0, 128)
     WC, GC, P7, P3, W16P, G3, R6 = c(0), c(1), c(2), c(3), c(8), c(4), c(5)
     COWN = r("cown", 0, 128); CMIN = r("cmin", 0, 128); CMAX = r("cmin", 128, 256); CEXP = r("cexp", 0, 8); NOB = r("nob", 0, 128)
@@ -142,16 +159,17 @@ def plan():
     def YW(h): return r("Y", YH * h, YH * h + YH)
     def vt(t, step, h, a, b): o = VT * (4 * t + 2 * (step - 2) + h); return r("vt", o + a, o + b)
 
+    def part(name, a, b, q): return r(name, a, b, 1, 64 * q + 64, 64 * q)
+    load("y", r("wk", 16, 17), ("wu", 0, 128, 0, 1))
     for h in range(2):
         cur[0] = h
-        for q in range(2):
-            def part(name, a, b): return r(name, a, b, 1, 64 * q + 64, 64 * q)
-            load("y", part("v0s", 8 * h, 8 * h + 8), ("v0", 64 * h, 64 * h + 64, 8 * q, 8 * q + 8))
-            load("y", part("ces", 512 * h, 512 * h + 512), ("ce", 64 * h, 64 * h + 64, 0, 512))
-            load("s" if h == 0 else "y", part("pxs", 2048 * h, 2048 * h + 2048), ("px", 64 * h, 64 * h + 64, 0, 2048))
-            load("y", part("sz", 128 * h, 128 * h + 128), ("z0", 64 * h, 64 * h + 64, 128 * q, 128 * q + 128))
+        for q in range(2): load("y", part("v0s", 8 * h, 8 * h + 8, q), ("v0", 64 * h, 64 * h + 64, 8 * q, 8 * q + 8))
+        for q in range(2): load("y", part("ces", 512 * h, 512 * h + 512, q), ("ce", 64 * h, 64 * h + 64, 0, 512))
+        for q in range(2): load("y", part("sz", 128 * h, 128 * h + 128, q), ("z0", 64 * h, 64 * h + 64, 128 * q, 128 * q + 128))
+        for q in range(2): load("sy"[h], part("pxs", 2048 * h, 2048 * h + 2048, q), ("px", 64 * h, 64 * h + 64, 0, 2048))
     cur[0] = None
-    load("y", r("wk", 16, 17), ("wu", 0, 128, 0, 1)); load("y", r("wk", 0, 16), ("kap", 0, 128, 0, 16))
+    load("y", r("wk", 0, 16), ("kap", 0, 128, 0, 16))
+    send("u", -1, r("wk", 24, 25), r("wk", 16, 17))
     iota(r("pi", 0, 1), [[0, 1]], 0, 1)
     iota(K16, [[0, 8], [1, 16]], 0, 0)
     iota(UG, [[1, 8], [0, 16]], 0, 0)
@@ -160,15 +178,19 @@ def plan():
     for h in range(2):
         cur[0] = h
         send("z%d0" % h, 1, hf("lzz", h), hf("sz", h))
-        for j in range(4): act(r("tab%d" % h, 512 * j, 512 * j + 512), r("pxs", 2048 * h + 512 * j, 2048 * h + 512 * j + 512), AF.Copy)
+        if h in CAST:
+            src = r("pxs", 2048 * h, 2048 * h + 2048)
+            ops.append(["g", "load", (PLAS(h), src), [src], [PLAS(h)], h])
+        else:
+            for j in range(4): act(r("tab%d" % h, 512 * j, 512 * j + 512), r("pxs", 2048 * h + 512 * j, 2048 * h + 512 * j + 512), AF.Copy)
         cp(sm("bu", h), sm("v0s", h))
         cp(CELL(h), r("ces", 512 * h, 512 * h + 512))
-        mset(r("tab%d" % h, 2560, TABW), 0.0)
+        mset(r("tab%d" % h, 2560, 2568), 0.0)
     cur[0] = None
     iota(row(0, 128), [[0, 8], [4096, 16]], 0, 0)
     iota(U4, [[0, 2], [1, 4], [0, 16]], 0, 0)
     mset(r("one", 0, 128), 1.0); mset(r("Y", 0, 16), 0.0); mset(r("Y", YH, YH + 16), 0.0)
-    ts(r("sna", 0, 32), r("k16", 0, 32), 0.0, A.mult); mset(r("rows", 384, 640), -0.25); mset(r("rows", 256, 384), -1024.0)
+    ts(r("sna", 0, 48), r("k16", 0, 48), 0.0, A.mult); mset(r("rows", 384, 640), -0.25)
     ts(r("pj", 0, 1), r("pi", 0, 1), 15, A.bitwise_and); ts(r("pj", 1, 2), r("pi", 0, 1), 4, A.logical_shift_right)
     ts(r("pj", 2, 3), r("pi", 0, 1), 7, A.bitwise_and); ts(r("pj", 3, 4), r("pi", 0, 1), 3, A.logical_shift_right)
     ts(r("pj", 4, 5), r("pi", 0, 1), 4, A.logical_shift_right, 3, A.bitwise_and)
@@ -182,10 +204,15 @@ def plan():
     ts(r("bb", 0, 8), r("bf8", 0, 8), -16.0, A.mult)
     cp(r("bb", 8, 16), r("bf8", 0, 8)); cp(r("bh8", 0, 8), r("bf8", 0, 8))
     cp(CEXP, r("k16", 0, 8))
+    for n in ("bj", "jj", "mm", "qd"): mset(r(n, 0, 32), 0)
+    ts(c(12), WC, 8.0, A.is_ge); ts(c(13), P7, -8.0, A.add)
+    ts(r("col", 28, 32), r("k16", 0, 4), 2.0, A.mult, c(12), A.add)
+    ts(r("col", 32, 36), r("col", 28, 32), GC, A.is_equal, c(13), A.mult)
+    ts(r("cr", 0, 4), r("col", 32, 36), 8.0, A.add)
+    act(r("wp", 0, 48), r("wm", 0, 48), AF.Identity, 0.0, 0.0); act(r("wp", 16, 32), r("wm", 0, 16), AF.Copy)
     if NFS: ts(r("cid", 0, 8), r("k16", 0, 8), 16.0, A.mult, WC, A.add)
     ts(CMIN, K16, 0.0, A.is_equal, float(1 << 30), A.mult)
-    act(COWN, WM, AF.Identity, 0.0, -2 * BIG)
-    act(NOB, WM, AF.Identity, -BIG, BIG)
+    act(COWN, WM, AF.Identity, 0.0, -2 * OWN)
     ts(r("c01", 0, 128), K16, 0.0, A.not_equal)
     act(IDF, IDB, AF.Copy)
     ts(r("bb", 16, 24), r("bf8", 0, 8), 65536.0, A.mult)
@@ -203,15 +230,17 @@ def plan():
         act(hf("seh", q), hf("sef", q), AF.Identity, 0.0, 0.5)
     for h in range(2):
         cur[0] = h
-        mm(ps("RB", h, 0, 17), hf("seh", h), r("wk", 0, 17), True, True)
-        act(r("kps", 24 * h, 24 * h + 17), ps("RB", h, 0, 17), AF.Identity, 0.0, 2.0)
-        wu = r("kps", 24 * h + 16, 24 * h + 17)
-        ts(hf("bwu", h), BO, wu, A.mult)
-        ts(sm("bw8", h), r("bf8", 0, 8), wu, A.mult)
+        mm(ps("RB", h, 0, 16), hf("seh", h), r("wk", 0, 16), True, True)
+        act(r("kps", 24 * h, 24 * h + 16), ps("RB", h, 0, 16), AF.Identity, 0.0, 2.0)
+        mm(ps("RB", h, 16, 17), hf("seh", h), r("wk", 24, 25), True, True)
+        for j in range(2): ts(sm("bwn", j, 16 * h), r("bf8", 0, 8), ps("RB", h, 16, 17), A.mult, 1.0 / 256, A.mult)
         for g8 in range(8):
             add("s", "act", r("bkap", 128 * h + 16 * g8, 128 * h + 16 * g8 + 16), [r("kps", 24 * h, 24 * h + 16), r("bf8", g8, g8 + 1)],
                 (r("bkap", 128 * h + 16 * g8, 128 * h + 16 * g8 + 16), r("kps", 24 * h, 24 * h + 16), AF.Identity, 0.0, r("bf8", g8, g8 + 1)))
     cur[0] = None
+    mset(r("rows", 1296, 1424), -0.5); mset(r("rows", 1424, 1552), 0.0); mset(r("rows", 1552, 1680), 1.0 / 1024)
+    mset(r("rows", 1680, 1808), 2040.0 * 8192)
+    act(r("bb", 24, 32), r("bf8", 0, 8), AF.Identity, 0.0, -8192.0); act(r("id5", 0, 128), IDB, AF.Identity, 0.0, 512.0)
     if DIRECT:
         iota(r("s2", 0, 256), [[1, 256]], 2560, 0)
         for q in range(2): tt(hf("dum", q), hf("s2", q), WM, A.mult)
@@ -222,19 +251,16 @@ def plan():
         tt(r("s2", 256, 384), r("s2", 128, 256), WM, A.mult)
         act(hf("dum", 0), r("s2", 256, 384), AF.Identity, -2048.0)
     ts(c(16), P3, 0.0, A.is_equal); ts(c(17), P3, 3.0, A.is_equal)
-    ts(c(18), P3, 0.0, A.is_equal, 2047.0, A.mult); ts(c(19), P3, 4.0, A.is_equal, 4095.0, A.mult)
-    tt(c(20), c(18), c(19), A.add); tt(c(24), c(20), c(17), A.subtract); ts(c(25), c(24), 1.0, A.add)
+    ts(c(18), P3, 0.0, A.is_equal, 2047.0, A.mult); ts(c(19), P3, 4.0, A.is_equal, 4096.0, A.mult)
+    ts(c(20), P3, 3.0, A.is_lt, c(18), A.add); tt(c(25), c(20), c(19), A.add)
     ts(r("selk", 0, 128), UG, P7, A.is_equal, c(25), A.mult)
-    if DIRECT:
-        ts(r("pj", 6, 7), r("pi", 0, 1), 2, A.logical_shift_right, 1, A.bitwise_and); ts(r("pj", 7, 8), r("pi", 0, 1), 3, A.bitwise_and)
-        cp(r("col", 6, 8), r("pj", 6, 8))
-        for q in range(2):
-            ts(c(26 + q), c(6), float(q), A.is_equal, c(25), A.mult)
-            ts(r("selk", 256 + 128 * q, 384 + 128 * q), U4, c(7), A.is_equal, c(26 + q), A.mult)
-            act(hf("bo4", q), hf("w4", q), AF.Identity, 0.0, 4096.0)
-        act(r("nob", 128, 256), WM, AF.Identity, -BIG, BIG)
-    else:
-        act(r("bo4", 0, 128), BO, AF.Identity, 0.0, 4096.0)
+    ts(c(22), GC, 3.0, A.is_equal)
+    for j in range(4): act(hf("tf", j), WM, AF.Identity, 0.0, c(22))
+    act(hf("s1", 0), WM, AF.Identity, -OWN, OWN); act(hf("s1", 1), WM, AF.Identity, OWN - 1024.0, -OWN)
+    for j in range(2):
+        act(hf("val", j), hf("s1", j), AF.Identity, 0.0, c(22))
+        tt(hf("selk", 2 + j), hf("val", j), hf("selk", 0), A.add)
+    act(r("bo4", 0, 128), BO, AF.Identity, 0.0, 4096.0)
     ts(c(21), c(16), 4096.0, A.mult, c(17), A.add)
     ts(r("selk", 128, 256), UG, P7, A.is_equal, c(21), A.mult)
     for i, w in enumerate((-256.0, 4096.0, 0.5)):
@@ -250,9 +276,10 @@ def plan():
         if step == 2:
             mm(ps("SC", h, 0, 128), ONE, row(0, 128), True, False)
             mm(ps("SC", h, 0, 128), x, r("bx", 0, 128), False, False)
-            mm(ps("RB", h, 128, 256), ONE, row(128, 256), True, False)
+            mm(ps("RB", h, 128, 256), ONE, row(128, 256), True, False);
         elif step == 1:
-            mm(ps("SC", h, 0, 128), ONE, row(128, 256), True, False)
+            mm(ps("SC", h, 0, 128), ONE, row(784, 912), True, False); mm(ps("SC", h, 0, 128), ONE, row(1680, 1808), False, False)
+            mm(ps("RA", h, 0, 256), ONE, row(1296, 1552), True, False); mm(ps("RA", h, 0, 128), ONE, row(1552, 1680), False, False)
         else:
             mm(ps("SC", h, 0, 256), ONE, row(784, 1040), True, False); mm(ps("SC", h, 0, 256), ONE, row(1040, 1296), False, False)
             mm(ps("SC", h, 0, 256), x, r("bx", 128, 384), False, False)
@@ -265,13 +292,19 @@ def plan():
         if step > 1:
             for k in range(16):
                 mm(ps("SC", h, k, w, 16), r("Y", y0 + k, y0 + 2048, 16), r("bb", 16, 24) if step == 2 else r("bb", 48, 64), False, False)
+        else:
+            for k in range(16):
+                mm(ps("RA", h, k, 256, 16), r("Y", y0 + k, y0 + 2048, 16), r("bwn", 16 * h, 16 * h + 16), False, k == 15)
+            ts(hf("qf", h), ps("RA", h, 0, 128), MAGIC, A.add, -MAGIC, A.add)
+            tt(hf("fr", h), ps("RA", h, 128, 256), hf("qf", h), A.subtract)
         for a, b in MINS[step]:
             for k in range(16):
                 m0 = 2048 * h + 128 * k
                 tt(r("M", m0 + a, m0 + b), r("Y", y0 + 16 * a + k, y0 + 16 * b, 16), ps("X", h, a, b), A.min)
         for k in range(16):
             mm(ps("SC", h, k, w, 16), r("M", 2048 * h + 128 * k, 2048 * h + 128 * k + 128),
-               (r("bb", 0, 8), r("bb", 32, 40), r("bb", 64, 80))[step - 1], False, k == 15 and step == 1)
+               (r("bb", 24, 32), r("bb", 32, 40), r("bb", 64, 80))[step - 1], False, False)
+        if step == 1: mm(ps("SC", h, 0, 128), r("id5", 0, 128), hf("fr", h), False, True)
         if step == 3:
             mm(ps("SC", h, 0, 128), nf, IDF, False, False); mm(ps("SC", h, 128, 256), nf, IDF, False, True)
         if step == 2:
@@ -279,15 +312,33 @@ def plan():
             for k in range(16):
                 mm(ps("RB", h, 128 + k, 256, 16), r("M", 2048 * h + 128 * k, 2048 * h + 128 * k + 128), r("bb", 0, 8), False, False)
 
-    def names(step, h, win):
-        act(hf("nf", h, 256 * (step - 1)), ind(win, sm("bu", h)), AF.Copy)
-        cp(hf("offn", h), hf("nf", h, 256 * (step - 1)) if OFFS else ind(win, sm("bu", h)))
+    def names(step, h, win, cells):
+        act(hf("nf", h, 256 * (step - 1)), ind(win, cells), AF.Copy)
+        for a in range(0, 128, CN):
+            cp(r("offn", 128 * h + a, 128 * h + a + CN), ind(win, r(cells[0], cells[1] + a // 16, cells[1] + (a + CN) // 16)))
 
-    def to_list(src, h, slots):
-        tt(hf("ex", h), ind(sm(src, h), CEXP), WM, A.mult)
+    def pick(o, h, v):
+        if v: cp(o, ind(YW(h), sm("go", h)))
+        else: act(o, ind(YW(h), sm("go", h)), AF.Copy)
+
+    def spread(src, dst, h, q):
+        if not SPREAD: return tt(hf(dst, h), ind(s16(src, h), CEXP), WM, A.mult)
+        o = r(dst, 64 * h, 64 * h + 64); i = ind(r(src, 16 * h, 16 * h + 16), r("cr", 0, 4))
+        if q == "v": cp(o, i)
+        else: act(o, i, AF.Copy)
+
+    def turn(src, h, bank, a, start):
+        if not SPREAD: return mm(ps(bank, h, a, a + 8), hf(src, h), r("bh8", 0, 8), start, True)
+        for g8 in range(8):
+            p0 = 32 * (g8 // 2); w0 = 16 * (1 - g8 % 2)
+            mm(r("%s%d" % (bank, h), a, a + 8, 1, p0 + 32, p0), r("wp", w0, w0 + 32), r(src, 64 * h + g8, 64 * h + 64, 8),
+               start and g8 % 2 == 0, g8 % 2 == 1)
+
+    def to_list(src, h, slots, q):
+        spread(src, "ex", h, q)
         mm(ps("RB", h, 0, 8), ONE, row(768, 776), True, False)
-        mm(ps("RB", h, 0, 8), hf("ex", h), r("bb", 8, 16), False, True)
-        if slots: mm(ps("RB", h, 8, 16), hf("ex", h), r("bb", 8, 16), True, True)
+        turn("ex", h, "RB", 0, False)
+        if slots: turn("ex", h, "RB", 8, True)
         ts(sm("go", h), ps("RB", h, 0, 8), W16P, A.add)
         if slots: cp(sm("gs", h), ps("RB", h, 8, 16))
 
@@ -302,35 +353,33 @@ def plan():
         mm(ps("RB", h, 16, 24), hf("nm", h), r("bh8", 0, 8), True, True)
         act(dst, ps("RB", h, 16, 24), AF.Copy)
 
+    def rows(o, sel, i, j, start, stop):
+        K = 64 if sel == "selk" else 8
+        mm(o, r(sel, 128 * i, 128 * i + 128, 1, K), r("tf", 128 * j, 128 * j + 128, 1, K), start, stop)
+
     def write(t, step, h, x, between=None):
-        K = 32 if step == 2 else 40; j = 2 * (step - 2) + h
+        j = 2 * (step - 2) + h
+        KM = ps("X", h, 0, 128); KR = ps("RA", h, 128, 256); P = ps("SC", h, 256, 384)
+        K = 32 if step == 2 else 40
         mm(ps("RA", h, 0, 128, 1, K), vt(t, step, h, 16, 16 + K), IDF, True, True)
-        TF = r("tf", 128 * j, 128 * j + 128, 1, K); TB = r("tf", 128 * j, 128 * j + 128, 1, 8)
-        act(TF, ps("RA", h, 0, 128, 1, K), AF.Copy)
-        def sel(i): return r("selk", 128 * i, 128 * i + 128, 1, K)
-        KM = ps("X", h, 0, 128)
-        mm(KM, IDB, NOB, True, False); mm(KM, sel(0), TF, False, True)
-        mm(ps("RA", h, 128, 256), sel(0), TF, True, True)
+        act(r("tf", 128 * j, 128 * j + 128, 1, K), ps("RA", h, 0, 128, 1, K), AF.Copy)
+        rows(KM, "selk", 2, j, True, True)
+        rows(KR, "selk", 0, j, True, True)
         scan(hf("s1", h), COWN, KM, -1.0, A.add, A.max)
         o = ps("RB", h, 128, 256)
-        mm(o, hf("noh", h), IDB, True, False); mm(o, selb(2), TB, False, True)
+        mm(o, hf("noh", h), IDB, True, False); rows(o, "selb", 2, j, False, True)
         o = ps("RB", h, 256, 384)
-        mm(o, IDB, x, True, False); mm(o, selb(0), TB, False, True)
+        mm(o, IDB, x, True, False); rows(o, "selb", 0, j, False, True)
         o = ps("RB", h, 384, 512)
-        mm(o, hf("noh", h), ID4, True, False); mm(o, sel(1), TF, False, True)
+        mm(o, hf("noh", h), ID4, True, False); rows(o, "selk", 1, j, False, True)
         act(hf("bc", h), ps("RB", h, 128, 256), AF.Abs, -0.5)
         act(hf("xe", h), ps("RB", h, 256, 384), AF.Relu)
         act(hf("r2", h), ps("RB", h, 384, 512), AF.Relu, -4096.0)
         if between: between()
-        if DIRECT:
-            mm(ps("SC", h, 256, 512), IDN, r("nob", 0, 256), True, False)
-            for q in range(2): mm(ps("SC", h, 256 + 128 * q, 384 + 128 * q), sel(2 + q), TF, False, False)
-        else:
-            mm(ps("SC", h, 256, 384), IDN, NOB, True, False); mm(ps("SC", h, 256, 384), ONE, row(256, 384), False, False)
-            mm(ps("SC", h, 256, 384), sel(0), TF, False, False)
+        rows(P, "selk", 3, j, True, False)
         T_ = hf("tt", h, 256 * (step - 2))
         ts(sm("ku", h), ends("s1", h), 2560.0, A.min)
-        tt(T_, ind(TAB(h), sm("ku", h)), hf("bc", h), A.mult)
+        tt(T_, ind(r("tab%d" % h, 0, 2568), sm("ku", h)), hf("bc", h), A.mult)
         for i in range(NSH):
             s = 1 + 16 * i; e = 256 * i + 128 * h
             tt(r("E", e + s, e + 128), r("s1", 128 * h, 128 * h + 128 - s), ps("RA", h, 128 + s, 256), A.is_equal)
@@ -359,53 +408,55 @@ def plan():
     def stream(h):
         to_psum(h, hf("sz", h))
         for t in range(RO):
-            o = 256 * t; na = 32 * t + 16 * h
-            names(1, h, r("ces", 512 * h, 512 * h + 512) if t == 0 else CELL(h))
+            o = 256 * t; na = 48 * t + 24 * h
+            names(1, h, r("ces", 512 * h, 512 * h + 512) if t == 0 else CELL(h), sm("bu", h, 16 * t))
             scores(1, h, r("pxs", 2048 * h, 2048 * h + 2048) if t == 0 else PLAS(h), None)
             scan(hf("so", h), CMIN, ps("SC", h, 0, 128), 0.0, A.add, A.min)
-            ts(sm("jj", h), ends("so", h), 15, A.bitwise_and)
-            to_list("jj", h, True)
-            act(hf("sx", h, o), ind(YW(h), sm("go", h)), AF.Copy)
+            ts(s16("bj", h), ends("so", h), 511, A.bitwise_and)
+            spread("bj", "exb", h, SPQ[0])
+            turn("exb", h, "RA", 256, True)
+            cp(sm("sb", h, 16 * t), ps("RA", h, 256, 264))
+            BU = sm("bu", h, 16 * t + 16)
+            send("b%d%d" % (h, t), 1, BU, sm("sb", h, 16 * t))
+            ts(s16("jj", h), ends("so", h), 9, A.arith_shift_right, 15, A.bitwise_and)
+            to_list("jj", h, True, SPQ[1])
+            pick(hf("sx", h, o), h, SXV)
             send("x%d%d" % (h, t), 1, hf("lx", h, o), hf("sx", h, o))
+            cp(r("sna", na + 16, na + 24), s16("bj", h))
             pick_name(1, h, r("sna", na, na + 8))
-            send("n%d%d" % (h, t), 1, vt(t, 2, h, 40, 56), r("sna", na, na + 16))
-            x = hf("lx", h, o); bank = ps("RA", h, 256, 384)
-            mm(bank, IDB, NOB, True, False); mm(bank, hf("bwu", h), x, False, True)
+            send("n%d%d" % (h, t), 1, vt(t, 2, h, 40, 64), r("sna", na, na + 24))
+            x = hf("lx", h, o)
             to_psum(h, x)
-            scan(hf("bs", h), COWN, bank, 0.0, A.add, A.max)
-            ts(sm("bj", h), ends("bs", h), 511, A.bitwise_and)
-            cp(sm("bu", h), sm("bj", h))
-            names(2, h, CELL(h))
+            names(2, h, r("ces", 512 * h, 512 * h + 512) if t == 0 and PX2 else CELL(h), BU)
             act(sm("thr", h, 16), vt(t, 2, h, 48, 56), AF.Abs, -2.0, 2.0)
             act(sm("thr", h), sm("thr", h, 16), AF.Identity, -10.0, -1.0)
-            mm(ps("RB", h, 24, 32), x, sm("bw8", h), True, True)
-            cp(sm("bt", h), ps("RB", h, 24, 32)); ts(r("kk", 16 * h + 8, 16 * h + 16), sm("bt", h), 511, A.bitwise_and)
-            scores(2, h, PLAS(h), x)
+            scores(2, h, r("pxs", 2048 * h, 2048 * h + 2048) if t == 0 and PX2 else PLAS(h), x)
             scan(hf("so", h), CMIN, ps("SC", h, 0, 128), 0.0, A.add, A.min)
             act(hf("ind", h), ps("SC", h, 0, 128), AF.Sign, 255.985, -1.0 / 65536)
-            ts(sm("jj", h), ends("so", h), 12, A.arith_shift_right, 15, A.bitwise_and)
-            tt(hf("noh", h), ind(sm("jj", h), CEXP), K16, A.not_equal)
+            ts(s16("jj", h), ends("so", h), 12, A.arith_shift_right, 15, A.bitwise_and)
+            tt(hf("noh", h), ind(s16("jj", h), CEXP), K16, A.not_equal)
             mm(ps("RB", h, 128, 256), IDG, hf("noh", h), False, True)
             ts(r("kk", 16 * h, 16 * h + 8), ends("so", h), 2047, A.bitwise_and)
             scan(hf("sc", h), r("c01", 0, 128), hf("ind", h), 0.0, A.mult, A.add)
             tt(vt(t, 2, h, 16, 24), ends("sc", h), sm("thr", h), A.is_lt)
             e = vt(t, 2, h, 8, 16)
             tt(e, ends("sc", h), sm("thr", h), A.is_ge)
-            tt(vt(t, 2, h, 24, 40), r("kk", 16 * h, 16 * h + 16), vt(t, 2, h, 8, 24), A.mult)
+            tt(vt(t, 2, h, 24, 32), r("kk", 16 * h, 16 * h + 8), e, A.mult)
+            tt(vt(t, 2, h, 32, 40), vt(t, 2, h, 56, 64), vt(t, 2, h, 16, 24), A.mult)
             scan(hf("so", h, 256), CMIN, ps("RB", h, 128, 256), 0.0, A.add, A.min)
-            ts(sm("mm", h), ends("so", h, 256), 15, A.bitwise_and)
-            to_list("mm", h, True)
+            ts(s16("mm", h), ends("so", h, 256), 15, A.bitwise_and)
+            to_list("mm", h, True, SPQ[2])
             tt(hf("sf", h, o), ind(YW(h), sm("go", h)), x, A.max)
             send("f%d%d" % (h, t), 1, hf("lf", h, o), hf("sf", h, o))
-            tt(r("sna", na + 40, na + 48), vt(t, 2, h, 48, 56), e, A.add)
+            tt(r("sna", na + 56, na + 64), vt(t, 2, h, 48, 56), e, A.add)
 
             def name_m():
                 pick_name(2, h, vt(t, 2, h, 0, 8))
                 send("m%d%d" % (h, t), 1, vt(t, 3, h, 40, 56), vt(t, 2, h, 0, 16))
             write(t, 2, h, x, name_m)
             if t == RO - 1:
-                cp(sm("vf", h), sm("bj", h))
-                mm(ps("RB", h, 0, 128, 1, 8), r("sna", na + 40, na + 48), IDF, True, True)
+                cp(sm("vf", h), BU)
+                mm(ps("RB", h, 0, 128, 1, 8), r("sna", na + 56, na + 64), IDF, True, True)
                 act(r("at", 128 * h, 128 * h + 128, 1, 8), ps("RB", h, 0, 128, 1, 8), AF.Copy)
                 for q in range(2):
                     store("y", ("yv", 64 * h, 64 * h + 64, 8 * q, 8 * q + 8), r("vf", 8 * h, 8 * h + 8, 1, 64 * q + 64, 64 * q))
@@ -413,15 +464,17 @@ def plan():
             f = hf("lf", h, o); bank = ps("RA", h, 256, 384)
             mm(bank, hf("bkap", h), f, True, True)
             to_psum(h, f)
-            cp(hf("ci", h), bank)
-            ts(hf("cj", h), hf("ci", h), 2047, A.bitwise_and)
-            cp(hf("offn", h), hf("cj", h))
+            for a in range(0, 128, CH):
+                def pc(n): return r(n, 128 * h + a, 128 * h + a + CH)
+                cp(pc("ci"), ps("RA", h, 256 + a, 256 + a + CH))
+                ts(pc("cj"), pc("ci"), 2047, A.bitwise_and)
+                cp(pc("offn"), pc("cj"))
             if NFS: act(hf("nf", h, 512), ind(hf("cj", h), r("cid", 0, 8)), AF.Copy)
             else: cp(hf("nf", h, 512), hf("cj", h))
             act(hf("nhi", h), hf("nf", h, 512), AF.Identity, 98304.0 - 255.5)
-            TB = r("tf", 128 * h, 128 * h + 128, 1, 8); z = hf("lzz", h, o)
-            mm(ps("RB", h, 0, 128), r("idm2", 0, 128), hf("tt", h), True, False); mm(ps("RB", h, 0, 128), selb(1), TB, False, True)
-            mm(ps("RB", h, 128, 256), IDN, z, True, False); mm(ps("RB", h, 128, 256), selb(0), TB, False, True)
+            z = hf("lzz", h, o)
+            mm(ps("RB", h, 0, 128), r("idm2", 0, 128), hf("tt", h), True, False); rows(ps("RB", h, 0, 128), "selb", 1, h, False, True)
+            mm(ps("RB", h, 128, 256), IDN, z, True, False); rows(ps("RB", h, 128, 256), "selb", 0, h, False, True)
             act(hf("ey", h), ps("RB", h, 0, 128), AF.Relu, 0.0, -1.0)
             act(hf("lz", h), ps("RB", h, 128, 256), AF.Relu, -256.0, -1.0)
             mm(ps("RB", h, 256, 384), IDB, z, True, False); mm(ps("RB", h, 256, 384), IDN, hf("ey", h), False, True)
@@ -430,12 +483,12 @@ def plan():
             scores(3, h, PLAS(h), f)
             scan(hf("so", h), CMIN, ps("SC", h, 0, 128), 0.0, A.add, A.min)
             scan(hf("so", h, 256), CMIN, ps("SC", h, 128, 256), 0.0, A.add, A.min)
-            ts(sm("jj", h), ends("so", h), 9, A.arith_shift_right, 15, A.bitwise_and)
-            tt(sm("qd", h), sm("jj", h), sm("dn", h), A.add)
-            to_list("qd", h, False)
-            act(hf("sw", h, o), ind(YW(h), sm("go", h)), AF.Copy)
+            ts(s16("jj", h), ends("so", h), 9, A.arith_shift_right, 15, A.bitwise_and)
+            tt(s16("qd", h), s16("jj", h), sm("dn", h), A.add)
+            to_list("qd", h, False, SPQ[3])
+            pick(hf("sw", h, o), h, SWV)
             send("w%d%d" % (h, t), -1, hf("lw", h, o), hf("sw", h, o))
-            tt(hf("noh", h), ind(sm("jj", h), CEXP), K16, A.not_equal)
+            tt(hf("noh", h), ind(s16("jj", h), CEXP), K16, A.not_equal)
             ts(vt(t, 3, h, 16, 24), ends("so", h), float((600 - 2044) * 8192), A.is_ge)
             if NPS: act(vt(t, 3, h, 8, 16), vt(t, 3, h, 16, 24), AF.Identity, 1.0, -1.0)
             else: ts(vt(t, 3, h, 8, 16), ends("so", h), float((600 - 2044) * 8192), A.is_lt)
@@ -446,8 +499,11 @@ def plan():
             p = ps("RB", h, 0, 128); ZN = hf("sz", h, o + 256)
             mm(p, ONE, row(384, 512), True, False); mm(p, IDB, hf("z1", h), False, False)
             mm(p, IDNH, hf("lz", h), False, False); mm(p, IDH, hf("lw", h, o), False, True)
-            act(hf("zm", h), p, AF.Identity, MAGIC)
-            act(ZN, hf("zm", h), AF.Identity, -MAGIC)
+            if ZV:
+                ts(ZN, p, MAGIC, A.add, -MAGIC, A.add)
+            else:
+                act(hf("zm", h), p, AF.Identity, MAGIC)
+                act(ZN, hf("zm", h), AF.Identity, -MAGIC)
             if t < RO - 1:
                 to_psum(h, ZN)
                 send("z%d%d" % (h, t + 1), 1, hf("lzz", h, o + 256), ZN)
@@ -456,12 +512,14 @@ def plan():
                 for q in range(2):
                     store("y", ("yz", 64 * h, 64 * h + 64, 128 * q, 128 * q + 128), r("sz", 768 + 128 * h, 896 + 128 * h, 1, 64 * q + 64, 64 * q))
                 store("y", ("yc", 64 * h, 64 * h + 64, 0, 512), r(tab, 2048, 2560, 1, 64))
-                n = ENDV
-                if n:
-                    cp(r("pxs", o, o + n, 1, 64), r(tab, 0, n, 1, 64))
-                    store("y", ("yx", 64 * h, 64 * h + 64, 0, n), r("pxs", o, o + n, 1, 64))
-                act(r("pxs", o + n, o + 2048, 1, 128, 64), r(tab, n, 2048, 1, 128, 64), AF.Copy)
-                store("s", ("yx", 64 * h, 64 * h + 64, n, 2048), r("pxs", o + n, o + 2048, 1, 128, 64))
+                a = 0
+                for q, n in ENDS[h]:
+                    p0 = 0 if q == "v" else 64
+                    dst = r("pxs", o + a, o + a + n, 1, p0 + 64, p0); src = r(tab, a, a + n, 1, p0 + 64, p0)
+                    if q == "v": cp(dst, src)
+                    else: act(dst, src, AF.Copy)
+                    store("y", ("yx", 64 * h, 64 * h + 64, a, a + n), dst)
+                    a += n
 
     for h in range(2):
         cur[0] = h
@@ -497,18 +555,19 @@ def needs(ops):
             seen[x[0]].append((i, x, True))
         for x in rd:
             seen[x[0]].append((i, x, False))
+        if kind == "load":
+            f.update(j for j in range(i) if ops[j][1] == "load" and ops[j][0] == q)
         d.discard(i)
         deps.append(d); after.append(f)
     return deps, after
 
 
-def cost(o):
+def cost(o, E):
     q, kind, a = o[:3]
-    E = EST
     def n(x): return 16 * n(x[2]) if x[0] == "*" else len(range(x[1], x[2], x[3]))
     def two(x): return SCRATCH[x[0]][2] in (BF, U16, "float16")
     if kind == "land": return 0.0, E["rem"] + n(a[2]) * 128 * (2 if two(a[2]) else 4) / E["rbw"]
-    if kind == "send": return 300.0, 0.0
+    if kind == "send": return (2300.0 if a[0] == "u" else 300.0), 0.0
     if kind in ("load", "store"):
         x = a[0] if kind == "load" else a[1]
         return (1000.0 if q == "g" else 100.0), E["dma"] + n(x) * (x[4] - x[5]) * (2 if two(x) else 4) / 100.0
@@ -524,18 +583,32 @@ def cost(o):
 
 def arrange(ops):
     deps, after = needs(ops)
-    N = len(ops); cs = [cost(o) for o in ops]
-    pre = [dict() for o in ops]
-    for i, o in enumerate(ops):
-        for j in after[i]: pre[i][j] = cs[j][0]
-        for j in deps[i]: pre[i][j] = cs[j][0] + cs[j][1] + (EST["same"] if ops[j][0] == o[0] else EST["other"])
-        if o[1] == "land": pre[i][i - 1] = cs[i - 1][0]
-    dur = [x[0] for x in cs]; tail = [x[1] for x in cs]; qs = [o[0] for o in ops]
-    back = [dict() for o in ops]
-    for i in range(N):
-        for j, w in pre[i].items(): back[j][i] = w + dur[i] - dur[j]
+    N = len(ops); qs = [o[0] for o in ops]
 
-    def issue(links, nxt, first, prio, look):
+    def graph(E):
+        cs = [cost(o, E) for o in ops]
+        pre = [dict() for o in ops]; back = [dict() for o in ops]
+        for i, o in enumerate(ops):
+            for j in after[i]: pre[i][j] = cs[j][0]
+            for j in deps[i]: pre[i][j] = cs[j][0] + cs[j][1] + (E["same"] if ops[j][0] == o[0] else E["other"])
+            if o[1] == "land": pre[i][i - 1] = cs[i - 1][0]
+            for j, w in pre[i].items(): back[j][i] = w + cs[i][0] - cs[j][0]
+        return pre, back, [x[0] for x in cs], [x[1] for x in cs]
+    cases = [graph(dict(EST, **x)) for x in CASES]
+
+    def length(order, case):
+        pre, back, dur, tail = case
+        at = [0.0] * N; free = {q: 0.0 for q in QS + [None]}; last = 0.0
+        for i in order:
+            t = free[qs[i]]
+            for j, w in pre[i].items():
+                if at[j] + w > t: t = at[j] + w
+            at[i] = t
+            if qs[i] is not None: free[qs[i]] = t + dur[i]
+            if t + dur[i] + tail[i] > last: last = t + dur[i] + tail[i]
+        return last
+
+    def issue(dur, links, nxt, first, prio, look):
         todo = [len(p) for p in links]; ready = list(first); at = [0.0] * N
         pool = {q: [] for q in QS + [None]}; free = {q: 0.0 for q in pool}
         for i in range(N):
@@ -558,20 +631,24 @@ def arrange(ops):
                 if not todo[j]: pool[qs[j]].append(j)
         return at
 
-    def end(s): return max(s[i] + dur[i] + tail[i] for i in range(N))
+    def judge(s):
+        order = sorted(range(N), key=lambda i: (s[i], i))
+        return sum(length(order, x) for x in cases) / len(cases), s, order
+    pre, back, dur, tail = cases[0]
     left = [dur[i] + tail[i] + (BIAS if ops[i][5] == 0 else 0.0) for i in range(N)]
     for i in range(N - 1, -1, -1):
         for j, w in pre[i].items(): left[j] = max(left[j], w + left[i])
-    s = issue(pre, back, [0.0] * N, left, 0.6)
-    best = cur = (end(s), s)
+    hold = [HOLD if o[5] == 1 and o[4] and o[4][0][0] == "Y" else 0.0 for o in ops]
+    best = cur = judge(issue(dur, pre, back, hold, left, 0.6))
     rng = np.random.default_rng(SEED)
     for it in range(PASSES):
+        pre, back, dur, tail = cases[int(rng.integers(PLAN))]
         shake = rng.random(N // 25 + 1) * NOISE * rng.random()
-        u = issue(back, pre, tail, [cur[1][i] + dur[i] + float(shake[i // 25]) for i in range(N)], float(rng.random()))
-        s = issue(pre, back, [0.0] * N, [u[i] + dur[i] for i in range(N)], float(rng.random()))
-        if end(s) < cur[0] + 800.0: cur = (end(s), s)
-        if end(s) < best[0]: best = (end(s), s)
-    out = sorted(range(N), key=lambda i: (best[1][i], i))
+        u = issue(dur, back, pre, tail, [cur[1][i] + dur[i] + float(shake[i // 25]) for i in range(N)], float(rng.random()))
+        new = judge(issue(dur, pre, back, hold, [u[i] + dur[i] for i in range(N)], float(rng.random())))
+        if new[0] < cur[0] + 800.0: cur = new
+        if new[0] < best[0]: best = new
+    out = best[2]
     INFO[:] = [best[0]]
     pos = {i: k for k, i in enumerate(out)}
     return [ops[i] for i in out], [sorted((pos[j] for j in deps[i]), reverse=True) for i in out]
@@ -642,7 +719,7 @@ def rank_program(g, core, T, topo):
             g.remote_dma(ap(a[2]), ap(a[3]), T.sem[a[0]], T.sem.sent, pid, rid, topo.mask(core, dst))
             sent += len(topo.engines(core, dst))
             continue
-        if kind == "load": ins = e.dma_start(ap(a[0]), hbm(a[1]))
+        if kind == "load": ins = e.dma_start(ap(a[0]), ap(a[1]) if rd else hbm(a[1]))
         elif kind == "store":
             ins = e.dma_start(hbm(a[0]), ap(a[1]))
             stores.append(i)
@@ -652,10 +729,11 @@ def rank_program(g, core, T, topo):
             if a[5] is None: ins = e.tensor_scalar(ap(a[0]), ap(a[1]), ap(a[2]), None, a[4])
             else: ins = e.tensor_scalar(ap(a[0]), ap(a[1]), ap(a[2]), ap(a[3]), a[4], a[5])
         elif kind == "scan": ins = e.tensor_tensor_scan(ap(a[0]), ap(a[1]), ap(a[2]), a[3], a[4], a[5])
+        elif kind == "tr": ins = e.transpose(ap(a[0]), ap(a[1]))
         elif kind == "mset": ins = e.memset(ap(a[0]), a[1])
         elif kind == "act":
             if a[2] == AF.Copy: ins = e.activation(ap(a[0]), ap(a[1]), a[2])
-            else: ins = e.activation(ap(a[0]), ap(a[1]), a[2], bias=a[3], scale=ap(a[4]))
+            else: ins = e.activation(ap(a[0]), ap(a[1]), a[2], bias=ap(a[3]), scale=ap(a[4]))
         elif kind == "mm": ins = e.matmul(ap(a[0]), ap(a[1]), ap(a[2]), a[3], a[4])
         elif kind == "iota":
             if SCRATCH[a[0][0]][2] == I32: ins = e.iota(ap(a[0]), a[1], a[2], a[3])

@@ -6,86 +6,40 @@ BIG = float(1 << 21)
 OWN = 16384.0
 MAGIC = 12582912.0
 BLK = 64
-NSH = BLK // 16
-NC = BLK // 16
 TABW = 2560 + 256
-DIRECT = False
-NMS = False
-NFS = False
-NPS = False
-ENDS = [(("v", 512), ("s", 512), ("v", 512), ("s", 512))] * 2
-SPQ = "vsvv"
-HOLD = 0.0
-SPREAD = False
-CH = 64
-CN = 64
-PX2 = True
-CAST = (0,)
-SXV = False
-SWV = False
-ZV = False
 YH = 2064
-GA = (("v", 0, 16), ("s", 16, 64), ("s", 64, 96), ("s", 96, 128))
-GATHER = {1: GA, 2: GA, 3: GA}
-M1 = ((0, 64), (64, 128))
-MINS = {1: M1, 2: M1, 3: M1}
-BIAS = 1500.0
-PASSES = 120
-SPLIT = False
-SEED = 3
-NOISE = 500.0
-OFFS = False
-WAW = False
+VT = 200
+SN = 160
+GATHER = (("v", 0, 16), ("s", 16, 64), ("s", 64, 96), ("s", 96, 128))
+HALVES = ((0, 64), (64, 128))
+EST = {"cy": 0.83, "gam": 1.56, "sca": 3.8, "pe": 0.5, "same": 150.0, "other": 200.0, "rem": 1450.0, "rbw": 70.0, "rows": 300.0,
+       "dma": 1500.0, "lbw": 150.0}
+CASES = ({}, {"cy": 0.92, "pe": 0.55}, {"rem": 800.0, "rbw": 100.0}, {"rem": 1800.0, "rbw": 55.0},
+         {"gam": 1.9, "sca": 5.0, "cy": 1.0, "pe": 0.6})
+BIAS, PASSES, SEED, NOISE = 1500.0, 80, 2, 500.0
 INFO = []
-EST = {"cy": 0.83, "gam": 1.56, "sca": 3.8, "pe": 0.5, "same": 150.0, "other": 200.0, "rem": 2200.0, "rbw": 40.0, "dma": 2000.0}
-
-CASES = ({"cy": 0.9, "pe": 0.55, "rem": 2000.0}, {}, {"cy": 1.05, "pe": 0.62, "rem": 1600.0}, {"gam": 1.9, "sca": 5.0, "rem": 2800.0},
-         {"gam": 1.2, "sca": 2.5, "same": 190.0, "other": 250.0})
-PLAN = 2
 
 S_, P_ = "sbuf", "psum"
-F32, BF, I32, U16 = "float32", "bfloat16", "int32", "uint16"
-H = "float16"
-VT = 64
-SCRATCH = {
-    "tab0": (S_, [128, TABW], F32), "tab1": (S_, [128, TABW], F32), "pxs": (S_, [128, 4096], BF), "ces": (S_, [128, 1024], I32),
-    "v0s": (S_, [128, 16], I32), "wk": (S_, [128, 32], BF),
-    "Y": (S_, [128, 2 * YH], BF), "M": (S_, [128, 4096], BF),
-    "offn": (S_, [128, 256], U16), "nf": (S_, [128, 768], H),
-    "ci": (S_, [128, 256], I32), "cj": (S_, [128, 256], I32),
-    "bu": (S_, [128, 16 * (RO + 1)], U16), "bj": (S_, [128, 32], I32), "bs": (S_, [128, 256], I32),
-    "bt": (S_, [128, 16], I32), "kk": (S_, [128, 32], I32), "vf": (S_, [128, 16], F32),
-    "so": (S_, [128, 512], I32), "sc": (S_, [128, 256], F32), "ind": (S_, [128, 256], BF), "ko": (S_, [128, 256], F32),
-    "jj": (S_, [128, 32], I32), "mm": (S_, [128, 32], I32), "thr": (S_, [128, 32], F32),
-    "dn": (S_, [128, 16], F32), "qd": (S_, [128, 32], F32), "wf": (S_, [128, 16], H),
-    "noh": (S_, [128, 288], BF), "ex": (S_, [128, 256], H), "go": (S_, [128, 16], U16), "gs": (S_, [128, 16], U16),
-    "nm": (S_, [128, 256], H), "vt": (S_, [128, 4 * RO * VT], H),
-    "tf": (S_, [128, 512], H),
-    "s1": (S_, [128, 256], F32), "s2": (S_, [128, 512], F32), "E": (S_, [128, 256 * 8], BF),
-    "ku": (S_, [128, 16], U16), "wo": (S_, [128, 32], U16),
-    "xe": (S_, [128, 256], BF), "r2": (S_, [128, 256], H), "bc": (S_, [128, 256], BF), "tt": (S_, [128, 512], H),
-    "val": (S_, [128, 512], F32), "ey": (S_, [128, 256], BF), "z1": (S_, [128, 256], BF), "lz": (S_, [128, 256], BF),
-    "zm": (S_, [128, 256], F32), "at": (S_, [128, 256], F32),
-    "sx": (S_, [128, 256 * RO], BF), "lx": (S_, [128, 256 * RO], BF),
-    "sz": (S_, [128, 256 * (RO + 1)], BF), "lzz": (S_, [128, 256 * RO], BF),
-    "sna": (S_, [128, 48 * (RO + 1)], H),
-    "sf": (S_, [128, 256 * RO], BF), "lf": (S_, [128, 256 * RO], BF),
-    "sw": (S_, [128, 256 * RO], BF), "lw": (S_, [128, 256 * RO], BF),
-    "pi": (S_, [128, 8], I32), "pj": (S_, [128, 8], I32), "col": (S_, [128, 40], F32), "cr": (S_, [128, 4], U16), "wp": (S_, [128, 48], H),
-    "k16": (S_, [128, 128], F32), "ug": (S_, [128, 128], F32), "u4": (S_, [128, 128], F32), "cexp": (S_, [128, 8], U16), "cid": (S_, [128, 8], U16), "oh": (S_, [128, 256], BF),
-    "wm": (S_, [128, 128], F32), "cown": (S_, [128, 256], F32), "cmin": (S_, [128, 256], F32), "c01": (S_, [128, 128], F32),
-    "rows": (S_, [128, 1936], BF), "cend": (S_, [128, 8], U16), "bws": (S_, [128, 32], BF), "bwn": (S_, [128, 32], BF), "id5": (S_, [128, 128], H),
-    "qf": (S_, [128, 256], H), "fr": (S_, [128, 256], H), "exb": (S_, [128, 256], H), "sb": (S_, [128, 16 * RO], U16), "nhi": (S_, [128, 256], BF), "one": (S_, [128, 128], BF), "dum": (S_, [128, 256], F32), "s2h": (S_, [128, 256], H), "nob": (S_, [128, 256], BF),
-    "bo": (S_, [128, 128], F32), "idf": (S_, [128, 128], H), "idm2": (S_, [128, 128], H), "bh8": (S_, [128, 8], H),
-    "idb": (S_, [128, 1024], BF), "bf8": (S_, [128, 8], F32), "bb": (S_, [128, 96], BF),
-    "bx": (S_, [128, 384], BF), "bo4": (S_, [128, 256], BF), "bwu": (S_, [128, 256], BF), "bw8": (S_, [128, 16], BF),
-    "bkap": (S_, [128, 256], BF), "kps": (S_, [128, 48], F32), "selk": (S_, [128, 512], H), "selb": (S_, [128, 384], H),
-    "sef": (S_, [128, 256], H), "seh": (S_, [128, 256], BF), "w4": (S_, [128, 256], F32),
-}
+F32, BF, I32, U16, H = "float32", "bfloat16", "int32", "uint16", "float16"
+SCRATCH = {}
+for _dt, _bufs in (
+    (F32, {"tab0": TABW, "tab1": TABW, "vf": 16, "sc": 256, "thr": 32, "qd": 16, "s1": 256, "tmp": 384, "val": 512, "at": 256,
+           "col": 32, "k16": 128, "ug": 128, "u4": 128, "wm": 128, "cown": 128, "cmin": 128, "c01": 128, "dum": 128, "bo": 128,
+           "bf8": 8, "kps": 32, "w4": 256}),
+    (BF, {"pxs": 4096, "wk": 32, "Y": 2 * YH, "M": 4096, "ind": 256, "noh": 256, "oh": 256, "E": 1024, "xe": 256, "bc": 256, "ey": 256,
+          "z1": 256, "lz": 256, "nhi": 256, "sz": 512, "sx": 256 * RO, "lx": 256 * RO, "sf": 272 * RO, "lf": 272 * RO, "sw": 256 * RO,
+          "lw": 256 * RO, "rows": 1936, "one": 256, "idb": 768, "bb": 64, "bx": 384, "bo4": 128, "bwn": 32, "bkap": 512, "seh": 256}),
+    (H, {"nf": 768, "nm": 256, "ex": 256, "exb": 256, "qf": 256, "fr": 256, "vt": 4 * RO * VT, "sna": 2 * SN * (RO + 1), "tf": 512,
+         "s2": 256, "r2": 256, "tt": 512, "idf": 512, "bh8": 8, "selk": 512, "selb": 384, "sef": 256}),
+    (I32, {"ces": 1024, "v0s": 16, "bj": 32, "kk": 32, "so": 512, "jj": 16, "mm": 16, "pi": 8, "pj": 8}),
+    (U16, {"offn": 256, "bu": 16 * (RO + 1), "sb": 16 * RO, "go": 16, "gs": 16, "ku": 16, "wo": 32, "cexp": 8, "cid": 8}),
+):
+    for _n, _w in _bufs.items():
+        SCRATCH[_n] = (S_, [128, _w], _dt)
 for _h in range(2):
     for _n in ("X", "SC", "RA", "RB"):
         SCRATCH["%s%d" % (_n, _h)] = (P_, [128, 512], F32)
-MSG = ["b", "x", "z", "n", "f", "m", "w"]
+MSG = ["b", "x", "n", "f", "m", "w"]
 NDMA = 48
 SEMAPHORES = (["qv", "qs", "qp", "qg", "sent", "u"] + ["d%d" % i for i in range(NDMA)]
               + ["%s%d%d" % (m, h, t) for m in MSG for h in range(2) for t in range(RO)])
@@ -124,14 +78,9 @@ def plan():
     def scan(o, d0, d1, init, op0, op1): add("v", "scan", o, [d0, d1], (o, d0, d1, init, op0, op1))
     def mset(o, c): add("v", "mset", o, [], (o, c))
     def act(o, i, f, bias=0.0, scale=1.0): add("s", "act", o, [i, bias, scale], (o, i, f, bias, scale))
-    def mm(o, l, rh, st, sp):
-        if SPLIT and l[0] in ("Y", "M"):
-            m = l[1] + 64 * l[3]
-            l0 = r(l[0], l[1], m, l[3]); l1 = r(l[0], m, l[2], l[3])
-            o0 = o[:4] + (64, 0); o1 = o[:4] + (128, 64)
-            add("p", "mm", o0, [l0, rh], (o0, l0, rh, st, sp)); add("p", "mm", o1, [l1, rh], (o1, l1, rh, st, sp))
-        else:
-            add("p", "mm", o, [l, rh], (o, l, rh, st, sp))
+    def copy(q, o, i): return cp(o, i) if q == "v" else act(o, i, AF.Copy)
+    def times(o, i, w): act(o, i, AF.Identity, 0.0, w)
+    def mm(o, l, rh, st, sp): add("p", "mm", o, [l, rh], (o, l, rh, st, sp))
     def iota(o, pat, base, cm): add("g", "iota", o, [], (o, pat, base, cm))
     def load(q, o, src): ops.append([q, "load", (o, src), [], [o], cur[0]])
     def store(q, dst, i): ops.append([q, "store", (dst, i), [i], [], cur[0]])
@@ -142,24 +91,26 @@ def plan():
 
     def hf(name, h, base=0): return r(name, base + 128 * h, base + 128 * h + 128)
     def sm(name, h, base=0): return r(name, base + 8 * h, base + 8 * h + 8)
-    def s16(name, h): return r(name, 16 * h, 16 * h + 8)
     def ends(name, h, base=0): return r(name, base + 128 * h + 15, base + 128 * h + 128, 16)
     def c(i): return r("col", i, i + 1)
     def ps(name, h, a, b, step=1, p=128): return r("%s%d" % (name, h), a, b, step, p)
-    IDB, IDN, ID4, IDH, IDNH, IDG = [hf("idb", i) for i in range(6)]
-    IDF = r("idf", 0, 128); K16 = r("k16", 0, 128); UG = r("ug", 0, 128); U4 = r("u4", 0, 128); WM = r("wm", 0, 128); BO = r("bo", 0, 128)
-    WC, GC, P7, P3, W16P, G3, R6 = c(0), c(1), c(2), c(3), c(8), c(4), c(5)
-    COWN = r("cown", 0, 128); CMIN = r("cmin", 0, 128); CMAX = r("cmin", 128, 256); CEXP = r("cexp", 0, 8); NOB = r("nob", 0, 128)
-    def selb(i): return r("selb", 128 * i, 128 * i + 128, 1, 8)
-    def row(a, b): return r("rows", a, b, 1, 1)
-    ONE = r("one", 0, 128, 1, 1); QUART = row(384, 640)
-    def PLAS(h): return r("tab%d" % h, 0, 2048)
-    def CELL(h): return r("tab%d" % h, 2048, 2560)
-    def TAB(h): return r("tab%d" % h, 0, TABW)
+    def part(name, a, b, q): return r(name, a, b, 1, 64 * q + 64, 64 * q)
+    def row(a, n=128): return r("rows", a, a + n, 1, 1)
+    def PX(h): return r("pxs", 2048 * h, 2048 * h + 2048)
+    def CE(h): return r("ces", 512 * h, 512 * h + 512)
+    def tab(h, a, b): return r("tab%d" % h, a, b)
     def YW(h): return r("Y", YH * h, YH * h + YH)
     def vt(t, step, h, a, b): o = VT * (4 * t + 2 * (step - 2) + h); return r("vt", o + a, o + b)
+    def sna(t, h, a, b): o = SN * (2 * t + h); return r("sna", o + a, o + b)
+    IDB, IDN, ID4, IDH, IDNH, IDG = [hf("idb", i) for i in range(6)]
+    IDF, IDFN, IDF2, ID5 = [hf("idf", i) for i in range(4)]
+    K16, UG, U4, WM, BO, COWN, CMIN = [hf(n, 0) for n in ("k16", "ug", "u4", "wm", "bo", "cown", "cmin")]
+    WC, GC, P7, P3, G3, R6, W16P = c(0), c(1), c(2), c(3), c(4), c(5), c(8)
+    CEXP = r("cexp", 0, 8); BF8 = r("bf8", 0, 8); BH8 = r("bh8", 0, 8)
+    ONE = r("one", 0, 128, 1, 1); NONE = r("one", 128, 256, 1, 1)
+    K4096, KM16, K512, POS = 0, 128, 256, 1920
+    QUART, OFF3, MHALF, TIE, OFF1, C1024, M34, M23 = 512, 768, 1024, 1280, 1408, 1536, 1664, 1792
 
-    def part(name, a, b, q): return r(name, a, b, 1, 64 * q + 64, 64 * q)
     load("y", r("wk", 16, 17), ("wu", 0, 128, 0, 1))
     for h in range(2):
         cur[0] = h
@@ -170,187 +121,139 @@ def plan():
     cur[0] = None
     load("y", r("wk", 0, 16), ("kap", 0, 128, 0, 16))
     send("u", -1, r("wk", 24, 25), r("wk", 16, 17))
-    iota(r("pi", 0, 1), [[0, 1]], 0, 1)
-    iota(K16, [[0, 8], [1, 16]], 0, 0)
-    iota(UG, [[1, 8], [0, 16]], 0, 0)
-    iota(row(128, 256), [[0, 8], [1, 16]], -16, 0)
-    iota(row(768, 776), [[256, 8]], 0, 0)
     for h in range(2):
         cur[0] = h
-        send("z%d0" % h, 1, hf("lzz", h), hf("sz", h))
-        if h in CAST:
-            src = r("pxs", 2048 * h, 2048 * h + 2048)
-            ops.append(["g", "load", (PLAS(h), src), [src], [PLAS(h)], h])
+        act(sna(0, h, 32, SN), hf("sz", h), AF.Copy)
+        if h == 0: ops.append(["g", "load", (tab(h, 0, 2048), PX(h)), [PX(h)], [tab(h, 0, 2048)], h])
         else:
-            for j in range(4): act(r("tab%d" % h, 512 * j, 512 * j + 512), r("pxs", 2048 * h + 512 * j, 2048 * h + 512 * j + 512), AF.Copy)
+            for j in range(0, 2048, 512): act(tab(h, j, j + 512), r("pxs", 2048 * h + j, 2048 * h + j + 512), AF.Copy)
         cp(sm("bu", h), sm("v0s", h))
-        cp(CELL(h), r("ces", 512 * h, 512 * h + 512))
-        mset(r("tab%d" % h, 2560, 2568), 0.0)
+        cp(tab(h, 2048, 2560), CE(h))
+        mset(tab(h, 2560, 2568), 0.0)
     cur[0] = None
-    iota(row(0, 128), [[0, 8], [4096, 16]], 0, 0)
-    iota(U4, [[0, 2], [1, 4], [0, 16]], 0, 0)
-    mset(r("one", 0, 128), 1.0); mset(r("Y", 0, 16), 0.0); mset(r("Y", YH, YH + 16), 0.0)
-    ts(r("sna", 0, 48), r("k16", 0, 48), 0.0, A.mult); mset(r("rows", 384, 640), -0.25)
-    ts(r("pj", 0, 1), r("pi", 0, 1), 15, A.bitwise_and); ts(r("pj", 1, 2), r("pi", 0, 1), 4, A.logical_shift_right)
-    ts(r("pj", 2, 3), r("pi", 0, 1), 7, A.bitwise_and); ts(r("pj", 3, 4), r("pi", 0, 1), 3, A.logical_shift_right)
-    ts(r("pj", 4, 5), r("pi", 0, 1), 4, A.logical_shift_right, 3, A.bitwise_and)
-    ts(r("pj", 5, 6), r("pi", 0, 1), 6, A.logical_shift_right)
+
+    iota(r("pi", 0, 1), [[0, 1]], 0, 1)
+    iota(K16, [[0, 8], [1, 16]], 0, 0); iota(UG, [[1, 8], [0, 16]], 0, 0); iota(U4, [[0, 2], [1, 4], [0, 16]], 0, 0)
+    iota(row(POS, 8), [[256, 8]], 0, 0); iota(r("tmp", 0, 128), [[1, 128]], 2560 + 1024, 0)
+    k1 = r("k16", 0, 128, 1, 1)
+    times(row(K4096), k1, 4096.0); act(row(KM16), k1, AF.Identity, -16.0); times(row(K512), k1, 512.0); times(row(K512 + 128), k1, 2048.0)
+    mset(r("one", 0, 128), 1.0); mset(r("one", 128, 256), -1.0)
+    mset(r("Y", 0, 16), 0.0); mset(r("Y", YH, YH + 16), 0.0); mset(r("bj", 0, 32), 0)
+    for a, n, w in ((QUART, 256, -0.25), (OFF3, 128, -2032.0 * 8192), (OFF3 + 128, 128, -300.0 * 32768), (MHALF, 128, -0.5),
+                    (MHALF + 128, 128, 0.0), (TIE, 128, 1.0 / 1024), (OFF1, 128, 2040.0 * 8192), (C1024, 128, 1024.0),
+                    (M34, 128, MAGIC * 2048), (M23, 128, MAGIC)):
+        mset(r("rows", a, a + n), w)
+    for h in range(2): times(sna(0, h, 8, 16), r("k16", 0, 8), 0.0)
+    PI = r("pi", 0, 1)
+    ts(r("pj", 0, 1), PI, 15, A.bitwise_and); ts(r("pj", 1, 2), PI, 4, A.logical_shift_right)
+    ts(r("pj", 2, 3), PI, 7, A.bitwise_and); ts(r("pj", 3, 4), PI, 3, A.logical_shift_right)
+    ts(r("pj", 4, 5), PI, 4, A.logical_shift_right, 3, A.bitwise_and); ts(r("pj", 5, 6), PI, 6, A.logical_shift_right)
     cp(r("col", 0, 6), r("pj", 0, 6))
-    ts(W16P, WC, 16.0, A.mult, 16.0, A.add)
-    ts(BO, UG, GC, A.is_equal)
-    ts(WM, K16, WC, A.is_equal)
-    tt(IDB, BO, WM, A.mult)
-    ts(r("bf8", 0, 8), r("k16", 0, 8), GC, A.is_equal)
-    ts(r("bb", 0, 8), r("bf8", 0, 8), -16.0, A.mult)
-    cp(r("bb", 8, 16), r("bf8", 0, 8)); cp(r("bh8", 0, 8), r("bf8", 0, 8))
-    cp(CEXP, r("k16", 0, 8))
-    for n in ("bj", "jj", "mm", "qd"): mset(r(n, 0, 32), 0)
-    ts(c(12), WC, 8.0, A.is_ge); ts(c(13), P7, -8.0, A.add)
-    ts(r("col", 28, 32), r("k16", 0, 4), 2.0, A.mult, c(12), A.add)
-    ts(r("col", 32, 36), r("col", 28, 32), GC, A.is_equal, c(13), A.mult)
-    ts(r("cr", 0, 4), r("col", 32, 36), 8.0, A.add)
-    act(r("wp", 0, 48), r("wm", 0, 48), AF.Identity, 0.0, 0.0); act(r("wp", 16, 32), r("wm", 0, 16), AF.Copy)
-    if NFS: ts(r("cid", 0, 8), r("k16", 0, 8), 16.0, A.mult, WC, A.add)
-    ts(CMIN, K16, 0.0, A.is_equal, float(1 << 30), A.mult)
-    act(COWN, WM, AF.Identity, 0.0, -2 * OWN)
-    ts(r("c01", 0, 128), K16, 0.0, A.not_equal)
-    act(IDF, IDB, AF.Copy)
-    ts(r("bb", 16, 24), r("bf8", 0, 8), 65536.0, A.mult)
-    ts(r("bb", 32, 40), r("bf8", 0, 8), -131072.0, A.mult)
-    for i, w in enumerate((8192.0, 32768.0, -16384.0, -65536.0)):
-        act(r("bb", 48 + 8 * i, 56 + 8 * i), r("bf8", 0, 8), AF.Identity, 0.0, w)
-    for i, w in enumerate((65536.0, 8192.0, 32768.0)):
-        act(hf("bx", i), BO, AF.Identity, 0.0, w)
-    iota(row(784, 912), [[0, 8], [512, 16]], 0, 0); iota(row(912, 1040), [[0, 8], [2048, 16]], 0, 0)
-    mset(r("rows", 1040, 1168), -2032.0 * 8192); mset(r("rows", 1168, 1296), -300.0 * 32768)
+    act(W16P, WC, AF.Identity, 16.0, 16.0)
+    ts(BO, UG, GC, A.is_equal); ts(WM, K16, WC, A.is_equal); tt(IDB, BO, WM, A.mult)
+    ts(BF8, r("k16", 0, 8), GC, A.is_equal); act(BH8, BF8, AF.Copy)
+    cp(CEXP, r("k16", 0, 8)); cp(r("cid", 0, 1), WC)
+    ts(CMIN, K16, 0.0, A.is_equal, float(1 << 30), A.mult); act(hf("c01", 0), CMIN, AF.Identity, 1.0, -1.0 / (1 << 30))
+    times(COWN, WM, -2 * OWN)
+    for i, w in enumerate((-16.0, 65536.0, -8192.0, -131072.0, 8192.0, 32768.0, -16384.0, -65536.0)): times(sm("bb", i), BF8, w)
+    for i, w in enumerate((65536.0, 8192.0, 32768.0)): times(hf("bx", i), BO, w)
+    times(hf("bo4", 0), BO, 4096.0)
+    for ap, w in ((IDF, 1.0), (IDN, -1.0), (ID4, -4096.0), (IDH, 0.5), (IDNH, -0.5), (IDG, -BIG), (IDFN, -1.0), (IDF2, -2.0), (ID5, 512.0)):
+        times(ap, IDB, w)
     for q in range(2):
         ts(c(9 + q), R6, float(q), A.is_equal)
         ts(hf("w4", q), U4, G3, A.is_equal, c(9 + q), A.mult)
         tt(hf("sef", q), hf("w4", q), WM, A.mult)
-        act(hf("seh", q), hf("sef", q), AF.Identity, 0.0, 0.5)
+        times(hf("seh", q), hf("sef", q), 0.5)
     for h in range(2):
         cur[0] = h
+        kp = r("kps", 16 * h, 16 * h + 16)
         mm(ps("RB", h, 0, 16), hf("seh", h), r("wk", 0, 16), True, True)
-        act(r("kps", 24 * h, 24 * h + 16), ps("RB", h, 0, 16), AF.Identity, 0.0, 2.0)
+        times(kp, ps("RB", h, 0, 16), 2.0)
         mm(ps("RB", h, 16, 17), hf("seh", h), r("wk", 24, 25), True, True)
-        for j in range(2): ts(sm("bwn", j, 16 * h), r("bf8", 0, 8), ps("RB", h, 16, 17), A.mult, 1.0 / 256, A.mult)
-        for g8 in range(8):
-            add("s", "act", r("bkap", 128 * h + 16 * g8, 128 * h + 16 * g8 + 16), [r("kps", 24 * h, 24 * h + 16), r("bf8", g8, g8 + 1)],
-                (r("bkap", 128 * h + 16 * g8, 128 * h + 16 * g8 + 16), r("kps", 24 * h, 24 * h + 16), AF.Identity, 0.0, r("bf8", g8, g8 + 1)))
+        for j in range(2): ts(sm("bwn", j, 16 * h), BF8, ps("RB", h, 16, 17), A.mult, 1.0 / 256, A.mult)
+        for g8 in range(8): times(r("bkap", 128 * h + 16 * g8, 128 * h + 16 * g8 + 16), kp, r("bf8", g8, g8 + 1))
+        times(hf("bkap", h, 256), hf("bkap", h), -1.0)
     cur[0] = None
-    mset(r("rows", 1296, 1424), -0.5); mset(r("rows", 1424, 1552), 0.0); mset(r("rows", 1552, 1680), 1.0 / 1024)
-    mset(r("rows", 1680, 1808), 2040.0 * 8192)
-    act(r("bb", 24, 32), r("bf8", 0, 8), AF.Identity, 0.0, -8192.0); act(r("id5", 0, 128), IDB, AF.Identity, 0.0, 512.0)
-    if DIRECT:
-        iota(r("s2", 0, 256), [[1, 256]], 2560, 0)
-        for q in range(2): tt(hf("dum", q), hf("s2", q), WM, A.mult)
-    else:
-        iota(r("s2", 0, 128), [[1, 128]], 2560 + 1024, 0)
-        ts(c(11), R6, 128.0, A.mult)
-        ts(r("s2", 128, 256), r("s2", 0, 128), c(11), A.add)
-        tt(r("s2", 256, 384), r("s2", 128, 256), WM, A.mult)
-        act(hf("dum", 0), r("s2", 256, 384), AF.Identity, -2048.0)
+    times(c(11), R6, 128.0)
+    act(r("tmp", 128, 256), r("tmp", 0, 128), AF.Identity, c(11))
+    tt(r("tmp", 256, 384), r("tmp", 128, 256), WM, A.mult)
+    act(hf("dum", 0), r("tmp", 256, 384), AF.Identity, -2048.0)
     ts(c(16), P3, 0.0, A.is_equal); ts(c(17), P3, 3.0, A.is_equal)
-    ts(c(18), P3, 0.0, A.is_equal, 2047.0, A.mult); ts(c(19), P3, 4.0, A.is_equal, 4096.0, A.mult)
-    ts(c(20), P3, 3.0, A.is_lt, c(18), A.add); tt(c(25), c(20), c(19), A.add)
-    ts(r("selk", 0, 128), UG, P7, A.is_equal, c(25), A.mult)
+    times(c(18), c(16), 2047.0); ts(c(19), P3, 4.0, A.is_equal, 4096.0, A.mult)
+    ts(c(20), P3, 3.0, A.is_lt, c(18), A.add); act(c(25), c(20), AF.Identity, c(19))
+    ts(hf("selk", 0), UG, P7, A.is_equal, c(25), A.mult)
+    act(c(21), c(16), AF.Identity, c(17), 4096.0)
+    ts(hf("selk", 1), UG, P7, A.is_equal, c(21), A.mult)
     ts(c(22), GC, 3.0, A.is_equal)
-    for j in range(4): act(hf("tf", j), WM, AF.Identity, 0.0, c(22))
+    for j in range(4): times(hf("tf", j), WM, c(22))
     act(hf("s1", 0), WM, AF.Identity, -OWN, OWN); act(hf("s1", 1), WM, AF.Identity, OWN - 1024.0, -OWN)
     for j in range(2):
-        act(hf("val", j), hf("s1", j), AF.Identity, 0.0, c(22))
+        times(hf("val", j), hf("s1", j), c(22))
         tt(hf("selk", 2 + j), hf("val", j), hf("selk", 0), A.add)
-    act(r("bo4", 0, 128), BO, AF.Identity, 0.0, 4096.0)
-    ts(c(21), c(16), 4096.0, A.mult, c(17), A.add)
-    ts(r("selk", 128, 256), UG, P7, A.is_equal, c(21), A.mult)
-    for i, w in enumerate((-256.0, 4096.0, 0.5)):
-        ts(r("selb", 128 * i, 128 * i + 128), UG, P7, A.is_equal, w, A.mult)
-    for ap, w in ((IDN, -1.0), (ID4, -4096.0), (IDH, 0.5), (IDNH, -0.5), (IDG, -BIG), (r("idm2", 0, 128), -2.0)):
-        act(ap, IDB, AF.Identity, 0.0, w)
+    ts(hf("selb", 0), UG, P7, A.is_equal, -256.0, A.mult)
+    times(hf("selb", 1), hf("selb", 0), -16.0); times(hf("selb", 2), hf("selb", 0), -1.0 / 512)
 
     def to_psum(h, x):
         mm(ps("X", h, 0, 128), IDB, x, True, True)
 
+    def names(step, h, win, cells):
+        for a, b in HALVES:
+            cp(r("offn", 128 * h + a, 128 * h + b), ind(win, r(cells[0], cells[1] + a // 16, cells[1] + b // 16)))
+        cp(hf("nf", h, 256 * (step - 1)), hf("offn", h))
+
     def scores(step, h, win, x):
-        nf = hf("nf", h, 256 * (step - 1)); y0 = YH * h + 16
-        if step == 2:
-            mm(ps("SC", h, 0, 128), ONE, row(0, 128), True, False)
-            mm(ps("SC", h, 0, 128), x, r("bx", 0, 128), False, False)
-            mm(ps("RB", h, 128, 256), ONE, row(128, 256), True, False);
-        elif step == 1:
-            mm(ps("SC", h, 0, 128), ONE, row(784, 912), True, False); mm(ps("SC", h, 0, 128), ONE, row(1680, 1808), False, False)
-            mm(ps("RA", h, 0, 256), ONE, row(1296, 1552), True, False); mm(ps("RA", h, 0, 128), ONE, row(1552, 1680), False, False)
+        nf = hf("nf", h, 256 * (step - 1)); y0 = YH * h + 16; S0 = ps("SC", h, 0, 128); w = 256 if step == 3 else 128
+        def Yk(k): return r("Y", y0 + k, y0 + 2048, 16)
+        def Mk(k): return hf("M", k, 2048 * h)
+        if step == 1:
+            mm(S0, ONE, row(K512), True, False); mm(S0, ONE, row(OFF1), False, False)
+            mm(ps("RA", h, 0, 256), ONE, row(MHALF, 256), True, False); mm(ps("RA", h, 0, 128), ONE, row(TIE), False, False)
+        elif step == 2:
+            mm(S0, ONE, row(K4096), True, False); mm(S0, x, hf("bx", 0), False, False)
+            mm(ps("RB", h, 128, 256), ONE, row(KM16), True, False)
         else:
-            mm(ps("SC", h, 0, 256), ONE, row(784, 1040), True, False); mm(ps("SC", h, 0, 256), ONE, row(1040, 1296), False, False)
+            mm(ps("SC", h, 0, 256), ONE, row(K512, 256), True, False); mm(ps("SC", h, 0, 256), ONE, row(OFF3, 256), False, False)
             mm(ps("SC", h, 0, 256), x, r("bx", 128, 384), False, False)
-            mm(ps("SC", h, 0, 128), hf("nhi", h), IDN, False, False)
-        w = 256 if step == 3 else 128
-        for q, a, b in GATHER[step]:
-            o = r("Y", y0 + 16 * a, y0 + 16 * b); i = ind(win, r("offn", 128 * h + a, 128 * h + b))
-            if q == "v": cp(o, i)
-            else: act(o, i, AF.Copy)
-        if step > 1:
-            for k in range(16):
-                mm(ps("SC", h, k, w, 16), r("Y", y0 + k, y0 + 2048, 16), r("bb", 16, 24) if step == 2 else r("bb", 48, 64), False, False)
-        else:
-            for k in range(16):
-                mm(ps("RA", h, k, 256, 16), r("Y", y0 + k, y0 + 2048, 16), r("bwn", 16 * h, 16 * h + 16), False, k == 15)
+            mm(S0, hf("nhi", h), IDN, False, False)
+        for q, a, b in GATHER:
+            copy(q, r("Y", y0 + 16 * a, y0 + 16 * b), ind(win, r("offn", 128 * h + a, 128 * h + b)))
+        if step == 1:
+            for k in range(16): mm(ps("RA", h, k, 256, 16), Yk(k), r("bwn", 16 * h, 16 * h + 16), False, k == 15)
             ts(hf("qf", h), ps("RA", h, 0, 128), MAGIC, A.add, -MAGIC, A.add)
             tt(hf("fr", h), ps("RA", h, 128, 256), hf("qf", h), A.subtract)
-        for a, b in MINS[step]:
+        else:
+            for k in range(16): mm(ps("SC", h, k, w, 16), Yk(k), sm("bb", 1) if step == 2 else r("bb", 32, 48), False, False)
+        for a, b in HALVES:
             for k in range(16):
                 m0 = 2048 * h + 128 * k
                 tt(r("M", m0 + a, m0 + b), r("Y", y0 + 16 * a + k, y0 + 16 * b, 16), ps("X", h, a, b), A.min)
-        for k in range(16):
-            mm(ps("SC", h, k, w, 16), r("M", 2048 * h + 128 * k, 2048 * h + 128 * k + 128),
-               (r("bb", 24, 32), r("bb", 32, 40), r("bb", 64, 80))[step - 1], False, False)
-        if step == 1: mm(ps("SC", h, 0, 128), r("id5", 0, 128), hf("fr", h), False, True)
-        if step == 3:
-            mm(ps("SC", h, 0, 128), nf, IDF, False, False); mm(ps("SC", h, 128, 256), nf, IDF, False, True)
-        if step == 2:
-            mm(ps("SC", h, 0, 128), nf, IDF, False, True)
-            for k in range(16):
-                mm(ps("RB", h, 128 + k, 256, 16), r("M", 2048 * h + 128 * k, 2048 * h + 128 * k + 128), r("bb", 0, 8), False, False)
+        for k in range(16): mm(ps("SC", h, k, w, 16), Mk(k), (sm("bb", 2), sm("bb", 3), r("bb", 48, 64))[step - 1], False, False)
+        if step == 1:
+            mm(S0, ID5, hf("fr", h), False, True)
+        elif step == 2:
+            mm(S0, nf, IDF, False, True)
+            for k in range(16): mm(ps("RB", h, 128 + k, 256, 16), Mk(k), sm("bb", 0), False, False)
+        else:
+            mm(S0, nf, IDF, False, False); mm(ps("SC", h, 128, 256), nf, IDF, False, True)
 
-    def names(step, h, win, cells):
-        act(hf("nf", h, 256 * (step - 1)), ind(win, cells), AF.Copy)
-        for a in range(0, 128, CN):
-            cp(r("offn", 128 * h + a, 128 * h + a + CN), ind(win, r(cells[0], cells[1] + a // 16, cells[1] + (a + CN) // 16)))
-
-    def pick(o, h, v):
-        if v: cp(o, ind(YW(h), sm("go", h)))
-        else: act(o, ind(YW(h), sm("go", h)), AF.Copy)
-
-    def spread(src, dst, h, q):
-        if not SPREAD: return tt(hf(dst, h), ind(s16(src, h), CEXP), WM, A.mult)
-        o = r(dst, 64 * h, 64 * h + 64); i = ind(r(src, 16 * h, 16 * h + 16), r("cr", 0, 4))
-        if q == "v": cp(o, i)
-        else: act(o, i, AF.Copy)
-
-    def turn(src, h, bank, a, start):
-        if not SPREAD: return mm(ps(bank, h, a, a + 8), hf(src, h), r("bh8", 0, 8), start, True)
-        for g8 in range(8):
-            p0 = 32 * (g8 // 2); w0 = 16 * (1 - g8 % 2)
-            mm(r("%s%d" % (bank, h), a, a + 8, 1, p0 + 32, p0), r("wp", w0, w0 + 32), r(src, 64 * h + g8, 64 * h + 64, 8),
-               start and g8 % 2 == 0, g8 % 2 == 1)
-
-    def to_list(src, h, slots, q):
-        spread(src, "ex", h, q)
-        mm(ps("RB", h, 0, 8), ONE, row(768, 776), True, False)
-        turn("ex", h, "RB", 0, False)
-        if slots: turn("ex", h, "RB", 8, True)
-        ts(sm("go", h), ps("RB", h, 0, 8), W16P, A.add)
-        if slots: cp(sm("gs", h), ps("RB", h, 8, 16))
+    def to_list(src, h, slots):
+        tt(hf("ex", h), ind(sm(src, h), CEXP), WM, A.mult)
+        mm(ps("SC", h, 400, 408), ONE, row(POS, 8), True, False)
+        mm(ps("SC", h, 400, 408), hf("ex", h), BH8, False, True)
+        if slots: mm(ps("SC", h, 408, 416), hf("ex", h), BH8, True, True)
+        ts(sm("go", h), ps("SC", h, 400, 408), W16P, A.add)
+        if slots: cp(sm("gs", h), ps("SC", h, 408, 416))
 
     def pick_name(step, h, dst):
-        if NMS:
-            act(hf("oh", h), ind(r("wm", 0, 16), sm("gs", h)), AF.Identity, 0.0, -1.0)
-            mm(ps("RB", h, 384, 512), ID4, hf("oh", h), True, False)
-            mm(ps("RB", h, 384, 512), IDF, hf("nf", h, 256 * (step - 1)), False, True)
-            act(hf("nm", h), ps("RB", h, 384, 512), AF.Relu, -4096.0)
+        nf = hf("nf", h, 256 * (step - 1)); slot = ind(r("wm", 0, 16), sm("gs", h))
+        if step == 1:
+            tt(hf("nm", h), slot, nf, A.mult)
         else:
-            tt(hf("nm", h), ind(r("wm", 0, 16), sm("gs", h)), hf("nf", h, 256 * (step - 1)), A.mult)
-        mm(ps("RB", h, 16, 24), hf("nm", h), r("bh8", 0, 8), True, True)
+            times(hf("oh", h), slot, -1.0)
+            mm(ps("RB", h, 384, 512), ID4, hf("oh", h), True, False); mm(ps("RB", h, 384, 512), IDF, nf, False, True)
+            act(hf("nm", h), ps("RB", h, 384, 512), AF.Relu, -4096.0)
+        mm(ps("RB", h, 16, 24), hf("nm", h), BH8, True, True)
         act(dst, ps("RB", h, 16, 24), AF.Copy)
 
     def rows(o, sel, i, j, start, stop):
@@ -358,9 +261,8 @@ def plan():
         mm(o, r(sel, 128 * i, 128 * i + 128, 1, K), r("tf", 128 * j, 128 * j + 128, 1, K), start, stop)
 
     def write(t, step, h, x, between=None):
-        j = 2 * (step - 2) + h
+        j = 2 * (step - 2) + h; K = 32 if step == 2 else 40; NC = BLK // 16
         KM = ps("X", h, 0, 128); KR = ps("RA", h, 128, 256); P = ps("SC", h, 256, 384)
-        K = 32 if step == 2 else 40
         mm(ps("RA", h, 0, 128, 1, K), vt(t, step, h, 16, 16 + K), IDF, True, True)
         act(r("tf", 128 * j, 128 * j + 128, 1, K), ps("RA", h, 0, 128, 1, K), AF.Copy)
         rows(KM, "selk", 2, j, True, True)
@@ -377,149 +279,127 @@ def plan():
         act(hf("r2", h), ps("RB", h, 384, 512), AF.Relu, -4096.0)
         if between: between()
         rows(P, "selk", 3, j, True, False)
-        T_ = hf("tt", h, 256 * (step - 2))
+        T_ = hf("tt", j)
         ts(sm("ku", h), ends("s1", h), 2560.0, A.min)
-        tt(T_, ind(r("tab%d" % h, 0, 2568), sm("ku", h)), hf("bc", h), A.mult)
-        for i in range(NSH):
+        tt(T_, ind(tab(h, 0, 2568), sm("ku", h)), hf("bc", h), A.mult)
+        for i in range(NC):
             s = 1 + 16 * i; e = 256 * i + 128 * h
             tt(r("E", e + s, e + 128), r("s1", 128 * h, 128 * h + 128 - s), ps("RA", h, 128 + s, 256), A.is_equal)
-            if DIRECT:
-                for q in range(2):
-                    mm(ps("SC", h, 256 + 128 * q + s, 384 + 128 * q), hf("bo4", q), r("E", e + s, e + 128), False, i == NSH - 1 and q == 1)
-            else:
-                mm(ps("SC", h, 256 + s, 384), r("bo4", 0, 128), r("E", e + s, e + 128), False, i == NSH - 1)
-        mm(ps("X", h, 256, 512), ONE, QUART, True, False)
+            mm(ps("SC", h, 256 + s, 384), hf("bo4", 0), r("E", e + s, e + 128), False, i == NC - 1)
+        def new(q): return ps("X", h, 256 + 128 * q, 384 + 128 * q)
+        mm(ps("X", h, 256, 512), ONE, row(QUART, 256), True, False)
         for q in range(2):
-            o = ps("X", h, 256 + 128 * q, 384 + 128 * q)
-            mm(o, hf("seh", q), hf("xe", h), False, False); mm(o, hf("sef", q), hf("r2", h), False, False)
-        for q in (1, 0): mm(ps("X", h, 256 + 128 * q, 384 + 128 * q), hf("sef", q), T_, False, q == 0)
-        for q in (1, 0): act(hf("val", q, 256 * h), ps("X", h, 256 + 128 * q, 384 + 128 * q), AF.Identity, MAGIC)
-        if DIRECT:
-            scan(r("s2", 256 * h, 256 * h + 256), r("dum", 0, 256), ps("SC", h, 256, 512), 0.0, A.max, A.min)
-            cp(r("wo", 16 * h, 16 * h + 16), r("s2", 256 * h + 15, 256 * h + 256, 16))
-        else:
-            scan(hf("s2h", h), r("dum", 0, 128), ps("SC", h, 256, 384), -2048.0, A.max, A.min)
-            for q in range(2): mm(ps("SC", h, 384 + 8 * q, 392 + 8 * q), hf("sef", q), ends("s2h", h), True, True)
-            ts(r("wo", 16 * h, 16 * h + 16), ps("SC", h, 384, 400), 1024.0, A.add)
+            mm(new(q), hf("seh", q), hf("xe", h), False, False); mm(new(q), hf("sef", q), hf("r2", h), False, False)
+        for q in (1, 0): mm(new(q), hf("sef", q), T_, False, q == 0)
+        for q in (1, 0): act(hf("val", q, 256 * h), new(q), AF.Identity, MAGIC)
+        scan(hf("s2", h), hf("dum", 0), P, -2048.0, A.max, A.min)
+        for q in range(2): mm(ps("SC", h, 384 + 8 * q, 392 + 8 * q), hf("sef", q), ends("s2", h), True, True)
+        ts(r("wo", 16 * h, 16 * h + 16), ps("SC", h, 384, 400), 1024.0, A.add)
         for b in range(256 // BLK - 1, -1, -1):
-            ts(ind(TAB(h), r("wo", 16 * h + NC * b, 16 * h + NC * b + NC)), r("val", 256 * h + BLK * b, 256 * h + BLK * b + BLK),
-               1.0, A.mult, -MAGIC, A.add)
+            ts(ind(tab(h, 0, TABW), r("wo", 16 * h + NC * b, 16 * h + NC * b + NC)),
+               r("val", 256 * h + BLK * b, 256 * h + BLK * b + BLK), 1.0, A.mult, -MAGIC, A.add)
 
     def stream(h):
         to_psum(h, hf("sz", h))
+        bj = r("bj", 16 * h, 16 * h + 8); kk = r("kk", 16 * h, 16 * h + 16); k0 = sm("kk", 2 * h); k1 = sm("kk", 2 * h + 1)
         for t in range(RO):
-            o = 256 * t; na = 48 * t + 24 * h
-            names(1, h, r("ces", 512 * h, 512 * h + 512) if t == 0 else CELL(h), sm("bu", h, 16 * t))
-            scores(1, h, r("pxs", 2048 * h, 2048 * h + 2048) if t == 0 else PLAS(h), None)
+            o = 256 * t; cells = CE(h) if t == 0 else tab(h, 2048, 2560); plas = PX(h) if t == 0 else tab(h, 0, 2048)
+            names(1, h, cells, sm("bu", h, 16 * t))
+            scores(1, h, plas, None)
             scan(hf("so", h), CMIN, ps("SC", h, 0, 128), 0.0, A.add, A.min)
-            ts(s16("bj", h), ends("so", h), 511, A.bitwise_and)
-            spread("bj", "exb", h, SPQ[0])
-            turn("exb", h, "RA", 256, True)
+            ts(bj, ends("so", h), 511, A.bitwise_and)
+            tt(hf("exb", h), ind(bj, CEXP), WM, A.mult)
+            mm(ps("RA", h, 256, 264), hf("exb", h), BH8, True, True)
             cp(sm("sb", h, 16 * t), ps("RA", h, 256, 264))
             BU = sm("bu", h, 16 * t + 16)
             send("b%d%d" % (h, t), 1, BU, sm("sb", h, 16 * t))
-            ts(s16("jj", h), ends("so", h), 9, A.arith_shift_right, 15, A.bitwise_and)
-            to_list("jj", h, True, SPQ[1])
-            pick(hf("sx", h, o), h, SXV)
+            ts(sm("jj", h), ends("so", h), 9, A.arith_shift_right, 15, A.bitwise_and)
+            to_list("jj", h, True)
+            act(hf("sx", h, o), ind(YW(h), sm("go", h)), AF.Copy)
             send("x%d%d" % (h, t), 1, hf("lx", h, o), hf("sx", h, o))
-            cp(r("sna", na + 16, na + 24), s16("bj", h))
-            pick_name(1, h, r("sna", na, na + 8))
-            send("n%d%d" % (h, t), 1, vt(t, 2, h, 40, 64), r("sna", na, na + 24))
-            x = hf("lx", h, o)
+            act(sna(t, h, 16, 32), ind(r("bj", 16 * h, 16 * h + 16), r("cid", 0, 1)), AF.Copy)
+            pick_name(1, h, sna(t, h, 0, 8))
+            send("n%d%d" % (h, t), 1, vt(t, 2, h, 40, 40 + SN), sna(t, h, 0, SN))
+            x = hf("lx", h, o); e = vt(t, 2, h, 8, 16); phi = vt(t, 2, h, 16, 24); a = vt(t, 2, h, 48, 56)
             to_psum(h, x)
-            names(2, h, r("ces", 512 * h, 512 * h + 512) if t == 0 and PX2 else CELL(h), BU)
-            act(sm("thr", h, 16), vt(t, 2, h, 48, 56), AF.Abs, -2.0, 2.0)
+            names(2, h, cells, BU)
+            act(sm("thr", h, 16), a, AF.Abs, -2.0, 2.0)
             act(sm("thr", h), sm("thr", h, 16), AF.Identity, -10.0, -1.0)
-            scores(2, h, r("pxs", 2048 * h, 2048 * h + 2048) if t == 0 and PX2 else PLAS(h), x)
+            scores(2, h, plas, x)
             scan(hf("so", h), CMIN, ps("SC", h, 0, 128), 0.0, A.add, A.min)
             act(hf("ind", h), ps("SC", h, 0, 128), AF.Sign, 255.985, -1.0 / 65536)
-            ts(s16("jj", h), ends("so", h), 12, A.arith_shift_right, 15, A.bitwise_and)
-            tt(hf("noh", h), ind(s16("jj", h), CEXP), K16, A.not_equal)
+            ts(sm("jj", h), ends("so", h), 12, A.arith_shift_right, 15, A.bitwise_and)
+            tt(hf("noh", h), ind(sm("jj", h), CEXP), K16, A.not_equal)
             mm(ps("RB", h, 128, 256), IDG, hf("noh", h), False, True)
-            ts(r("kk", 16 * h, 16 * h + 8), ends("so", h), 2047, A.bitwise_and)
-            scan(hf("sc", h), r("c01", 0, 128), hf("ind", h), 0.0, A.mult, A.add)
-            tt(vt(t, 2, h, 16, 24), ends("sc", h), sm("thr", h), A.is_lt)
-            e = vt(t, 2, h, 8, 16)
+            ts(k0, ends("so", h), 2047, A.bitwise_and)
+            scan(hf("sc", h), hf("c01", 0), hf("ind", h), 0.0, A.mult, A.add)
+            tt(phi, ends("sc", h), sm("thr", h), A.is_lt)
             tt(e, ends("sc", h), sm("thr", h), A.is_ge)
-            tt(vt(t, 2, h, 24, 32), r("kk", 16 * h, 16 * h + 8), e, A.mult)
-            tt(vt(t, 2, h, 32, 40), vt(t, 2, h, 56, 64), vt(t, 2, h, 16, 24), A.mult)
+            tt(vt(t, 2, h, 24, 32), k0, e, A.mult)
+            tt(vt(t, 2, h, 32, 40), vt(t, 2, h, 56, 64), phi, A.mult)
             scan(hf("so", h, 256), CMIN, ps("RB", h, 128, 256), 0.0, A.add, A.min)
-            ts(s16("mm", h), ends("so", h, 256), 15, A.bitwise_and)
-            to_list("mm", h, True, SPQ[2])
-            tt(hf("sf", h, o), ind(YW(h), sm("go", h)), x, A.max)
-            send("f%d%d" % (h, t), 1, hf("lf", h, o), hf("sf", h, o))
-            tt(r("sna", na + 56, na + 64), vt(t, 2, h, 48, 56), e, A.add)
+            ts(sm("mm", h), ends("so", h, 256), 15, A.bitwise_and)
+            to_list("mm", h, True)
+            of = 136 * (2 * t + h)
+            tt(r("sf", of, of + 128), ind(YW(h), sm("go", h)), x, A.max)
+            times(r("sf", of + 128, of + 136), e, -8192.0)
+            send("f%d%d" % (h, t), 1, r("lf", of, of + 136), r("sf", of, of + 136))
 
             def name_m():
+                mm(ps("RB", h, 24, 32), IDF, a, True, False); mm(ps("RB", h, 24, 32), IDF, e, False, True)
+                act(sna(t + 1, h, 8, 16), ps("RB", h, 24, 32), AF.Copy)
                 pick_name(2, h, vt(t, 2, h, 0, 8))
                 send("m%d%d" % (h, t), 1, vt(t, 3, h, 40, 56), vt(t, 2, h, 0, 16))
             write(t, 2, h, x, name_m)
             if t == RO - 1:
                 cp(sm("vf", h), BU)
-                mm(ps("RB", h, 0, 128, 1, 8), r("sna", na + 56, na + 64), IDF, True, True)
+                mm(ps("RB", h, 0, 128, 1, 8), sna(RO, h, 8, 16), IDF, True, True)
                 act(r("at", 128 * h, 128 * h + 128, 1, 8), ps("RB", h, 0, 128, 1, 8), AF.Copy)
                 for q in range(2):
-                    store("y", ("yv", 64 * h, 64 * h + 64, 8 * q, 8 * q + 8), r("vf", 8 * h, 8 * h + 8, 1, 64 * q + 64, 64 * q))
+                    store("y", ("yv", 64 * h, 64 * h + 64, 8 * q, 8 * q + 8), part("vf", 8 * h, 8 * h + 8, q))
                     store("y", ("ya", 4 * h, 4 * h + 4, 128 * q, 128 * q + 128), r("at", 128 * h, 128 * h + 128, 1, 4 * q + 4, 4 * q))
-            f = hf("lf", h, o); bank = ps("RA", h, 256, 384)
-            mm(bank, hf("bkap", h), f, True, True)
+            f = r("lf", of, of + 128); bank = ps("RA", h, 256, 384)
+            mm(bank, ONE, row(C1024), True, False); mm(bank, ONE, row(MHALF), False, False)
+            mm(bank, hf("bkap", h, 256), f, False, False)
+            mm(bank, ONE, row(M34), False, False); mm(bank, NONE, row(M34), False, False)
+            mm(bank, hf("bkap", h), f, False, True)
             to_psum(h, f)
-            for a in range(0, 128, CH):
-                def pc(n): return r(n, 128 * h + a, 128 * h + a + CH)
-                cp(pc("ci"), ps("RA", h, 256 + a, 256 + a + CH))
-                ts(pc("cj"), pc("ci"), 2047, A.bitwise_and)
-                cp(pc("offn"), pc("cj"))
-            if NFS: act(hf("nf", h, 512), ind(hf("cj", h), r("cid", 0, 8)), AF.Copy)
-            else: cp(hf("nf", h, 512), hf("cj", h))
-            act(hf("nhi", h), hf("nf", h, 512), AF.Identity, 98304.0 - 255.5)
-            z = hf("lzz", h, o)
-            mm(ps("RB", h, 0, 128), r("idm2", 0, 128), hf("tt", h), True, False); rows(ps("RB", h, 0, 128), "selb", 1, h, False, True)
-            mm(ps("RB", h, 128, 256), IDN, z, True, False); rows(ps("RB", h, 128, 256), "selb", 0, h, False, True)
+            for p, q in HALVES: cp(r("offn", 128 * h + p, 128 * h + q), ps("RA", h, 256 + p, 256 + q))
+            act(hf("nf", h, 512), bank, AF.Copy)
+            act(hf("nhi", h), bank, AF.Identity, 98304.0 - 255.5)
+            z = vt(t, 2, h, 72, 200)
+            mm(ps("RB", h, 0, 128), IDF2, hf("tt", h), True, False); rows(ps("RB", h, 0, 128), "selb", 1, h, False, True)
+            mm(ps("RB", h, 128, 256), IDFN, z, True, False); rows(ps("RB", h, 128, 256), "selb", 0, h, False, True)
             act(hf("ey", h), ps("RB", h, 0, 128), AF.Relu, 0.0, -1.0)
             act(hf("lz", h), ps("RB", h, 128, 256), AF.Relu, -256.0, -1.0)
-            mm(ps("RB", h, 256, 384), IDB, z, True, False); mm(ps("RB", h, 256, 384), IDN, hf("ey", h), False, True)
+            mm(ps("RB", h, 256, 384), IDF, z, True, False); mm(ps("RB", h, 256, 384), IDN, hf("ey", h), False, True)
             act(hf("z1", h), ps("RB", h, 256, 384), AF.Abs)
-            act(sm("dn", h), vt(t, 3, h, 48, 56), AF.Identity, 0.0, -8192.0)
-            scores(3, h, PLAS(h), f)
-            scan(hf("so", h), CMIN, ps("SC", h, 0, 128), 0.0, A.add, A.min)
-            scan(hf("so", h, 256), CMIN, ps("SC", h, 128, 256), 0.0, A.add, A.min)
-            ts(s16("jj", h), ends("so", h), 9, A.arith_shift_right, 15, A.bitwise_and)
-            tt(s16("qd", h), s16("jj", h), sm("dn", h), A.add)
-            to_list("qd", h, False, SPQ[3])
-            pick(hf("sw", h, o), h, SWV)
+            scores(3, h, tab(h, 0, 2048), f)
+            for q in range(2): scan(hf("so", h, 256 * q), CMIN, ps("SC", h, 128 * q, 128 * q + 128), 0.0, A.add, A.min)
+            ts(sm("jj", h), ends("so", h), 9, A.arith_shift_right, 15, A.bitwise_and)
+            tt(sm("qd", h), sm("jj", h), r("lf", of + 128, of + 136), A.add)
+            to_list("qd", h, False)
+            act(hf("sw", h, o), ind(YW(h), sm("go", h)), AF.Copy)
             send("w%d%d" % (h, t), -1, hf("lw", h, o), hf("sw", h, o))
-            tt(hf("noh", h), ind(s16("jj", h), CEXP), K16, A.not_equal)
+            tt(hf("noh", h), ind(sm("jj", h), CEXP), K16, A.not_equal)
             ts(vt(t, 3, h, 16, 24), ends("so", h), float((600 - 2044) * 8192), A.is_ge)
-            if NPS: act(vt(t, 3, h, 8, 16), vt(t, 3, h, 16, 24), AF.Identity, 1.0, -1.0)
-            else: ts(vt(t, 3, h, 8, 16), ends("so", h), float((600 - 2044) * 8192), A.is_lt)
-            ts(r("kk", 16 * h, 16 * h + 8), ends("so", h, 256), 2047, A.bitwise_and)
-            ts(r("kk", 16 * h + 8, 16 * h + 16), ends("so", h), 511, A.bitwise_and)
-            tt(vt(t, 3, h, 24, 40), r("kk", 16 * h, 16 * h + 16), vt(t, 3, h, 8, 24), A.mult)
+            ts(vt(t, 3, h, 8, 16), ends("so", h), float((600 - 2044) * 8192), A.is_lt)
+            ts(k0, ends("so", h, 256), 2047, A.bitwise_and)
+            ts(k1, ends("so", h), 511, A.bitwise_and)
+            tt(vt(t, 3, h, 24, 40), kk, vt(t, 3, h, 8, 24), A.mult)
             write(t, 3, h, f)
-            p = ps("RB", h, 0, 128); ZN = hf("sz", h, o + 256)
-            mm(p, ONE, row(384, 512), True, False); mm(p, IDB, hf("z1", h), False, False)
-            mm(p, IDNH, hf("lz", h), False, False); mm(p, IDH, hf("lw", h, o), False, True)
-            if ZV:
-                ts(ZN, p, MAGIC, A.add, -MAGIC, A.add)
-            else:
-                act(hf("zm", h), p, AF.Identity, MAGIC)
-                act(ZN, hf("zm", h), AF.Identity, -MAGIC)
-            if t < RO - 1:
-                to_psum(h, ZN)
-                send("z%d%d" % (h, t + 1), 1, hf("lzz", h, o + 256), ZN)
-            else:
-                tab = "tab%d" % h; o = 2048 * h
-                for q in range(2):
-                    store("y", ("yz", 64 * h, 64 * h + 64, 128 * q, 128 * q + 128), r("sz", 768 + 128 * h, 896 + 128 * h, 1, 64 * q + 64, 64 * q))
-                store("y", ("yc", 64 * h, 64 * h + 64, 0, 512), r(tab, 2048, 2560, 1, 64))
-                a = 0
-                for q, n in ENDS[h]:
-                    p0 = 0 if q == "v" else 64
-                    dst = r("pxs", o + a, o + a + n, 1, p0 + 64, p0); src = r(tab, a, a + n, 1, p0 + 64, p0)
-                    if q == "v": cp(dst, src)
-                    else: act(dst, src, AF.Copy)
-                    store("y", ("yx", 64 * h, 64 * h + 64, a, a + n), dst)
-                    a += n
+            for p in ([ps("X", h, 0, 128)] if t < RO - 1 else []) + [ps("RB", h, 0, 128)]:
+                mm(p, ONE, row(QUART), True, False); mm(p, IDB, hf("z1", h), False, False)
+                mm(p, IDNH, hf("lz", h), False, False); mm(p, IDH, hf("lw", h, o), False, False)
+                mm(p, ONE, row(M23), False, False); mm(p, NONE, row(M23), False, True)
+            act(sna(t + 1, h, 32, SN) if t < RO - 1 else hf("sz", h, 256), p, AF.Copy)
+        for q in range(2):
+            store("y", ("yz", 64 * h, 64 * h + 64, 128 * q, 128 * q + 128), part("sz", 256 + 128 * h, 384 + 128 * h, q))
+        store("y", ("yc", 64 * h, 64 * h + 64, 0, 512), part("tab%d" % h, 2048, 2560, 0))
+        for j in range(4):
+            dst = part("pxs", 2048 * h + 512 * j, 2048 * h + 512 * j + 512, j % 2)
+            copy("vs"[j % 2], dst, part("tab%d" % h, 512 * j, 512 * j + 512, j % 2))
+            store("y", ("yx", 64 * h, 64 * h + 64, 512 * j, 512 * j + 512), dst)
 
     for h in range(2):
         cur[0] = h
@@ -537,10 +417,7 @@ def needs(ops):
         for x in rd:
             d.update(j for (j, y, w) in seen[x[0]] if w and meet(x, y))
         for x in wr:
-            for (j, y, w) in seen[x[0]]:
-                if meet(x, y):
-                    if WAW and q in ("v", "s") and ops[j][0] == q and kind not in MOVES and ops[j][1] not in MOVES: f.add(j)
-                    else: d.add(j)
+            d.update(j for (j, y, w) in seen[x[0]] if meet(x, y))
         for n in set(x[0] for x in rd + wr):
             if n in run:
                 if run[n][0] != q: run[n] = [q, [], run[n][1]]
@@ -565,12 +442,12 @@ def needs(ops):
 def cost(o, E):
     q, kind, a = o[:3]
     def n(x): return 16 * n(x[2]) if x[0] == "*" else len(range(x[1], x[2], x[3]))
-    def two(x): return SCRATCH[x[0]][2] in (BF, U16, "float16")
-    if kind == "land": return 0.0, E["rem"] + n(a[2]) * 128 * (2 if two(a[2]) else 4) / E["rbw"]
+    def two(x): return SCRATCH[x[0]][2] in (BF, U16, H)
+    if kind == "land": return E["rows"] + n(a[2]) * 128 * (2 if two(a[2]) else 4) / E["rbw"], E["rem"] - E["rows"]
     if kind == "send": return (2300.0 if a[0] == "u" else 300.0), 0.0
     if kind in ("load", "store"):
         x = a[0] if kind == "load" else a[1]
-        return (1000.0 if q == "g" else 100.0), E["dma"] + n(x) * (x[4] - x[5]) * (2 if two(x) else 4) / 100.0
+        return (1000.0 if q == "g" else 100.0), E["dma"] + n(x) * (x[4] - x[5]) * (2 if two(x) else 4) / E["lbw"]
     if kind == "iota": return 130 + 2 * E["cy"] * n(a[0]), 0.0
     if kind == "mm": return max(min(64, n(a[1])), n(a[2])) * E["pe"] * (1 if two(a[1]) else 4), 60.0
     if a[0][0] == "*": return 50 + n(a[0]) * E["sca"] * E["cy"], 0.0
@@ -578,6 +455,7 @@ def cost(o, E):
     m = 1.0
     if kind == "tt" and SCRATCH[a[1][0]][0] == SCRATCH[a[2][0]][0]: m = 2.0
     if kind in ("cp", "ts") and two(a[0]) and two(a[1]): m = 0.5
+    if kind == "mset" and two(a[0]): m = 0.5
     return max(64, n(a[0]) * m) * E["cy"], 0.0
 
 
@@ -604,7 +482,7 @@ def arrange(ops):
             for j, w in pre[i].items():
                 if at[j] + w > t: t = at[j] + w
             at[i] = t
-            if qs[i] is not None: free[qs[i]] = t + dur[i]
+            free[qs[i]] = t + dur[i]
             if t + dur[i] + tail[i] > last: last = t + dur[i] + tail[i]
         return last
 
@@ -620,11 +498,14 @@ def arrange(ops):
                     t2 = max(free[q2], min([ready[i] for i in p2]))
                     if t2 < t: t = t2; q = q2; p = p2
             i = max([i for i in p if ready[i] <= t + 1.0], key=lambda i: prio[i])
-            if q is not None:
-                soon = [j for j in p if t < ready[j] < t + look * dur[i] and prio[j] > prio[i] + dur[i]]
+            if q is None:
+                i = min(p, key=lambda i: ready[i])
+            else:
+                d = dur[i] + (dur[i + 1] if ops[i][1] == "send" else 0.0)
+                soon = [j for j in p if t < ready[j] < t + look * d and prio[j] > prio[i] + d]
                 if soon:
                     i = min(soon, key=lambda j: ready[j]); t = ready[i]
-                free[q] = t + dur[i]
+            free[q] = t + dur[i]
             p.remove(i); at[i] = t
             for j in nxt[i]:
                 ready[j] = max(ready[j], t + links[j][i]); todo[j] -= 1
@@ -638,14 +519,13 @@ def arrange(ops):
     left = [dur[i] + tail[i] + (BIAS if ops[i][5] == 0 else 0.0) for i in range(N)]
     for i in range(N - 1, -1, -1):
         for j, w in pre[i].items(): left[j] = max(left[j], w + left[i])
-    hold = [HOLD if o[5] == 1 and o[4] and o[4][0][0] == "Y" else 0.0 for o in ops]
-    best = cur = judge(issue(dur, pre, back, hold, left, 0.6))
+    best = cur = judge(issue(dur, pre, back, [0.0] * N, left, 0.6))
     rng = np.random.default_rng(SEED)
     for it in range(PASSES):
-        pre, back, dur, tail = cases[int(rng.integers(PLAN))]
+        pre, back, dur, tail = cases[int(rng.integers(2))]
         shake = rng.random(N // 25 + 1) * NOISE * rng.random()
         u = issue(dur, back, pre, tail, [cur[1][i] + dur[i] + float(shake[i // 25]) for i in range(N)], float(rng.random()))
-        new = judge(issue(dur, pre, back, hold, [u[i] + dur[i] for i in range(N)], float(rng.random())))
+        new = judge(issue(dur, pre, back, [0.0] * N, [u[i] + dur[i] for i in range(N)], float(rng.random())))
         if new[0] < cur[0] + 800.0: cur = new
         if new[0] < best[0]: best = new
     out = best[2]
@@ -729,7 +609,6 @@ def rank_program(g, core, T, topo):
             if a[5] is None: ins = e.tensor_scalar(ap(a[0]), ap(a[1]), ap(a[2]), None, a[4])
             else: ins = e.tensor_scalar(ap(a[0]), ap(a[1]), ap(a[2]), ap(a[3]), a[4], a[5])
         elif kind == "scan": ins = e.tensor_tensor_scan(ap(a[0]), ap(a[1]), ap(a[2]), a[3], a[4], a[5])
-        elif kind == "tr": ins = e.transpose(ap(a[0]), ap(a[1]))
         elif kind == "mset": ins = e.memset(ap(a[0]), a[1])
         elif kind == "act":
             if a[2] == AF.Copy: ins = e.activation(ap(a[0]), ap(a[1]), a[2])

import numpy as np
from concourse.mybir import AluOpType, ActivationFunctionType

RO = 3
BIG = float(1 << 21)
OWN = 16384.0
MAGIC = 12582912.0
BLK = 64
TABW = 2560 + 256
YH = 2064
VT = 200
SN = 160
GATHER = (("v", 0, 16), ("s", 16, 64), ("s", 64, 96), ("s", 96, 128))
HALVES = ((0, 64), (64, 128))
EST = {"cy": 0.83, "gam": 1.56, "sca": 3.8, "pe": 0.5, "same": 150.0, "other": 200.0, "rem": 1450.0, "rbw": 70.0, "rows": 300.0,
       "dma": 1500.0, "lbw": 150.0}
CASES = ({}, {"cy": 0.92, "pe": 0.55}, {"rem": 800.0, "rbw": 100.0}, {"rem": 1800.0, "rbw": 55.0},
         {"gam": 1.9, "sca": 5.0, "cy": 1.0, "pe": 0.6})
BIAS, PASSES, SEED, NOISE = 1500.0, 80, 2, 500.0
INFO = []

S_, P_ = "sbuf", "psum"
F32, BF, I32, U16, H = "float32", "bfloat16", "int32", "uint16", "float16"
SCRATCH = {}
for _dt, _bufs in (
    (F32, {"tab0": TABW, "tab1": TABW, "vf": 16, "sc": 256, "thr": 32, "qd": 16, "s1": 256, "tmp": 384, "val": 512, "at": 256,
           "col": 32, "k16": 128, "ug": 128, "u4": 128, "wm": 128, "cown": 128, "cmin": 128, "c01": 128, "dum": 128, "bo": 128,
           "bf8": 8, "kps": 32, "w4": 256}),
    (BF, {"pxs": 4096, "wk": 32, "Y": 2 * YH, "M": 4096, "ind": 256, "noh": 256, "oh": 256, "E": 1024, "xe": 256, "bc": 256, "ey": 256,
          "z1": 256, "lz": 256, "nhi": 256, "sz": 512, "sx": 256 * RO, "lx": 256 * RO, "sf": 272 * RO, "lf": 272 * RO, "sw": 256 * RO,
          "lw": 256 * RO, "rows": 1936, "one": 256, "idb": 768, "bb": 64, "bx": 384, "bo4": 128, "bwn": 32, "bkap": 512, "seh": 256}),
    (H, {"nf": 768, "nm": 256, "ex": 256, "exb": 256, "qf": 256, "fr": 256, "vt": 4 * RO * VT, "sna": 2 * SN * (RO + 1), "tf": 512,
         "s2": 256, "r2": 256, "tt": 512, "idf": 512, "bh8": 8, "selk": 512, "selb": 384, "sef": 256}),
    (I32, {"ces": 1024, "v0s": 16, "bj": 32, "kk": 32, "so": 512, "jj": 16, "mm": 16, "pi": 8, "pj": 8}),
    (U16, {"offn": 256, "bu": 16 * (RO + 1), "sb": 16 * RO, "go": 16, "gs": 16, "ku": 16, "wo": 32, "cexp": 8, "cid": 8}),
):
    for _n, _w in _bufs.items():
        SCRATCH[_n] = (S_, [128, _w], _dt)
for _h in range(2):
    for _n in ("X", "SC", "RA", "RB"):
        SCRATCH["%s%d" % (_n, _h)] = (P_, [128, 512], F32)
MSG = ["b", "x", "n", "f", "m", "w"]
NDMA = 48
SEMAPHORES = (["qv", "qs", "qp", "qg", "sent", "u"] + ["d%d" % i for i in range(NDMA)]
              + ["%s%d%d" % (m, h, t) for m in MSG for h in range(2) for t in range(RO)])
A = AluOpType
AF = ActivationFunctionType
QS = ["v", "s", "p", "g", "y"]
MOVES = ("load", "store", "send", "land")


def r(name, a, b, step=1, p=128, p0=0):
    return (name, a, b, step, p, p0)


def ind(win, off):
    return ("*", win, off)


def plan():
    ops = []
    cur = [None]

    def acc(x):
        if x is None or isinstance(x, (int, float)):
            return []
        return [x[1], x[2]] if x[0] == "*" else [x]

    def add(q, kind, o, ins, args):
        rd, wr = ([o[2]], [o[1]]) if o[0] == "*" else ([], [o])
        for x in ins:
            rd = rd + acc(x)
        ops.append([q, kind, args, rd, wr, cur[0]])

    def cp(o, i): add("v", "cp", o, [i], (o, i))
    def tt(o, a, b, op): add("v", "tt", o, [a, b], (o, a, b, op))
    def ts(o, a, s1, op0, s2=None, op1=None): add("v", "ts", o, [a, s1, s2], (o, a, s1, s2, op0, op1))
    def scan(o, d0, d1, init, op0, op1): add("v", "scan", o, [d0, d1], (o, d0, d1, init, op0, op1))
    def mset(o, c): add("v", "mset", o, [], (o, c))
    def act(o, i, f, bias=0.0, scale=1.0): add("s", "act", o, [i, bias, scale], (o, i, f, bias, scale))
    def copy(q, o, i): return cp(o, i) if q == "v" else act(o, i, AF.Copy)
    def times(o, i, w): act(o, i, AF.Identity, 0.0, w)
    def mm(o, l, rh, st, sp): add("p", "mm", o, [l, rh], (o, l, rh, st, sp))
    def iota(o, pat, base, cm): add("g", "iota", o, [], (o, pat, base, cm))
    def load(q, o, src): ops.append([q, "load", (o, src), [], [o], cur[0]])
    def store(q, dst, i): ops.append([q, "store", (dst, i), [i], [], cur[0]])

    def send(name, step, dst, src):
        ops.append(["g", "send", (name, step, dst, src), [src], [], cur[0]])
        ops.append([None, "land", (name, step, dst), [], [dst], cur[0]])

    def hf(name, h, base=0): return r(name, base + 128 * h, base + 128 * h + 128)
    def sm(name, h, base=0): return r(name, base + 8 * h, base + 8 * h + 8)
    def ends(name, h, base=0): return r(name, base + 128 * h + 15, base + 128 * h + 128, 16)
    def c(i): return r("col", i, i + 1)
    def ps(name, h, a, b, step=1, p=128): return r("%s%d" % (name, h), a, b, step, p)
    def part(name, a, b, q): return r(name, a, b, 1, 64 * q + 64, 64 * q)
    def row(a, n=128): return r("rows", a, a + n, 1, 1)
    def PX(h): return r("pxs", 2048 * h, 2048 * h + 2048)
    def CE(h): return r("ces", 512 * h, 512 * h + 512)
    def tab(h, a, b): return r("tab%d" % h, a, b)
    def YW(h): return r("Y", YH * h, YH * h + YH)
    def vt(t, step, h, a, b): o = VT * (4 * t + 2 * (step - 2) + h); return r("vt", o + a, o + b)
    def sna(t, h, a, b): o = SN * (2 * t + h); return r("sna", o + a, o + b)
    IDB, IDN, ID4, IDH, IDNH, IDG = [hf("idb", i) for i in range(6)]
    IDF, IDFN, IDF2, ID5 = [hf("idf", i) for i in range(4)]
    K16, UG, U4, WM, BO, COWN, CMIN = [hf(n, 0) for n in ("k16", "ug", "u4", "wm", "bo", "cown", "cmin")]
    WC, GC, P7, P3, G3, R6, W16P = c(0), c(1), c(2), c(3), c(4), c(5), c(8)
    CEXP = r("cexp", 0, 8); BF8 = r("bf8", 0, 8); BH8 = r("bh8", 0, 8)
    ONE = r("one", 0, 128, 1, 1); NONE = r("one", 128, 256, 1, 1)
    K4096, KM16, K512, POS = 0, 128, 256, 1920
    QUART, OFF3, MHALF, TIE, OFF1, C1024, M34, M23 = 512, 768, 1024, 1280, 1408, 1536, 1664, 1792

    load("y", r("wk", 16, 17), ("wu", 0, 128, 0, 1))
    for h in range(2):
        cur[0] = h
        for q in range(2): load("y", part("v0s", 8 * h, 8 * h + 8, q), ("v0", 64 * h, 64 * h + 64, 8 * q, 8 * q + 8))
        for q in range(2): load("y", part("ces", 512 * h, 512 * h + 512, q), ("ce", 64 * h, 64 * h + 64, 0, 512))
        for q in range(2): load("y", part("sz", 128 * h, 128 * h + 128, q), ("z0", 64 * h, 64 * h + 64, 128 * q, 128 * q + 128))
        for q in range(2): load("sy"[h], part("pxs", 2048 * h, 2048 * h + 2048, q), ("px", 64 * h, 64 * h + 64, 0, 2048))
    cur[0] = None
    load("y", r("wk", 0, 16), ("kap", 0, 128, 0, 16))
    send("u", -1, r("wk", 24, 25), r("wk", 16, 17))
    for h in range(2):
        cur[0] = h
        act(sna(0, h, 32, SN), hf("sz", h), AF.Copy)
        if h == 0: ops.append(["g", "load", (tab(h, 0, 2048), PX(h)), [PX(h)], [tab(h, 0, 2048)], h])
        else:
            for j in range(0, 2048, 512): act(tab(h, j, j + 512), r("pxs", 2048 * h + j, 2048 * h + j + 512), AF.Copy)
        cp(sm("bu", h), sm("v0s", h))
        cp(tab(h, 2048, 2560), CE(h))
        mset(tab(h, 2560, 2568), 0.0)
    cur[0] = None

    iota(r("pi", 0, 1), [[0, 1]], 0, 1)
    iota(K16, [[0, 8], [1, 16]], 0, 0); iota(UG, [[1, 8], [0, 16]], 0, 0); iota(U4, [[0, 2], [1, 4], [0, 16]], 0, 0)
    iota(row(POS, 8), [[256, 8]], 0, 0); iota(r("tmp", 0, 128), [[1, 128]], 2560 + 1024, 0)
    k1 = r("k16", 0, 128, 1, 1)
    times(row(K4096), k1, 4096.0); act(row(KM16), k1, AF.Identity, -16.0); times(row(K512), k1, 512.0); times(row(K512 + 128), k1, 2048.0)
    mset(r("one", 0, 128), 1.0); mset(r("one", 128, 256), -1.0)
    mset(r("Y", 0, 16), 0.0); mset(r("Y", YH, YH + 16), 0.0); mset(r("bj", 0, 32), 0)
    for a, n, w in ((QUART, 256, -0.25), (OFF3, 128, -2032.0 * 8192), (OFF3 + 128, 128, -300.0 * 32768), (MHALF, 128, -0.5),
                    (MHALF + 128, 128, 0.0), (TIE, 128, 1.0 / 1024), (OFF1, 128, 2040.0 * 8192), (C1024, 128, 1024.0),
                    (M34, 128, MAGIC * 2048), (M23, 128, MAGIC)):
        mset(r("rows", a, a + n), w)
    for h in range(2): times(sna(0, h, 8, 16), r("k16", 0, 8), 0.0)
    PI = r("pi", 0, 1)
    ts(r("pj", 0, 1), PI, 15, A.bitwise_and); ts(r("pj", 1, 2), PI, 4, A.logical_shift_right)
    ts(r("pj", 2, 3), PI, 7, A.bitwise_and); ts(r("pj", 3, 4), PI, 3, A.logical_shift_right)
    ts(r("pj", 4, 5), PI, 4, A.logical_shift_right, 3, A.bitwise_and); ts(r("pj", 5, 6), PI, 6, A.logical_shift_right)
    cp(r("col", 0, 6), r("pj", 0, 6))
    act(W16P, WC, AF.Identity, 16.0, 16.0)
    ts(BO, UG, GC, A.is_equal); ts(WM, K16, WC, A.is_equal); tt(IDB, BO, WM, A.mult)
    ts(BF8, r("k16", 0, 8), GC, A.is_equal); act(BH8, BF8, AF.Copy)
    cp(CEXP, r("k16", 0, 8)); cp(r("cid", 0, 1), WC)
    ts(CMIN, K16, 0.0, A.is_equal, float(1 << 30), A.mult); act(hf("c01", 0), CMIN, AF.Identity, 1.0, -1.0 / (1 << 30))
    times(COWN, WM, -2 * OWN)
    for i, w in enumerate((-16.0, 65536.0, -8192.0, -131072.0, 8192.0, 32768.0, -16384.0, -65536.0)): times(sm("bb", i), BF8, w)
    for i, w in enumerate((65536.0, 8192.0, 32768.0)): times(hf("bx", i), BO, w)
    times(hf("bo4", 0), BO, 4096.0)
    for ap, w in ((IDF, 1.0), (IDN, -1.0), (ID4, -4096.0), (IDH, 0.5), (IDNH, -0.5), (IDG, -BIG), (IDFN, -1.0), (IDF2, -2.0), (ID5, 512.0)):
        times(ap, IDB, w)
    for q in range(2):
        ts(c(9 + q), R6, float(q), A.is_equal)
        ts(hf("w4", q), U4, G3, A.is_equal, c(9 + q), A.mult)
        tt(hf("sef", q), hf("w4", q), WM, A.mult)
        times(hf("seh", q), hf("sef", q), 0.5)
    for h in range(2):
        cur[0] = h
        kp = r("kps", 16 * h, 16 * h + 16)
        mm(ps("RB", h, 0, 16), hf("seh", h), r("wk", 0, 16), True, True)
        times(kp, ps("RB", h, 0, 16), 2.0)
        mm(ps("RB", h, 16, 17), hf("seh", h), r("wk", 24, 25), True, True)
        for j in range(2): ts(sm("bwn", j, 16 * h), BF8, ps("RB", h, 16, 17), A.mult, 1.0 / 256, A.mult)
        for g8 in range(8): times(r("bkap", 128 * h + 16 * g8, 128 * h + 16 * g8 + 16), kp, r("bf8", g8, g8 + 1))
        times(hf("bkap", h, 256), hf("bkap", h), -1.0)
    cur[0] = None
    times(c(11), R6, 128.0)
    act(r("tmp", 128, 256), r("tmp", 0, 128), AF.Identity, c(11))
    tt(r("tmp", 256, 384), r("tmp", 128, 256), WM, A.mult)
    act(hf("dum", 0), r("tmp", 256, 384), AF.Identity, -2048.0)
    ts(c(16), P3, 0.0, A.is_equal); ts(c(17), P3, 3.0, A.is_equal)
    times(c(18), c(16), 2047.0); ts(c(19), P3, 4.0, A.is_equal, 4096.0, A.mult)
    ts(c(20), P3, 3.0, A.is_lt, c(18), A.add); act(c(25), c(20), AF.Identity, c(19))
    ts(hf("selk", 0), UG, P7, A.is_equal, c(25), A.mult)
    act(c(21), c(16), AF.Identity, c(17), 4096.0)
    ts(hf("selk", 1), UG, P7, A.is_equal, c(21), A.mult)
    ts(c(22), GC, 3.0, A.is_equal)
    for j in range(4): times(hf("tf", j), WM, c(22))
    act(hf("s1", 0), WM, AF.Identity, -OWN, OWN); act(hf("s1", 1), WM, AF.Identity, OWN - 1024.0, -OWN)
    for j in range(2):
        times(hf("val", j), hf("s1", j), c(22))
        tt(hf("selk", 2 + j), hf("val", j), hf("selk", 0), A.add)
    ts(hf("selb", 0), UG, P7, A.is_equal, -256.0, A.mult)
    times(hf("selb", 1), hf("selb", 0), -16.0); times(hf("selb", 2), hf("selb", 0), -1.0 / 512)

    def to_psum(h, x):
        mm(ps("X", h, 0, 128), IDB, x, True, True)

    def names(step, h, win, cells):
        for a, b in HALVES:
            cp(r("offn", 128 * h + a, 128 * h + b), ind(win, r(cells[0], cells[1] + a // 16, cells[1] + b // 16)))
        cp(hf("nf", h, 256 * (step - 1)), hf("offn", h))

    def scores(step, h, win, x):
        nf = hf("nf", h, 256 * (step - 1)); y0 = YH * h + 16; S0 = ps("SC", h, 0, 128); w = 256 if step == 3 else 128
        def Yk(k): return r("Y", y0 + k, y0 + 2048, 16)
        def Mk(k): return hf("M", k, 2048 * h)
        if step == 1:
            mm(S0, ONE, row(K512), True, False); mm(S0, ONE, row(OFF1), False, False)
            mm(ps("RA", h, 0, 256), ONE, row(MHALF, 256), True, False); mm(ps("RA", h, 0, 128), ONE, row(TIE), False, False)
        elif step == 2:
            mm(S0, ONE, row(K4096), True, False); mm(S0, x, hf("bx", 0), False, False)
            mm(ps("RB", h, 128, 256), ONE, row(KM16), True, False)
        else:
            mm(ps("SC", h, 0, 256), ONE, row(K512, 256), True, False); mm(ps("SC", h, 0, 256), ONE, row(OFF3, 256), False, False)
            mm(ps("SC", h, 0, 256), x, r("bx", 128, 384), False, False)
            mm(S0, hf("nhi", h), IDN, False, False)
        for q, a, b in GATHER:
            copy(q, r("Y", y0 + 16 * a, y0 + 16 * b), ind(win, r("offn", 128 * h + a, 128 * h + b)))
        if step == 1:
            for k in range(16): mm(ps("RA", h, k, 256, 16), Yk(k), r("bwn", 16 * h, 16 * h + 16), False, k == 15)
            ts(hf("qf", h), ps("RA", h, 0, 128), MAGIC, A.add, -MAGIC, A.add)
            tt(hf("fr", h), ps("RA", h, 128, 256), hf("qf", h), A.subtract)
        else:
            for k in range(16): mm(ps("SC", h, k, w, 16), Yk(k), sm("bb", 1) if step == 2 else r("bb", 32, 48), False, False)
        for a, b in HALVES:
            for k in range(16):
                m0 = 2048 * h + 128 * k
                tt(r("M", m0 + a, m0 + b), r("Y", y0 + 16 * a + k, y0 + 16 * b, 16), ps("X", h, a, b), A.min)
        for k in range(16): mm(ps("SC", h, k, w, 16), Mk(k), (sm("bb", 2), sm("bb", 3), r("bb", 48, 64))[step - 1], False, False)
        if step == 1:
            mm(S0, ID5, hf("fr", h), False, True)
        elif step == 2:
            mm(S0, nf, IDF, False, True)
            for k in range(16): mm(ps("RB", h, 128 + k, 256, 16), Mk(k), sm("bb", 0), False, False)
        else:
            mm(S0, nf, IDF, False, False); mm(ps("SC", h, 128, 256), nf, IDF, False, True)

    def to_list(src, h, slots):
        tt(hf("ex", h), ind(sm(src, h), CEXP), WM, A.mult)
        mm(ps("SC", h, 400, 408), ONE, row(POS, 8), True, False)
        mm(ps("SC", h, 400, 408), hf("ex", h), BH8, False, True)
        if slots: mm(ps("SC", h, 408, 416), hf("ex", h), BH8, True, True)
        ts(sm("go", h), ps("SC", h, 400, 408), W16P, A.add)
        if slots: cp(sm("gs", h), ps("SC", h, 408, 416))

    def pick_name(step, h, dst):
        nf = hf("nf", h, 256 * (step - 1)); slot = ind(r("wm", 0, 16), sm("gs", h))
        if step == 1:
            tt(hf("nm", h), slot, nf, A.mult)
        else:
            times(hf("oh", h), slot, -1.0)
            mm(ps("RB", h, 384, 512), ID4, hf("oh", h), True, False); mm(ps("RB", h, 384, 512), IDF, nf, False, True)
            act(hf("nm", h), ps("RB", h, 384, 512), AF.Relu, -4096.0)
        mm(ps("RB", h, 16, 24), hf("nm", h), BH8, True, True)
        act(dst, ps("RB", h, 16, 24), AF.Copy)

    def rows(o, sel, i, j, start, stop):
        K = 64 if sel == "selk" else 8
        mm(o, r(sel, 128 * i, 128 * i + 128, 1, K), r("tf", 128 * j, 128 * j + 128, 1, K), start, stop)

    def write(t, step, h, x, between=None):
        j = 2 * (step - 2) + h; K = 32 if step == 2 else 40; NC = BLK // 16
        KM = ps("X", h, 0, 128); KR = ps("RA", h, 128, 256); P = ps("SC", h, 256, 384)
        mm(ps("RA", h, 0, 128, 1, K), vt(t, step, h, 16, 16 + K), IDF, True, True)
        act(r("tf", 128 * j, 128 * j + 128, 1, K), ps("RA", h, 0, 128, 1, K), AF.Copy)
        rows(KM, "selk", 2, j, True, True)
        rows(KR, "selk", 0, j, True, True)
        scan(hf("s1", h), COWN, KM, -1.0, A.add, A.max)
        o = ps("RB", h, 128, 256)
        mm(o, hf("noh", h), IDB, True, False); rows(o, "selb", 2, j, False, True)
        o = ps("RB", h, 256, 384)
        mm(o, IDB, x, True, False); rows(o, "selb", 0, j, False, True)
        o = ps("RB", h, 384, 512)
        mm(o, hf("noh", h), ID4, True, False); rows(o, "selk", 1, j, False, True)
        act(hf("bc", h), ps("RB", h, 128, 256), AF.Abs, -0.5)
        act(hf("xe", h), ps("RB", h, 256, 384), AF.Relu)
        act(hf("r2", h), ps("RB", h, 384, 512), AF.Relu, -4096.0)
        if between: between()
        rows(P, "selk", 3, j, True, False)
        T_ = hf("tt", j)
        ts(sm("ku", h), ends("s1", h), 2560.0, A.min)
        tt(T_, ind(tab(h, 0, 2568), sm("ku", h)), hf("bc", h), A.mult)
        for i in range(NC):
            s = 1 + 16 * i; e = 256 * i + 128 * h
            tt(r("E", e + s, e + 128), r("s1", 128 * h, 128 * h + 128 - s), ps("RA", h, 128 + s, 256), A.is_equal)
            mm(ps("SC", h, 256 + s, 384), hf("bo4", 0), r("E", e + s, e + 128), False, i == NC - 1)
        def new(q): return ps("X", h, 256 + 128 * q, 384 + 128 * q)
        mm(ps("X", h, 256, 512), ONE, row(QUART, 256), True, False)
        for q in range(2):
            mm(new(q), hf("seh", q), hf("xe", h), False, False); mm(new(q), hf("sef", q), hf("r2", h), False, False)
        for q in (1, 0): mm(new(q), hf("sef", q), T_, False, q == 0)
        for q in (1, 0): act(hf("val", q, 256 * h), new(q), AF.Identity, MAGIC)
        scan(hf("s2", h), hf("dum", 0), P, -2048.0, A.max, A.min)
        for q in range(2): mm(ps("SC", h, 384 + 8 * q, 392 + 8 * q), hf("sef", q), ends("s2", h), True, True)
        ts(r("wo", 16 * h, 16 * h + 16), ps("SC", h, 384, 400), 1024.0, A.add)
        for b in range(256 // BLK - 1, -1, -1):
            ts(ind(tab(h, 0, TABW), r("wo", 16 * h + NC * b, 16 * h + NC * b + NC)),
               r("val", 256 * h + BLK * b, 256 * h + BLK * b + BLK), 1.0, A.mult, -MAGIC, A.add)

    def stream(h):
        to_psum(h, hf("sz", h))
        bj = r("bj", 16 * h, 16 * h + 8); kk = r("kk", 16 * h, 16 * h + 16); k0 = sm("kk", 2 * h); k1 = sm("kk", 2 * h + 1)
        for t in range(RO):
            o = 256 * t; cells = CE(h) if t == 0 else tab(h, 2048, 2560); plas = PX(h) if t == 0 else tab(h, 0, 2048)
            names(1, h, cells, sm("bu", h, 16 * t))
            scores(1, h, plas, None)
            scan(hf("so", h), CMIN, ps("SC", h, 0, 128), 0.0, A.add, A.min)
            ts(bj, ends("so", h), 511, A.bitwise_and)
            tt(hf("exb", h), ind(bj, CEXP), WM, A.mult)
            mm(ps("RA", h, 256, 264), hf("exb", h), BH8, True, True)
            cp(sm("sb", h, 16 * t), ps("RA", h, 256, 264))
            BU = sm("bu", h, 16 * t + 16)
            send("b%d%d" % (h, t), 1, BU, sm("sb", h, 16 * t))
            ts(sm("jj", h), ends("so", h), 9, A.arith_shift_right, 15, A.bitwise_and)
            to_list("jj", h, True)
            act(hf("sx", h, o), ind(YW(h), sm("go", h)), AF.Copy)
            send("x%d%d" % (h, t), 1, hf("lx", h, o), hf("sx", h, o))
            act(sna(t, h, 16, 32), ind(r("bj", 16 * h, 16 * h + 16), r("cid", 0, 1)), AF.Copy)
            pick_name(1, h, sna(t, h, 0, 8))
            send("n%d%d" % (h, t), 1, vt(t, 2, h, 40, 40 + SN), sna(t, h, 0, SN))
            x = hf("lx", h, o); e = vt(t, 2, h, 8, 16); phi = vt(t, 2, h, 16, 24); a = vt(t, 2, h, 48, 56)
            to_psum(h, x)
            names(2, h, cells, BU)
            act(sm("thr", h, 16), a, AF.Abs, -2.0, 2.0)
            act(sm("thr", h), sm("thr", h, 16), AF.Identity, -10.0, -1.0)
            scores(2, h, plas, x)
            scan(hf("so", h), CMIN, ps("SC", h, 0, 128), 0.0, A.add, A.min)
            act(hf("ind", h), ps("SC", h, 0, 128), AF.Sign, 255.985, -1.0 / 65536)
            ts(sm("jj", h), ends("so", h), 12, A.arith_shift_right, 15, A.bitwise_and)
            tt(hf("noh", h), ind(sm("jj", h), CEXP), K16, A.not_equal)
            mm(ps("RB", h, 128, 256), IDG, hf("noh", h), False, True)
            ts(k0, ends("so", h), 2047, A.bitwise_and)
            scan(hf("sc", h), hf("c01", 0), hf("ind", h), 0.0, A.mult, A.add)
            tt(phi, ends("sc", h), sm("thr", h), A.is_lt)
            tt(e, ends("sc", h), sm("thr", h), A.is_ge)
            tt(vt(t, 2, h, 24, 32), k0, e, A.mult)
            tt(vt(t, 2, h, 32, 40), vt(t, 2, h, 56, 64), phi, A.mult)
            scan(hf("so", h, 256), CMIN, ps("RB", h, 128, 256), 0.0, A.add, A.min)
            ts(sm("mm", h), ends("so", h, 256), 15, A.bitwise_and)
            to_list("mm", h, True)
            of = 136 * (2 * t + h)
            tt(r("sf", of, of + 128), ind(YW(h), sm("go", h)), x, A.max)
            times(r("sf", of + 128, of + 136), e, -8192.0)
            send("f%d%d" % (h, t), 1, r("lf", of, of + 136), r("sf", of, of + 136))

            def name_m():
                mm(ps("RB", h, 24, 32), IDF, a, True, False); mm(ps("RB", h, 24, 32), IDF, e, False, True)
                act(sna(t + 1, h, 8, 16), ps("RB", h, 24, 32), AF.Copy)
                pick_name(2, h, vt(t, 2, h, 0, 8))
                send("m%d%d" % (h, t), 1, vt(t, 3, h, 40, 56), vt(t, 2, h, 0, 16))
            write(t, 2, h, x, name_m)
            if t == RO - 1:
                cp(sm("vf", h), BU)
                mm(ps("RB", h, 0, 128, 1, 8), sna(RO, h, 8, 16), IDF, True, True)
                act(r("at", 128 * h, 128 * h + 128, 1, 8), ps("RB", h, 0, 128, 1, 8), AF.Copy)
                for q in range(2):
                    store("y", ("yv", 64 * h, 64 * h + 64, 8 * q, 8 * q + 8), part("vf", 8 * h, 8 * h + 8, q))
                    store("y", ("ya", 4 * h, 4 * h + 4, 128 * q, 128 * q + 128), r("at", 128 * h, 128 * h + 128, 1, 4 * q + 4, 4 * q))
            f = r("lf", of, of + 128); bank = ps("RA", h, 256, 384)
            mm(bank, ONE, row(C1024), True, False); mm(bank, ONE, row(MHALF), False, False)
            mm(bank, hf("bkap", h, 256), f, False, False)
            mm(bank, ONE, row(M34), False, False); mm(bank, NONE, row(M34), False, False)
            mm(bank, hf("bkap", h), f, False, True)
            to_psum(h, f)
            for p, q in HALVES: cp(r("offn", 128 * h + p, 128 * h + q), ps("RA", h, 256 + p, 256 + q))
            act(hf("nf", h, 512), bank, AF.Copy)
            act(hf("nhi", h), bank, AF.Identity, 98304.0 - 255.5)
            z = vt(t, 2, h, 72, 200)
            mm(ps("RB", h, 0, 128), IDF2, hf("tt", h), True, False); rows(ps("RB", h, 0, 128), "selb", 1, h, False, True)
            mm(ps("RB", h, 128, 256), IDFN, z, True, False); rows(ps("RB", h, 128, 256), "selb", 0, h, False, True)
            act(hf("ey", h), ps("RB", h, 0, 128), AF.Relu, 0.0, -1.0)
            act(hf("lz", h), ps("RB", h, 128, 256), AF.Relu, -256.0, -1.0)
            mm(ps("RB", h, 256, 384), IDF, z, True, False); mm(ps("RB", h, 256, 384), IDN, hf("ey", h), False, True)
            act(hf("z1", h), ps("RB", h, 256, 384), AF.Abs)
            scores(3, h, tab(h, 0, 2048), f)
            for q in range(2): scan(hf("so", h, 256 * q), CMIN, ps("SC", h, 128 * q, 128 * q + 128), 0.0, A.add, A.min)
            ts(sm("jj", h), ends("so", h), 9, A.arith_shift_right, 15, A.bitwise_and)
            tt(sm("qd", h), sm("jj", h), r("lf", of + 128, of + 136), A.add)
            to_list("qd", h, False)
            act(hf("sw", h, o), ind(YW(h), sm("go", h)), AF.Copy)
            send("w%d%d" % (h, t), -1, hf("lw", h, o), hf("sw", h, o))
            tt(hf("noh", h), ind(sm("jj", h), CEXP), K16, A.not_equal)
            ts(vt(t, 3, h, 16, 24), ends("so", h), float((600 - 2044) * 8192), A.is_ge)
            ts(vt(t, 3, h, 8, 16), ends("so", h), float((600 - 2044) * 8192), A.is_lt)
            ts(k0, ends("so", h, 256), 2047, A.bitwise_and)
            ts(k1, ends("so", h), 511, A.bitwise_and)
            tt(vt(t, 3, h, 24, 40), kk, vt(t, 3, h, 8, 24), A.mult)
            write(t, 3, h, f)
            for p in ([ps("X", h, 0, 128)] if t < RO - 1 else []) + [ps("RB", h, 0, 128)]:
                mm(p, ONE, row(QUART), True, False); mm(p, IDB, hf("z1", h), False, False)
                mm(p, IDNH, hf("lz", h), False, False); mm(p, IDH, hf("lw", h, o), False, False)
                mm(p, ONE, row(M23), False, False); mm(p, NONE, row(M23), False, True)
            act(sna(t + 1, h, 32, SN) if t < RO - 1 else hf("sz", h, 256), p, AF.Copy)
        for q in range(2):
            store("y", ("yz", 64 * h, 64 * h + 64, 128 * q, 128 * q + 128), part("sz", 256 + 128 * h, 384 + 128 * h, q))
        store("y", ("yc", 64 * h, 64 * h + 64, 0, 512), part("tab%d" % h, 2048, 2560, 0))
        for j in range(4):
            dst = part("pxs", 2048 * h + 512 * j, 2048 * h + 512 * j + 512, j % 2)
            copy("vs"[j % 2], dst, part("tab%d" % h, 512 * j, 512 * j + 512, j % 2))
            store("y", ("yx", 64 * h, 64 * h + 64, 512 * j, 512 * j + 512), dst)

    for h in range(2):
        cur[0] = h
        stream(h)
    return ops


def needs(ops):
    seen = {n: [] for n in SCRATCH}
    run = {n: [None, [], []] for n, s in SCRATCH.items() if s[0] == P_}
    deps = []; after = []
    def meet(x, y): return x[1] < y[2] and y[1] < x[2] and x[5] < y[4] and y[5] < x[4]
    for i, (q, kind, args, rd, wr, st) in enumerate(ops):
        d = set(); f = set()
        for x in rd:
            d.update(j for (j, y, w) in seen[x[0]] if w and meet(x, y))
        for x in wr:
            d.update(j for (j, y, w) in seen[x[0]] if meet(x, y))
        for n in set(x[0] for x in rd + wr):
            if n in run:
                if run[n][0] != q: run[n] = [q, [], run[n][1]]
                d.update(run[n][2])
                if q == "p" and run[n][1]: f.add(run[n][1][-1])
                run[n][1].append(i)
        if q == "p":
            f.update(j for j in d if ops[j][0] == "p"); d = set(j for j in d if ops[j][0] != "p")
        for x in wr:
            if x[3] == 1 and args[0][0] != "*":
                seen[x[0]] = [s for s in seen[x[0]] if not (x[1] <= s[1][1] and s[1][2] <= x[2] and x[5] <= s[1][5] and s[1][4] <= x[4])]
            seen[x[0]].append((i, x, True))
        for x in rd:
            seen[x[0]].append((i, x, False))
        if kind == "load":
            f.update(j for j in range(i) if ops[j][1] == "load" and ops[j][0] == q)
        d.discard(i)
        deps.append(d); after.append(f)
    return deps, after


def cost(o, E):
    q, kind, a = o[:3]
    def n(x): return 16 * n(x[2]) if x[0] == "*" else len(range(x[1], x[2], x[3]))
    def two(x): return SCRATCH[x[0]][2] in (BF, U16, H)
    if kind == "land": return E["rows"] + n(a[2]) * 128 * (2 if two(a[2]) else 4) / E["rbw"], E["rem"] - E["rows"]
    if kind == "send": return (2300.0 if a[0] == "u" else 300.0), 0.0
    if kind in ("load", "store"):
        x = a[0] if kind == "load" else a[1]
        return (1000.0 if q == "g" else 100.0), E["dma"] + n(x) * (x[4] - x[5]) * (2 if two(x) else 4) / E["lbw"]
    if kind == "iota": return 130 + 2 * E["cy"] * n(a[0]), 0.0
    if kind == "mm": return max(min(64, n(a[1])), n(a[2])) * E["pe"] * (1 if two(a[1]) else 4), 60.0
    if a[0][0] == "*": return 50 + n(a[0]) * E["sca"] * E["cy"], 0.0
    if kind != "mset" and a[1][0] == "*": return (50 if q == "v" else 65) + n(a[0]) * E["gam"] * E["cy"], 0.0
    m = 1.0
    if kind == "tt" and SCRATCH[a[1][0]][0] == SCRATCH[a[2][0]][0]: m = 2.0
    if kind in ("cp", "ts") and two(a[0]) and two(a[1]): m = 0.5
    if kind == "mset" and two(a[0]): m = 0.5
    return max(64, n(a[0]) * m) * E["cy"], 0.0


def arrange(ops):
    deps, after = needs(ops)
    N = len(ops); qs = [o[0] for o in ops]

    def graph(E):
        cs = [cost(o, E) for o in ops]
        pre = [dict() for o in ops]; back = [dict() for o in ops]
        for i, o in enumerate(ops):
            for j in after[i]: pre[i][j] = cs[j][0]
            for j in deps[i]: pre[i][j] = cs[j][0] + cs[j][1] + (E["same"] if ops[j][0] == o[0] else E["other"])
            if o[1] == "land": pre[i][i - 1] = cs[i - 1][0]
            for j, w in pre[i].items(): back[j][i] = w + cs[i][0] - cs[j][0]
        return pre, back, [x[0] for x in cs], [x[1] for x in cs]
    cases = [graph(dict(EST, **x)) for x in CASES]

    def length(order, case):
        pre, back, dur, tail = case
        at = [0.0] * N; free = {q: 0.0 for q in QS + [None]}; last = 0.0
        for i in order:
            t = free[qs[i]]
            for j, w in pre[i].items():
                if at[j] + w > t: t = at[j] + w
            at[i] = t
            free[qs[i]] = t + dur[i]
            if t + dur[i] + tail[i] > last: last = t + dur[i] + tail[i]
        return last

    def issue(dur, links, nxt, first, prio, look):
        todo = [len(p) for p in links]; ready = list(first); at = [0.0] * N
        pool = {q: [] for q in QS + [None]}; free = {q: 0.0 for q in pool}
        for i in range(N):
            if not todo[i]: pool[qs[i]].append(i)
        for done in range(N):
            t = 1e18
            for q2, p2 in pool.items():
                if p2:
                    t2 = max(free[q2], min([ready[i] for i in p2]))
                    if t2 < t: t = t2; q = q2; p = p2
            i = max([i for i in p if ready[i] <= t + 1.0], key=lambda i: prio[i])
            if q is None:
                i = min(p, key=lambda i: ready[i])
            else:
                d = dur[i] + (dur[i + 1] if ops[i][1] == "send" else 0.0)
                soon = [j for j in p if t < ready[j] < t + look * d and prio[j] > prio[i] + d]
                if soon:
                    i = min(soon, key=lambda j: ready[j]); t = ready[i]
            free[q] = t + dur[i]
            p.remove(i); at[i] = t
            for j in nxt[i]:
                ready[j] = max(ready[j], t + links[j][i]); todo[j] -= 1
                if not todo[j]: pool[qs[j]].append(j)
        return at

    def judge(s):
        order = sorted(range(N), key=lambda i: (s[i], i))
        return sum(length(order, x) for x in cases) / len(cases), s, order
    pre, back, dur, tail = cases[0]
    left = [dur[i] + tail[i] + (BIAS if ops[i][5] == 0 else 0.0) for i in range(N)]
    for i in range(N - 1, -1, -1):
        for j, w in pre[i].items(): left[j] = max(left[j], w + left[i])
    best = cur = judge(issue(dur, pre, back, [0.0] * N, left, 0.6))
    rng = np.random.default_rng(SEED)
    for it in range(PASSES):
        pre, back, dur, tail = cases[int(rng.integers(2))]
        shake = rng.random(N // 25 + 1) * NOISE * rng.random()
        u = issue(dur, back, pre, tail, [cur[1][i] + dur[i] + float(shake[i // 25]) for i in range(N)], float(rng.random()))
        new = judge(issue(dur, pre, back, [0.0] * N, [u[i] + dur[i] for i in range(N)], float(rng.random())))
        if new[0] < cur[0] + 800.0: cur = new
        if new[0] < best[0]: best = new
    out = best[2]
    INFO[:] = [best[0]]
    pos = {i: k for k, i in enumerate(out)}
    return [ops[i] for i in out], [sorted((pos[j] for j in deps[i]), reverse=True) for i in out]


def waits_of(ops, deps):
    known = {q: {} for q in QS}
    clock = [None] * len(ops); waits = [[] for o in ops]
    def chan(j): return ("d", j) if ops[j][1] in MOVES else ("c", ops[j][0])
    for i, o in enumerate(ops):
        if o[0] is None:
            clock[i] = {chan(i): i}
            continue
        kn = known[o[0]]
        for j in deps[i]:
            if kn.get(chan(j), -1) < j:
                waits[i].append(j)
                for c2, v in clock[j].items():
                    if kn.get(c2, -1) < v: kn[c2] = v
        clock[i] = dict(kn); clock[i][chan(i)] = i
    return waits


PROGRAM = []


def rank_program(g, core, T, topo):
    rank = T.rank_of(core)
    if rank is None:
        return
    n = len(T.cores)
    if not PROGRAM:
        ops, deps = arrange(plan())
        PROGRAM.extend([ops, waits_of(ops, deps)])
    ops, waits = PROGRAM
    Q = {"v": g.vector, "s": g.scalar, "p": g.tensor, "g": g, "y": g.sync}
    need = set(j for w in waits for j in w)
    sig = {}; cnt = {q: 0 for q in QS}; nd = 0
    for i, o in enumerate(ops):
        if o[1] in ("load", "store"):
            sig[i] = ("d%d" % nd, 16); nd += 1
        elif o[1] == "land":
            sig[i] = (o[2][0], len(topo.engines(T.cores[(rank - o[2][1]) % n], core)))
        elif o[1] != "send" and i in need:
            cnt[o[0]] += 1; sig[i] = ("q" + o[0], cnt[o[0]])

    def ap(x):
        if x is None or isinstance(x, (int, float)):
            return x
        if x[0] == "*":
            return ap(x[1]).indirect(ap(x[2]))
        return T[x[0]][x[5]:x[4], x[1]:x[2]:x[3]] if x[3] != 1 else T[x[0]][x[5]:x[4], x[1]:x[2]]

    def hbm(x):
        t = T[x[0]]
        return t[:, :] if [x[2] - x[1], x[4] - x[3]] == list(t.shape) else t[x[1]:x[2], x[3]:x[4]]

    sent = 0; stores = []
    for i, (q, kind, a, rd, wr, st) in enumerate(ops):
        if kind == "land":
            continue
        e = Q[q]
        for j in waits[i]:
            e.wait_ge(T.sem[sig[j][0]], sig[j][1])
        if kind == "send":
            dst = T.cores[(rank + a[1]) % n]
            rid, pid = topo.addr(dst, core)
            g.remote_dma(ap(a[2]), ap(a[3]), T.sem[a[0]], T.sem.sent, pid, rid, topo.mask(core, dst))
            sent += len(topo.engines(core, dst))
            continue
        if kind == "load": ins = e.dma_start(ap(a[0]), ap(a[1]) if rd else hbm(a[1]))
        elif kind == "store":
            ins = e.dma_start(hbm(a[0]), ap(a[1]))
            stores.append(i)
        elif kind == "cp": ins = e.tensor_copy(ap(a[0]), ap(a[1]))
        elif kind == "tt": ins = e.tensor_tensor(ap(a[0]), ap(a[1]), ap(a[2]), a[3])
        elif kind == "ts":
            if a[5] is None: ins = e.tensor_scalar(ap(a[0]), ap(a[1]), ap(a[2]), None, a[4])
            else: ins = e.tensor_scalar(ap(a[0]), ap(a[1]), ap(a[2]), ap(a[3]), a[4], a[5])
        elif kind == "scan": ins = e.tensor_tensor_scan(ap(a[0]), ap(a[1]), ap(a[2]), a[3], a[4], a[5])
        elif kind == "mset": ins = e.memset(ap(a[0]), a[1])
        elif kind == "act":
            if a[2] == AF.Copy: ins = e.activation(ap(a[0]), ap(a[1]), a[2])
            else: ins = e.activation(ap(a[0]), ap(a[1]), a[2], bias=ap(a[3]), scale=ap(a[4]))
        elif kind == "mm": ins = e.matmul(ap(a[0]), ap(a[1]), ap(a[2]), a[3], a[4])
        elif kind == "iota":
            if SCRATCH[a[0][0]][2] == I32: ins = e.iota(ap(a[0]), a[1], a[2], a[3])
            else: ins = e.iota(ap(a[0]), a[1], a[2], a[3], allow_small_or_imprecise_dtypes=True)
        if i in sig:
            ins.then_inc(T.sem[sig[i][0]], 16 if kind in ("load", "store") else 1)
    for i in stores:
        Q[ops[i][0]].wait_ge(T.sem[sig[i][0]], 16)
    g.wait_ge(T.sem.sent, sent)
